import numpy as np, ml_dtypes
CORES = [8,136,40,168]
N = 4
BF = ml_dtypes.bfloat16
def gentries(a):
    return np.ascontiguousarray(a.reshape(8, 16, -1).transpose(0, 2, 1)).reshape(8, -1)
def gtable(e):
    e = np.asarray(e); return np.ascontiguousarray(e.reshape(8, -1, 16).transpose(0, 2, 1)).reshape(128, -1).astype(np.int32)
V, D, SD, L, M, P, RO, ST = 1024, 8, 3, 256, 1024, 128, 2, 4
DV, E = D * V, (N - 1) * L
def wire(rng, nm, no, vd, od=None, oa=None):
    if od is None: od = np.argsort(rng.random((N, 8, DV)), axis=2)
    if oa is None: oa = np.argsort(rng.random((N, 8, DV)), axis=2)
    a = np.full((N, 8, DV), -1, np.int64); b = np.full((N, 8, DV), -1, np.int64)
    ni = np.zeros((N, 8), np.int64); nu = np.zeros((N, 8), np.int64)
    for g in range(8):
        for q in range(N):
            for h in range(N - 1):
                r = (q + h + 1) % N; m = int(nm[q, g, h]); n = m + int(no[q, g, h])
                c = DV + D * (h * L + rng.permutation(L)[:n])
                i = int(nu[q, g]); b[q, g, oa[q, g, i:i + n]] = c; nu[q, g] += n
                i = int(ni[r, g]); a[r, g, od[r, g, i:i + m]] = c[:m]; ni[r, g] += m
        for q in range(N):
            i, j = int(ni[q, g]), int(nu[q, g]); n = max(min(DV - i - int(vd[q, g]), DV - j), 0)
            sd = od[q, g, i:i + n]; sa = oa[q, g, j:j + n]; a[q, g, sd] = sa; b[q, g, sa] = sd
    return a, b
def parts(rng):
    x = rng.integers(0, 16, (N, 8, 16, V))
    nm = rng.integers(L // 2, 3 * L // 4, (N, 8, N - 1)); no = rng.integers(0, L // 8 + 1, (N, 8, N - 1))
    vd = rng.integers(M // 2, 3 * M // 2, (N, 8)); p = np.zeros((N, 8, 4 + RO), np.int64)
    p[..., 0] = rng.integers(95, 112, (N, 8)); p[..., 1] = rng.integers(112, 150, (N, 8)); p[..., 2] = rng.integers(130, 147, (N, 8))
    p[..., 3] = 2 * rng.integers(0, 1024, (N, 8)) + 1; p[..., 4:] = rng.integers(0, DV, (N, 8, RO))
    return x, nm, no, vd, p
def pack(x, ab, p):
    return {"x0": np.ascontiguousarray(x.reshape(N, 128, V)).astype(BF), "den": np.stack([gtable(c) for c in ab[0]]), "axo": np.stack([gtable(c) for c in ab[1]]), "par": p.astype(np.int32)}
def setup_inputs(rng):
    x, nm, no, vd, p = parts(rng)
    return pack(x, wire(rng, nm, no, vd), p)
def setup_inputs_caps(rng):
    x, nm, no, vd, p = parts(rng); p[..., 0] = 0; p[..., 1] = 241; p[..., 2] = 241
    nm[:] = rng.choice(np.array([0, 1, L // 2, L - 1, L]), (1, 8, N - 1)); nm[:, 3:5] = L // 2
    no[:] = np.minimum(rng.choice(np.array([0, 1, 7, L]), no.shape), L - nm); no[1, :, 0] = L - nm[1, :, 0]; no[1, 3:5, N - 2] = 5
    nm[:, 5] = 0; no[1:, 5] = L; no[0] = 0
    vd[:] = rng.choice(np.array([0, 1, M - 1, M, M + 1, 2 * M]), (N, 8)); vd[0] = np.array([M, M + 1, M - 1, 0, 1, 2 * M, M, 5])
    return pack(x, wire(rng, nm, no, vd), p)
def setup_inputs_full(rng):
    x, nm, no, vd, p = parts(rng); nm[:] = L; no[:] = 0; vd[:] = 0
    p[..., 0] = rng.integers(105, 136, (N, 8)); p[..., 1] = rng.integers(90, 242, (N, 8)); p[..., 2] = rng.integers(105, 136, (N, 8))
    return pack(x, wire(rng, nm, no, vd), p)
def setup_inputs_alike(rng):
    x, nm, no, vd, p = parts(rng)
    od = np.argsort(rng.random((N, 8, DV)), axis=2); oa = np.argsort(rng.random((N, 8, DV)), axis=2); o = np.arange(DV)
    od[:, 0] = o; oa[:, 0] = o; od[:, 1] = o[::-1]; oa[:, 2] = o[::-1]
    for q in range(N):
        od[q, 3] = (D * rng.permutation(V)[:, None] + np.arange(D)).reshape(-1); oa[q, 3] = (D * rng.permutation(V)[:, None] + np.arange(D)).reshape(-1)
    x[:, 0:4:2] = 2 * rng.integers(0, 8, (N, 2, 1, 1)) + 1; x[:, 1:4:2] = rng.integers(0, 16, (N, 2, 1, V))
    p[:, :4, 0] = 16 * rng.integers(3, 8, (N, 4)); p[:, :4, 1] = 16 * rng.integers(7, 16, (N, 4)); p[:, :4, 2] = 16 * rng.integers(8, 13, (N, 4))
    p[:, 0::4, 3] = 1; p[:, 0::4, 4:] = 0; p[:, 1::4, 3] = 2047; p[:, 1::4, 4:] = DV - 1
    return pack(x, wire(rng, nm, no, vd, od, oa), p)
def setup_inputs_bare(rng):
    x, nm, no, vd, p = parts(rng); g = rng.permutation(8); q = int(rng.integers(0, N))
    nm[:, g[0]] = 0; no[:, g[0]] = 0; vd[:, g[0]] = DV
    nm[:, g[1]] = 0; no[:, g[1]] = rng.integers(0, L + 1, (N, N - 1)); vd[:, g[1]] = M
    vd[:, g[2]] = DV
    p[:, g[3], :3] = np.array([0, 0, 241]); p[:, g[4], :3] = np.array([241, 241, 0])
    nm[q] = 0; no[q] = 0
    return pack(x, wire(rng, nm, no, vd), p)
def setup_inputs_spread(rng):
    x, nm, no, vd, p = parts(rng)
    x = np.minimum((np.exp2(4.2 * rng.random((N, 8, 1, V))) * rng.random(x.shape)).astype(np.int64), 15)
    p[..., :3] = rng.integers(0, 242, (N, 8, 3))
    nm = rng.integers(0, L + 1, nm.shape); no = ((L - nm + 1) * rng.random(nm.shape)).astype(np.int64)
    vd = np.exp2(12.9 * rng.random((N, 8))).astype(np.int64)
    return pack(x, wire(rng, nm, no, vd), p)
def ends(c):
    o = np.full((N, 8, E), -1, np.int64); n, g, i = np.nonzero(c >= DV)
    o[n, g, (c[n, g, i] - DV) >> SD] = i
    return o
def gone(c, f):
    return (c >= DV) & np.take_along_axis(f, np.maximum(c - DV, 0) >> SD, 2)
def check_inputs(d):
    bad = []
    x = np.asarray(d["x0"]).astype(np.float32); p = np.asarray(d["par"]).astype(np.int64)
    if not np.all((x >= 0) & (x <= 15) & (x == np.floor(x))): bad.append("range of x0")
    if not np.all((p[..., :3] >= 0) & (p[..., :3] <= 241)): bad.append("range of the thresholds in par")
    if not np.all((p[..., 3] >= 1) & (p[..., 3] <= 2047) & ((p[..., 3] & 1) == 1)): bad.append("K in par")
    if not np.all((p[..., 4:] >= 0) & (p[..., 4:] < DV)): bad.append("C in par")
    a = np.stack([gentries(c) for c in d["den"]]).astype(np.int64); b = np.stack([gentries(c) for c in d["axo"]]).astype(np.int64)
    out = False
    for k, c in (("den", a), ("axo", b)):
        if not np.all((c >= -1) & (c < DV + D * E) & ((c < DV) | ((c & (D - 1)) == 0))): bad.append("range of " + k); out = True
    if out: return bad
    for k, c, o in (("den", a, b), ("axo", b, a)):
        n, g, i = np.nonzero(c >= DV); key = (n * 8 + g) * E + ((c[n, g, i] - DV) >> SD)
        if np.unique(key).size != key.size: bad.append("a link that stands twice in " + k)
        n, g, i = np.nonzero((c >= 0) & (c < DV))
        if np.any(o[n, g, c[n, g, i]] != i): bad.append("twins of " + k)
    ie, oe = ends(a), ends(b)
    for r in range(N):
        for h in range(1, N):
            z = slice((h - 1) * L, h * L)
            if np.any((ie[r][:, z] >= 0) & (oe[(r - h) % N][:, z] < 0)): bad.append("a link in den that no axonal slot holds")
    return sorted(set(bad))
def reference(x0, den, axo, par):
    x = np.asarray(x0).astype(np.float32).astype(np.int32).reshape(N, 8, 16, V)
    a = np.stack([gentries(c) for c in den]).astype(np.int64); b = np.stack([gentries(c) for c in axo]).astype(np.int64); p = par.astype(np.int64)
    blocks = [(r, (r - h) % N, slice((h - 1) * L, h * L)) for r in range(N) for h in range(1, N)]
    for t in range(RO):
        oe = ends(b)
        for k in range(ST):
            new, far = [], []
            for r in range(N):
                w = [x[r]]
                for h in range(1, N):
                    q = (r - h) % N; i = oe[q][:, (h - 1) * L:h * L]
                    w.append(np.take_along_axis(x[q], np.maximum(i, 0)[:, None, :] >> SD, 2) * (i >= 0)[:, None, :])
                w = np.concatenate(w, axis=2); held = a[r] >= 0
                v = (np.take_along_axis(w, np.maximum(a[r], 0)[:, None, :] >> SD, 2) * held[:, None, :]).reshape(8, 16, V, D)
                if k == ST - 1: far.append(np.where(held.reshape(8, V, D), np.add.reduce(np.abs(v - x[r][..., None]), axis=1), -1))
                new.append((x[r] + np.add.reduce(v, axis=3)) & 15)
            x = np.stack(new).astype(np.int32)
        far = np.stack(far); s = np.add.reduce(x, axis=2)
        best = np.argmax(far, axis=3)
        kd = ((s >= p[..., 2:3])[..., None] & (far >= 0) & (np.arange(D) == best[..., None])).reshape(N, 8, DV)
        ka = ((s < p[..., 0:1])[..., None] & (np.arange(D) == t)).reshape(N, 8, DV) & (b >= 0)
        mb = np.zeros((N, 8, DV + D * E), bool); n, g, i = np.nonzero(kd); mb[n, g, a[n, g, i]] = True
        ma = np.zeros((N, 8, DV + D * E), bool); n, g, i = np.nonzero(ka); ma[n, g, b[n, g, i]] = True
        gi = np.zeros((N, 8, E), bool); go = np.zeros((N, 8, E), bool)
        for r, q, z in blocks:
            gi[r][:, z] = ma[q][:, DV::D][:, z]; go[q][:, z] = mb[r][:, DV::D][:, z]
        a = np.where(kd | ma[..., :DV] | gone(a, gi), -1, a); b = np.where(ka | mb[..., :DV] | gone(b, go), -1, b)
        oe, ie = ends(b), ends(a); opn = np.zeros((N, 8, E), bool)
        for r, q, z in blocks: opn[r][:, z] = (oe[q][:, z] >= 0) & (ie[r][:, z] < 0)
        z0 = (t % (N - 1)) * L
        for r in range(N):
            for g in range(8):
                vac = np.nonzero((a[r, g] < 0) & np.repeat(s[r, g] < p[r, g, 1], D))[0][:M]
                links = np.nonzero(opn[r, g])[0]; o = (p[r, g, 3] * np.arange(DV) + p[r, g, 4 + t]) & (DV - 1); fr = o[b[r, g][o] < 0]
                giv = np.concatenate([DV + D * links, fr]); m = min(len(vac), len(giv)); u = max(m - len(links), 0)
                a[r, g, vac[:m]] = giv[:m]
                b[r, g, fr[:u]] = vac[m - u:m]
                rest = fr[u:u + P]; free = np.nonzero(oe[r, g, z0:z0 + L] < 0)[0]; n = min(len(rest), len(free))
                b[r, g, rest[:n]] = DV + D * (z0 + free[:n])
    return {"yx": x.reshape(N, 128, V).astype(np.float32).astype(BF), "yd": np.stack([gtable(c) for c in a]).astype(np.float32), "ya": np.stack([gtable(c) for c in b]).astype(np.float32)}

@@ -1,0 +1,745 @@
+import math
+from concourse.bass import DstId, RemoteDMATransfer
+from concourse.mybir import AluOpType as A, ActivationFunctionType as F, AxisListType
+
+B16, F32, I32, U16 = "bfloat16", "float32", "int32", "uint16"
+_SB = {
+    B16: dict(W00=1808, W01=1808, W10=1808, W11=1808, WB=1808, G0=4096, G1=4096, D=2048, OB0=768, OB1=768, BO=768, Z=15872, XL0=1024, XL1=1024,
+              Q0=512, Q1=512, ONE=576, DEC=1152, C15=512, NEG1=512, TIE=512, RST=512, ONESB=128, TRI=128, TRIQ=128, TRIC=128, DM=128, BW=208, BAND=208,
+              SPD=2304, SPR=2048, BP=432, BJ=144, SUM=128, S17=128, ID=128, NID=128, NBIG=128, SEL=16, PT=128, BX=128, XR=1024, LBM=256, POW2=128, TA=128, TB=128,
+              FT=544, FG=576, FI=512, F1=512, HELD=512, VAC=512, K1=512, STH=512, FB=512, WD=512, WJ=512, UH=512, POW0=512, POW1=512, ONEP=1024,
+              HIT=1152, HIG=768, VT=1152, TAB=768, SGA=784, SGB=784, C0=64, CX=128, CT=48, CG=48, OH=48, OKA=48, AR=48, IH=48, FR=16, HI=80, LO=80, TL=48,
+              FLK=64, KEEP=48, EX=16),
+    F32: dict(ONEF=144, ID32=128, ONESB32=128, BS32=144, SUM32=128, PA=136, R8=128, R8X=64, PARF=8, PL=16, PX=8, COL=16, J=512, TABV=512, DUM=72, DZ=72, DZ0=72,
+              DT=72, DG=72, DI=72, A1=512, BM=512, T1=512, T2=512, YB=512, MN=512, REM=528, PAY=544, PAYG=576, TABT=544, TABG0=576, TABG1=576, WT=2304, WG=10112,
+              INV=1936, ZT=1152, ZG=1152, YT=1152, YG=1152, FL=1168, FL2=784, ZX=128, WF=32, XT=48, PPT=48, ZZT=48, OOT=48, XG=48, PPG=48, ZZG=48, OOG=48,
+              ZZ=80, EQ=80, OO=80, IE1=48, DIFI=48, DIFK=64, S1=72, S2=72, S3=72, S4=72, NOP=8, RM2=32, VO=48),
+    I32: dict(DEN=512, AXO=512, BH=512, B1=512, CB=512, UI=512, FGI=544, PARI=8, PI=8, N1=80, N2=80, N3=80, N4=80, N5=80, N6=80, N7=80, N8=80),
+    U16: dict(LA=512, LB=512, LO0=48, LO1=48, LI=48, LKA=64, LGI=48, LST=48, LSG=48, LS=48, LE=48, LE2=8, LZ=72, LW0=32, LW1=32, LM=32),
+}
+_ALIAS = dict(XL0=("G0", 0), XL1=("G1", 0), SGA=("D", 0), SGB=("D", 784), ZG=("WG", 1152), YG=("WG", 2304), WT=("WG", 3456), INV=("WG", 5760),
+              T1=("WG", 7696), T2=("WG", 8208), MN=("WG", 8720), YB=("WG", 9232))
+PLACE, SCRATCH = {}, {}
+for _d, _t in _SB.items():
+    _o = 0
+    for _n, _w in _t.items():
+        if _n in _ALIAS:
+            PLACE[_n] = _ALIAS[_n] + (_w,)
+        elif _w > 600:
+            PLACE[_n] = (_n, 0, _w)
+            SCRATCH[_n] = ("sbuf", [128, _w], _d)
+        else:
+            PLACE[_n] = ("pool" + _d, _o, _w)
+            _o += (_w + 15) // 16 * 16
+    SCRATCH["pool" + _d] = ("sbuf", [128, _o], _d)
+for _i in range(8):
+    SCRATCH["P%d" % _i] = ("psum", [128, 512], F32)
+    PLACE["P%d" % _i] = ("P%d" % _i, 0, 512)
+SEMAPHORES = (["cV", "cS", "cP", "cG", "l0", "l1", "la", "lb"] + ["x%d" % i for i in range(16)] + ["al0", "al1", "be0", "be1"] + ["d%d" % i for i in range(16)])
+M20, M24 = float(2 ** 20), float(2 ** 24)
+MASK = 2 ** 20 - 1
+LN2 = math.log(2.0)
+CY, GCY, PECY, HOP, FAR, HALF, LOOK, GAP, PIECE, TURNS = 1.04e-3, 1.4e-3, 0.55e-3, 0.13, 4.3, 0.7, 0.8, 1.0, 128, 30
+SHY = ({"V": 6.0, "S": 3.0}, {"V": 12.0, "S": 12.0}, {"V": 2.0, "S": 1.0})
+ORDER = []
+
+
+def rank_program(g, core, T, topo):
+    rank = T.rank_of(core)
+    if rank is None:
+        return
+    N = len(T.cores)
+    QU = {"V": g.vector, "S": g.scalar, "P": g.tensor, "G": g, "Y": g.sync}
+    nodes, rec, nd, lsum, chain = [], {}, [0], {}, []
+
+    def a(n, lo=0, hi=None, st=1, p0=0, p1=128):
+        b, o, w = PLACE[n]
+        return (b, o + lo, o + (w if hi is None else hi), st, p0, p1)
+
+    def h64(n, lo=0, hi=None, st=1, s=0):
+        return a(n, lo, hi, st, 64 * s, 64 * s + 64)
+
+    def ap(x):
+        if not isinstance(x, tuple):
+            return x
+        if x[0] == "@":
+            return ap(x[1]).indirect(ap(x[2]))
+        return T[x[0]][x[4]:x[5], x[1]:x[2]:x[3]] if x[3] != 1 else T[x[0]][x[4]:x[5], x[1]:x[2]]
+
+    def flat(xs):
+        o = []
+        for x in xs:
+            if isinstance(x, tuple):
+                o += [x[1], x[2]] if x[0] == "@" else [x]
+        return o
+
+    def psum(x):
+        return SCRATCH[x[0]][0] == "psum"
+
+    def node(ways, rd, wr, lat=0.0, tok=None, after=()):
+        me, dep = len(nodes), set(after)
+        for kind, xs in (("r", rd), ("w", wr)):
+            for x in xs:
+                for (lo, hi, k, n) in rec.get(x[0], []):
+                    if psum(x) or (lo < x[2] and x[1] < hi and (kind == "w" or k == "w")):
+                        dep.add(n)
+        for kind, xs in (("r", rd), ("w", wr)):
+            for x in xs:
+                old = rec.get(x[0], [])
+                if psum(x):
+                    old = []
+                elif kind == "w" and x[3] == 1 and x[4] == 0 and x[5] == 128:
+                    old = [r for r in old if not (x[1] <= r[0] and r[1] <= x[2])]
+                rec[x[0]] = old + [(x[1], x[2], kind, me)]
+        nodes.append(dict(ways=ways, dep=sorted(dep), lat=lat, tok=tok))
+        return me
+
+    def size(x):
+        return (x[2] - x[1] + x[3] - 1) // x[3]
+
+    def est(e, out, ins, two=False):
+        xs = [x for x in [out] + ins if isinstance(x, tuple)]
+        ind = [x for x in xs if x[0] == "@"]
+        if ind:
+            return 16 * size(ind[0][2]) * (3.8 if out[0] == "@" else 1.56) * CY + 0.06
+        f = 1.0
+        if e == "V" and two:
+            f = 1.0 if any(psum(x) for x in xs[1:]) else 2.0
+        elif e == "V" and all(SCRATCH[x[0]][2] in (B16, U16) for x in xs if size(x) > 1):
+            f = 0.5
+        return max(64, max(size(x) for x in xs) * f) * CY + 0.06
+
+    def op(out, ins, ways, lat=0.0):
+        node(ways, flat(ins) + ([out[2]] if out[0] == "@" else []), [out[1]] if out[0] == "@" else [out], lat)
+
+    def ix(w, o):
+        return ("@", w, o)
+
+    def vop(o, ins, fn, two=False):
+        op(o, ins, {"V": (fn, est("V", o, ins, two))})
+
+    def cp(o, i):
+        vop(o, [i], lambda q: q.tensor_copy(ap(o), ap(i)))
+
+    def ms(o, c):
+        vop(o, [], lambda q: q.memset(ap(o), c))
+
+    def tt(o, x, y, f):
+        vop(o, [x, y], lambda q: q.tensor_tensor(ap(o), ap(x), ap(y), f), True)
+
+    def tsf(o, x, s1, f1, s2=None, f2=None):
+        if f2 is None:
+            return lambda q: q.tensor_scalar(ap(o), ap(x), ap(s1), None, f1)
+        return lambda q: q.tensor_scalar(ap(o), ap(x), ap(s1), ap(s2), f1, f2)
+
+    def ts(o, x, s1, f1, s2=None, f2=None):
+        vop(o, [x, s1, s2], tsf(o, x, s1, f1, s2, f2))
+
+    def scan(o, d0, d1, ini, f0, f1):
+        vop(o, [d0, d1, ini], lambda q: q.tensor_tensor_scan(ap(o), ap(d0), ap(d1), ap(ini), f0, f1))
+
+    def actf(o, i, f, bias, scale):
+        return lambda q: q.activation(ap(o), ap(i), f, bias=ap(bias), scale=ap(scale))
+
+    def act(o, i, f=F.Identity, bias=0.0, scale=1.0):
+        op(o, [i, bias, scale], {"S": (actf(o, i, f, bias, scale), est("S", o, [i]))})
+
+    def both(o, i, f=F.Identity, bias=0.0, scale=1.0, v=None):
+        if v is not None:
+            vf = tsf(o, i, *v)
+        elif bias == 0.0 and scale == 1.0:
+            vf = lambda q: q.tensor_copy(ap(o), ap(i))
+        else:
+            vf = tsf(o, i, scale, A.mult, bias, A.add)
+        op(o, [i, bias, scale], {"S": (actf(o, i, f, bias, scale), est("S", o, [i])), "V": (vf, est("V", o, [i]))})
+
+    def mms(items, start=True, stop=True):
+        def fn(q):
+            for i, (o, l, r) in enumerate(items):
+                last = q.matmul(ap(o), ap(l), ap(r), start and i == 0, stop and i == len(items) - 1)
+            return last
+        c = sum(max(min(64, size(l)), size(r)) * (4 if SCRATCH[l[0]][2] == F32 else 1) * PECY + 0.005 for o, l, r in items)
+        node({"P": (fn, c)}, [x for o, l, r in items for x in (l, r)], [items[0][0]], 0.06)
+
+    def mm(o, l, r, start=True, stop=True):
+        mms([(o, l, r)], start, stop)
+
+    def scatter(win, lst, n, src, piece=16):
+        for lo in range(0, n, piece):
+            hi = min(n, lo + piece)
+            cp(ix(a(win), a(lst, lo, hi)), a(src, 16 * lo, 16 * hi))
+
+    def iota(o, p, base, cm):
+        kw = {} if SCRATCH[o[0]][2] == I32 else {"allow_small_or_imprecise_dtypes": True}
+        op(o, [], {"G": (lambda q: q.iota(ap(o), p, base, cm, **kw), 0.2 + 2 * size(o) * GCY)})
+
+    def sel(o, i, p, base, cm, f=A.is_equal, fill=0.0):
+        op(o, [i], {"G": (lambda q: q.affine_select(ap(o), ap(i), p, f, fill, base, cm), 0.25 + 2 * size(o) * GCY)})
+
+    def band(o, i, p, base, p2, base2):
+        sel(o, i, p, base, 1, A.is_ge)
+        sel(o, o, p2, base2, -1, A.is_ge)
+
+    def dmas(e, items):
+        sem = "d%d" % nd[0]
+        nd[0] += 1
+
+        def fn(q):
+            for o, i in items:
+                q.dma_start(ap(o), ap(i)).then_inc(T.sem[sem], 16)
+        node({e: (fn, 0.1 * len(items))}, flat([i for o, i in items]), flat([o for o, i in items]), 2.5, (sem, 16 * len(items)))
+
+    def send(src, w, dst, off, sign, rsem, lsem):
+        tr = []
+        for h in range(1, N):
+            d = T.cores[(rank + sign * h) % N]
+            eng = topo.engines(core, d)
+            k = len(eng) // 4
+            mine = eng[:2 * k] if h == 1 else eng[h * k:(h + 1) * k]
+            rid, pid = topo.addr(d, core)
+            tr.append(RemoteDMATransfer(dst_ids=[DstId(rid=rid, pnc=pid)], dma_engine_mask=sum(1 << x for x in mine), remote_sem=T.sem[rsem],
+                                        src=ap(a(src, w * (h - 1), w * h)), dst=ap(a(dst, off + w * (h - 1), off + w * h))))
+        lsum[lsem] = lsum.get(lsem, 0) + 4 * k
+        n = node({"G": (lambda q: q.remote_dma_fused(tr, local_sem=T.sem[lsem]), 0.8)}, [a(src)], [], FAR - 0.8, (lsem, lsum[lsem]))
+        node({"R": (None, 0.0)}, [], [a(dst, off, off + 3 * w)], 0.0, (rsem, 4 * k), [n])
+
+    def schedule():
+        n = len(nodes)
+        fwd, bwd = [[] for _ in nodes], [[] for _ in nodes]
+        for u, x in enumerate(nodes):
+            for d in x["dep"]:
+                ways = nodes[d]["ways"]
+                gap = 0.0 if "P" in ways and "P" in x["ways"] else nodes[d]["lat"] + (0.0 if "R" in ways else HOP)
+                fwd[d].append((u, gap))
+                bwd[u].append((d, gap))
+
+        def run(out, into, link, prio, first, shy):
+            nxt = dict(zip(link, link[1:]))
+            left = [len(into[i]) for i in range(n)]
+            for i in link[1:]:
+                left[i] += 1
+            rdy = list(first)
+            ready = {e: set() for e in "RPGYVS"}
+            free = {e: 0.0 for e in "RPGYVS"}
+            order, fin = [], [0.0] * n
+            key = {e: [prio[i] - (shy.get(e, 0.0) if len(nodes[i]["ways"]) > 1 else 0.0) - 1e-7 * i for i in range(n)] for e in "RPGYVS"}
+            for i in range(n):
+                if left[i] == 0:
+                    for e in nodes[i]["ways"]:
+                        ready[e].add(i)
+            while len(order) < n:
+                t0, e = min((max(free[e], min(rdy[i] for i in ready[e])), j, e) for j, e in enumerate("RPGYVS") if ready[e])[::2]
+                ke = key[e]
+                i = max((i for i in ready[e] if rdy[i] <= t0 + 0.05), key=lambda j: ke[j])
+                soon = [j for j in ready[e] if t0 + 0.05 < rdy[j] <= t0 + min(LOOK, nodes[i]["ways"][e][1]) and ke[j] > ke[i] + GAP]
+                if soon:
+                    i = max(soon, key=lambda j: ke[j])
+                for x in nodes[i]["ways"]:
+                    ready[x].discard(i)
+                free[e] = fin[i] = max(t0, rdy[i]) + nodes[i]["ways"][e][1]
+                order.append((i, e))
+                for u, t1 in [(u, fin[i] + gap) for u, gap in out[i]] + ([(nxt[i], t0)] if i in nxt else []):
+                    rdy[u] = max(rdy[u], t1)
+                    left[u] -= 1
+                    if left[u] == 0:
+                        for x in nodes[u]["ways"]:
+                            ready[x].add(u)
+            return max(fin[i] + nodes[i]["lat"] for i in range(n)), order, fin
+
+        level = [0.0] * n
+        nxt = dict(zip(chain, chain[1:]))
+        for i in range(n - 1, -1, -1):
+            level[i] = min(c for f, c in nodes[i]["ways"].values()) + max([level[u] + gap for u, gap in fwd[i]] + [nodes[i]["lat"]])
+            if i in nxt:
+                level[i] = max(level[i], level[nxt[i]] + HALF * nodes[i]["ways"]["S"][1])
+        best, seed = None, 1
+        for shy in SHY:
+            prio = level
+            for it in range(TURNS):
+                got = run(fwd, bwd, chain, prio, [0.0] * n, shy)
+                if best is None or got[0] < best[0]:
+                    best = got
+                back = run(bwd, fwd, chain[::-1], (best if it % 3 == 2 else got)[2], [x["lat"] for x in nodes], shy)[2]
+                prio = []
+                for x in back:
+                    seed = seed * 48271 % 2147483647
+                    prio.append(x + seed / 2147483647)
+        return best[1]
+
+    def emit():
+        if not ORDER:
+            ORDER.extend(schedule())
+        for i, e in ORDER:
+            nodes[i]["e"] = e
+        cnt = {e: 0 for e in "VSPG"}
+        seen = {e: {} for e in QU}
+        total = {}
+
+        def wait(e, tok):
+            if seen[e].get(tok[0], 0) < tok[1]:
+                QU[e].wait_ge(T.sem[tok[0]], tok[1])
+                seen[e][tok[0]] = tok[1]
+        for i, e in ORDER:
+            x = nodes[i]
+            if e != "R":
+                need = {}
+                for d in x["dep"]:
+                    if not (e == "P" and nodes[d]["e"] == "P"):
+                        sem, c = nodes[d]["tok"]
+                        need[sem] = max(need.get(sem, 0), c)
+                for tok in need.items():
+                    wait(e, tok)
+                if e == "G" and x["tok"] is None:
+                    wait(e, ("cG", cnt[e]))
+                r = x["ways"][e][0](QU[e])
+                if x["tok"] is None:
+                    cnt[e] += 1
+                    r.then_inc(T.sem["c" + e], 1)
+                    x["tok"] = ("c" + e, cnt[e])
+            total[x["tok"][0]] = max(total.get(x["tok"][0], 0), x["tok"][1])
+        for tok in total.items():
+            wait("G", tok)
+
+    def P(i, lo=0, hi=512, st=1, p0=0, p1=128):
+        return a("P%d" % i, lo, hi, st, p0, p1)
+
+    def col(n, i, p1=128):
+        return a(n, i, i + 1, 1, 0, p1)
+
+    def row(n, lo, hi, p1=1):
+        return a(n, lo, hi, 1, 0, p1)
+
+    def view(n, m, off=0):
+        return a(n, off + 15 - m, off + 143 - m)
+
+    def spd(q, m):
+        return view("SPD", m, 144 * q)
+
+    def Wn(s, k):
+        return "W%d%d" % (s, k % 2)
+
+    dmas("Y", [(a("AXO"), T.axo[:])])
+    dmas("S", [(a("DEN"), T.den[:])])
+    dmas("Y", [(h64("XL%d" % s, s=hh), T.x0[64 * s:64 * s + 64, :]) for s in range(2) for hh in range(2)])
+    dmas("Y", [(row("PARI", 0, 6, 8), T.par[:])])
+    dmas("Y", [(a("BH", 32 * r, 32 * r + 32), T.axo[r::16, :]) for r in range(16)])
+
+    ms(a("ONE"), 1.0)
+    ms(a("ONEF"), 1.0)
+    ms(a("TA"), M20)
+    ms(a("TB"), -2064.0)
+    ms(a("SEL", 8, 16), -8.0)
+    ms(a("DEC"), -M20)
+    iota(col("PI", 0), [[0, 1]], 0, 1)
+    blk, blk2 = [[-16, 8], [0, 16]], [[16, 8], [0, 16]]
+    band(a("TRIQ"), a("TA"), blk, 0, blk2, 15)
+    sel(a("TRIQ"), a("TRIQ"), [[1, 128]], 0, -1, A.is_ge)
+    sel(a("TRIQ"), a("TRIQ"), [[1, 128]], 0, -1, A.not_equal, M24)
+    band(a("BW"), a("ONE", 0, 208), [[-16, 13], [1000, 16]], 64 - 15000, [[16, 13], [0, 16]], 15 - 64)
+    band(a("ONESB"), a("ONE", 0, 128), blk, 0, blk2, 15)
+    iota(a("DUM"), [[1, 72]], 0, 72)
+    iota(a("TABV"), [[2, 512]], 0, 0)
+    ts(col("PI", 1), col("PI", 0), 15, A.bitwise_and)
+    ts(col("PI", 2), col("PI", 0), 112, A.bitwise_and)
+    ts(col("PI", 3), col("PI", 0), 3, A.arith_shift_right, 1, A.bitwise_and)
+    ts(col("PI", 6), col("PI", 0), 1, A.add)
+    ts(col("PI", 4), col("PI", 6), 7, A.bitwise_and)
+    ts(col("PI", 5), col("PI", 0), 7, A.bitwise_and)
+    cp(a("COL", 0, 5), a("PI", 1, 6))
+    ts(col("COL", 4), col("COL", 4), 0.5, A.mult)
+    ts(col("COL", 8), col("COL", 1), -72.0, A.mult)
+    ts(col("COL", 10), col("COL", 3), -1.0, A.mult)
+    ts(col("COL", 11), col("COL", 1), -1.0, A.mult)
+    ts(a("DUM"), a("DUM"), col("COL", 8), A.add)
+    both(a("TABV"), a("TABV"), bias=col("COL", 2), v=(col("COL", 2), A.add))
+    ts(a("DM"), a("ONESB"), -1.0, A.mult)
+    sel(a("DM"), a("DM"), [[-1, 128]], 0, 1, A.is_ge)
+    cp(a("BS32"), a("BW", 64, 208))
+    for n, c in (("DT", 1152.0), ("DI", 784.0), ("DZ", 14337.0), ("DG", 8960.0), ("DZ0", 14336.0)):
+        ts(a(n), a("DUM"), c, A.add)
+    ms(a("PA", 0, 8), 0.0)
+    for s in range(2):
+        sel(h64("SUM", s=s), h64("ONE", 0, 128, s=s), [[0, 2], [-1, 64]], 0, 1)
+        sel(h64("SUM32", s=s), h64("ONEF", 0, 128, s=s), [[0, 2], [-1, 64]], 0, 1)
+        for hh in range(2):
+            sel(h64("PA", 8 + 64 * hh, 72 + 64 * hh, s=s), h64("ONEF", 0, 64, s=s), [[-16, 4], [-8, 4], [-1, 4]], -4 * hh, 1)
+    sel(a("PA", 8, 136), a("PA", 8, 136), [[0, 8], [-1, 4], [0, 4]], 1, 0, A.is_ge)
+    sel(a("ID"), a("ONE", 0, 128), [[-1, 128]], 0, 1)
+    sel(row("R8", 0, 128, 8), row("ONEF", 0, 128, 8), [[-1, 8], [0, 16]], 0, 1)
+    sel(row("R8X", 0, 64, 8), row("ONEF", 0, 64, 8), [[0, 8], [-1, 8]], 0, 1)
+    iota(a("J"), [[16, 512]], 0, 1)
+    for i in range(8):
+        sel(a("SPD", 288 * i, 288 * i + 288), a("ONE", 0, 288), [[-1, 2], [-16, 9], [1000, 16]], -2 * i - 15000, 1)
+        sel(a("SPR", 256 * i, 256 * i + 256), a("ONE", 0, 256), [[-1, 2], [-16, 8], [0, 16]], -2 * i, 1)
+    iota(row("TIE", 0, 512), [[0, 64], [1, 8]], -7, 0)
+    sel(a("RST"), a("ONE", 0, 512), [[0, 64], [1, 8]], 0, 0, A.not_equal)
+    band(a("SEL", 0, 8), a("SEL", 8, 16), [[-16, 4], [-64, 2]], 0, [[16, 4], [64, 2]], 15)
+    sel(a("PT"), a("TB"), [[-8, 2], [-16, 8], [-1, 8]], 0, 1)
+    band(h64("BAND"), h64("ONE", 0, 208), [[-16, 13], [1000, 2], [0, 8]], 64 - 1000, [[16, 13], [0, 2], [0, 8]], 15 - 64)
+    band(h64("BX"), h64("ONE", 0, 128), [[-16, 128]], 16 * 63, [[16, 128]], 15 - 16 * 63)
+    for i in range(4):
+        sel(h64("XR", 256 * i, 256 * i + 256), h64("ONE", 0, 256), [[-8, 2], [-1, 8], [0, 16]], -16 * i, 1)
+    for b in range(2):
+        sel(a("LBM", 128 * b, 128 * b + 128), a("ONE", 0, 128), [[-16, 8], [1000, 2], [0, 8]], -1000 * b, 1)
+    sel(a("TRI"), a("ONESB"), [[1, 128]], 0, -1, A.is_ge)
+    sel(a("TRIC"), a("TRI"), [[1, 128]], 0, -1, A.not_equal, -4096.0)
+    band(a("POW2"), a("ONE", 0, 128), [[-16, 8], [-1000, 8], [-8, 2]], 0, [[16, 8], [0, 8], [8, 2]], 7)
+    iota(a("TABG0", 0, 48), [[128, 48]], 8193, 8)
+    iota(a("S4", 0, 32), [[0, 16], [16, 2]], 0, 0)
+    ts(h64("S17"), h64("SUM"), 17.0, A.mult)
+    ms(h64("C15"), 1536.0)
+    ts(a("NID"), a("ID"), -1.0, A.mult)
+    cp(a("ID32"), a("ID"))
+    ts(a("NBIG"), a("ID"), -16384.0, A.mult)
+    both(a("J"), a("J"), bias=col("COL", 11), v=(col("COL", 11), A.add))
+    act(col("EX", 0), col("COL", 0), F.Exp, scale=LN2)
+    cp(col("COL", 5), col("EX", 0))
+    ts(a("POW2"), a("POW2"), col("COL", 5), A.mult)
+    for t in range(2):
+        ts(col("COL", 6 + t), col("COL", 0), float(t), A.is_equal, -1.0 / M20, A.mult)
+    for i in range(3):
+        tt(a("BP", 144 * i, 144 * i + 144), a("SPD", 288 * i, 288 * i + 144), a("SPD", 288 * i + 144, 288 * i + 288), A.add)
+    cp(a("ONESB32"), a("ONESB"))
+    ts(a("BJ"), a("BW", 64, 208), col("COL", 4), A.mult)
+    ts(col("COL", 9), col("COL", 1), -8.0, A.mult, -M24, A.add)
+    ts(a("TABG0", 0, 48), a("TABG0", 0, 48), col("COL", 9), A.add)
+    cp(a("TABG1", 0, 48), a("TABG0", 0, 48))
+    ts(a("LM"), a("S4", 0, 32), col("COL", 0), A.add)
+    both(a("TABT", 0, 512), a("J"), bias=1.0 - M24)
+    for n, lo, hi, c in (("TABT", 528, 544, -M24), ("TABG0", 560, 576, -M24), ("TABG1", 560, 576, -M24), ("FT", 528, 544, 0.0), ("FG", 560, 576, 0.0),
+                         ("FL", 1152, 1168, 0.0), ("FL2", 768, 784, 0.0), ("WB", 0, 16, 0.0), ("REM", 0, 1, -3072.0), ("RM2", 0, 1, -3968.0),
+                         ("W00", 0, 16, 96.0), ("W01", 0, 16, 96.0), ("W10", 0, 16, 96.0), ("W11", 0, 16, 96.0)):
+        ms(a(n, lo, hi), c)
+    ms(row("NEG1", 0, 512), -1.0)
+    for i in range(8):
+        both(a("Z", 1024 * i, 1024 * i + 1024), a("DEC", 0, 1024), scale=0.0)
+    both(a("Z", 8192, 14336, 8), a("DEC", 0, 768), scale=0.0)
+
+    def offsets(fl, nl, x, b0, b1, linkcol=False):
+        c, xx, pp, oo = [a(n + x, 0, nl) for n in ("C", "X", "PP", "OO")]
+        mms([(P(b0, 0, nl), view("BW", m, 64), a(fl, m, 16 * nl, 16)) for m in range(16)])
+        both(c, P(b0, 0, nl))
+        mm(P(b1, 0, nl), a("ONESB"), c)
+        mm(P(b1, 64, 64 + nl), a("DM"), c)
+        mms([(P(b0, 64, 64 + nl), a("ID32"), a("D" + x, 0, nl)), (P(b0, 64, 64 + nl), a("NBIG"), c)])
+        scan(xx, a("ONE", 0, nl), P(b1, 0, nl), 0.0, A.mult, A.add)
+        tt(pp, xx, P(b1, 64, 64 + nl), A.add)
+        if linkcol:
+            ts(col("NOP", 1), col("XT", 31), -1.0, A.mult, col("NOP", 0), A.add)
+            ts(col("PPT", 32), col("NOP", 1), 0.0, A.max, col("PPT", 32), A.add)
+        tt(oo, pp, P(b0, 64, 64 + nl), A.max)
+        cp(a("LS" + x, 0, nl), oo)
+
+    def ends(le, nl, x, zero):
+        c, zz, xx, pp = [a(n + x, 0, nl) for n in ("C", "ZZ", "X", "PP")]
+        tt(xx, pp, c, A.add)
+        both(zz, c, bias=zero + 1.0, scale=-16384.0)
+        tt(xx, xx, zz, A.max)
+        ts(a(le, 0, nl), xx, -1.0, A.add)
+
+    def pack(x, nl, n):
+        scatter("W" + x, "LS" + x, nl, "PAYG" if x == "G" else "PAY", 18)
+        scan(a("Z" + x, 0, n), a("DEC", 0, n), a("W" + x, 0, n), -2 * M24, A.add, A.max)
+        if x == "T" and n == 1152:
+            act(a("YT"), a("ZT"), F.Relu)
+            act(a("YT"), a("YT"), F.Relu, M20, -1.0)
+        else:
+            ts(a("Y" + x, 0, n), a("Z" + x, 0, n), 0.0, A.max, M20, A.min)
+
+    def invert(src, held):
+        ts(a("FI"), a(src), 8192.0, A.is_ge)
+        both(a("WT", 0, 768), a("DEC", 0, 768), scale=32.0)
+        both(a("INV", 0, 784), a("DEC", 0, 784), scale=0.0)
+        offsets("FI", 32, "T", 4, 5)
+        mm(P(7), a("TRIQ"), a("FI"))
+        ts(P(6), a(src), -8184.0 - 131072.0, A.add, 128.0, A.mult)
+        tt(a("T2"), a("TABV"), P(6), A.add)
+        tt(a("PAY", 0, 512), a("T2"), P(7), A.add)
+        pack("T", 32, 768)
+        mms([(P(4, 0, 48), view("BS32", m), a("YT", m, 768, 16)) for m in range(16)])
+        cp(a("N1", 0, 48), P(4, 0, 48))
+        ts(a("N2", 0, 48), a("N1", 0, 48), MASK, A.bitwise_and, 10, A.arith_shift_right)
+        ts(a("EQ", 0, 48), a("N2", 0, 48), 0.0, A.is_equal)
+        tt(a("ZZ", 0, 48), a("EQ", 0, 48), a("DI", 0, 48), A.mult)
+        tt(a("OO", 0, 48), a("ZZ", 0, 48), a("N2", 0, 48), A.max)
+        cp(a("LS"), a("OO", 0, 48))
+        scatter("INV", "LS", 48, "YT")
+        mms([(P(5, 0, 48), view("BS32", m), a("INV", 1 + m, 769, 16)) for m in range(16)])
+        cp(a("N1", 0, 48), P(5, 0, 48))
+        ts(a("N2", 0, 48), a("N1", 0, 48), 1023, A.bitwise_and)
+        ts(a("N3", 0, 48), a("N1", 0, 48), MASK, A.bitwise_and)
+        ts(a(held), a("N3", 0, 48), 0.0, A.is_gt)
+
+    def lists_a(b):
+        for s in range(2):
+            mms([(P(b + s, 0, 256), h64("PA", 8 - 8 * a0, 136 - 8 * a0, s=s), h64("A1", a0, 512, 2, s=s)) for a0 in range(2)])
+            ts(a("LA", 256 * s, 256 * s + 256), P(b + s, 0, 256), 0.125, A.mult, 15.4375, A.add)
+
+    def outgoing(s, k):
+        w = Wn(s, k)
+        for lo, hi in ((0, 24), (24, 48)):
+            both(a("OB%d" % s, 16 * lo, 16 * hi), ix(a(w, 0, 1040), a("LO%d" % s, lo, hi)))
+        send("OB%d" % s, 256, w, 1040, 1, "x%d" % (2 * k + s), "l%d" % s)
+
+    def order_tables(t):
+        ts(a("UI"), a("J"), col("PL", 3), A.mult, col("PL", 4 + t), A.add)
+        ts(a("UI"), a("UI"), 8191, A.bitwise_and)
+        ts(a("UH"), a("UI"), 1.0 / 512, A.mult, 191.5009765625, A.add)
+        act(a("POW%d" % t), a("UH"), F.Exp, bias=191 * LN2, scale=-LN2)
+        ts(a("TABG%d" % t, 48, 560), a("UI"), 1.0 - M24, A.add)
+        ts(a("N5", 0, 32), a("UI", 0, 32), 15, A.bitwise_and)
+        ts(a("N6", 0, 32), a("UI", 0, 32), 4, A.arith_shift_right, 31, A.bitwise_and)
+        ts(a("N5", 0, 32), a("N5", 0, 32), 32.0, A.mult)
+        tt(a("N5", 0, 32), a("N5", 0, 32), a("N6", 0, 32), A.add)
+        cp(a("LW%d" % t), a("N5", 0, 32))
+
+    def round_tables(t):
+        ts(a("LB"), a("B1"), 0.125, A.mult, 15.4375, A.add)
+        ts(a("CB"), a("B1"), 7, A.bitwise_and)
+        both(a("HELD"), a("A1"), F.Sign, v=(0.0, A.is_gt))
+        both(a("VAC"), a("HELD"), bias=1.0, scale=-1.0)
+        for b in range(2):
+            c0 = 32 * (8 * b + t)
+            tt(a("S1", 0, 32), a("B1", c0, c0 + 32), a("DZ", b, 64, 2), A.subtract)
+            ts(a("S2", 0, 32), a("B1", c0, c0 + 32), 0.0, A.is_gt)
+            tt(a("DIFK", b, 64, 2), a("S1", 0, 32), a("S2", 0, 32), A.mult)
+        cp(a("TABT", 512, 528), a("TABG0", 16 * t, 16 * t + 16))
+        both(a("ONEP"), a("DEC", 0, 1024), scale=col("COL", 6 + t), v=(col("COL", 6 + t), A.mult))
+        ts(a("LI"), a("IE1"), 0.125, A.mult, 15.4375, A.add)
+        tt(a("DIFI"), a("IE1"), a("DZ", 0, 48), A.subtract)
+        cp(a("N1", 0, 48), a("IE1"))
+        ts(a("N1", 0, 48), a("N1", 0, 48), 7, A.bitwise_and)
+        both(a("S3", 0, 48), a("IH"), bias=99.0, scale=-99.0)
+        tt(a("TL"), a("S3", 0, 48), a("N1", 0, 48), A.add)
+        mms([(P(4, m, 512, 16), a("SPR", 128 * m, 128 * m + 128), a("TL", 0, 32)) for m in range(16)])
+        mms([(P(5, m, 256, 16), a("SPR", 128 * m, 128 * m + 128), a("TL", 32, 48)) for m in range(16)])
+        both(a("TAB", 0, 512), P(4))
+        both(a("TAB", 512, 768), P(5, 0, 256))
+        both(a("WT", 0, 1152), a("DEC"), scale=32.0)
+        both(a("WG", 0, 1152), a("DEC"), scale=32.0)
+        mms([(P(6), row("ONE", 0, 128), row("TIE", 0, 512))]
+            + [(P(6, 256 * b + 64 * bl, 256 * b + 64 * bl + 64), a("HELD", 128 * bl, 128 * bl + 128), a("PT", 64 * b, 64 * b + 64)) for b in range(2) for bl in range(4)],
+            True, False)
+
+    def step(s, k):
+        w, gs = Wn(s, k), "G%d" % s
+        for hv in range(2):
+            b, o = 2 * s + hv, a(Wn(s, k + 1), 16 + 512 * hv, 528 + 512 * hv)
+            mm(P(b), h64("SUM" if k % 4 < 2 else "S17"), h64(w, 16 + 512 * hv, 528 + 512 * hv), True, False)
+            if k % 4 == 1:
+                mm(P(b), h64("SUM"), h64("C15"), False, False)
+            for q in (2 * hv, 2 * hv + 1):
+                for lo in range(256 * q, 256 * q + 256, PIECE):
+                    both(a(gs, 4 * lo, 4 * (lo + PIECE)), ix(a(w), a("LA", 256 * s + lo // 4, 256 * s + (lo + PIECE) // 4)))
+                    chain.append(len(nodes) - 1)
+                mms([(P(b, 256 * (q % 2), 256 * (q % 2) + 256), a("SUM"), a(gs, 1024 * q + j, 1024 * q + 1024, 4)) for j in range(4)], False, q % 2 == 1)
+            if k % 4 == 0:
+                both(o, P(b), bias=-768.0)
+            else:
+                both(a("Q%d" % hv), P(b), bias=-7.5 if k == 7 else -103.5)
+                tt(o, P(b), a("Q%d" % hv), A.subtract)
+        if k < 7:
+            outgoing(s, k + 1)
+        if k % 4 == 3:
+            for hv in range(2):
+                for j in range(4):
+                    b = (4, 5, 7)[(8 * s + 4 * hv + j) % 3]
+                    mms([(P(b), a("NID"), a(w, 16 + 512 * hv, 528 + 512 * hv)), (P(b), a("ID"), a(gs, 2048 * hv + j, 2048 * hv + 2048, 4))])
+                    act(a("D", 512 * j, 512 * j + 512), P(b), F.Abs)
+                    c0 = 128 * hv + 32 * s + j
+                    mms([(P(6, c0 + 256 * pb + 64 * bb, c0 + 256 * pb + 64 * bb + 32 - j, 4), a("D", 512 * j + 256 * bb + pb, 512 * j + 256 * bb + 256, 2),
+                          a("SEL", 0, 8)) for bb in range(2) for pb in range(2)], False, s == 1 and hv == 1 and j == 3)
+
+    def control(t):
+        w = [Wn(s, 0) for s in range(2)]
+        th = 8 if t == 0 else 0
+        for s in range(2):
+            mms([(P(0, 0, 64), h64("BW", 79 - 64 * s - u, 207 - 64 * s - u), h64(w[s], 16 + 64 * u, 80 + 64 * u)) for u in range(16)], s == 0, s == 1)
+        ts(a("FLK"), P(0, 0, 64), col("PL", th), A.is_lt)
+        tt(a("S1", 0, 64), a("FLK"), a("DIFK"), A.mult)
+        tt(a("S1", 0, 64), a("S1", 0, 64), a("DZ", 0, 64), A.add)
+        ts(a("LKA"), a("S1", 0, 64), -1.0, A.add)
+        scatter("Z", "LKA", 64, "ONEP")
+        mms([(P(0, 0, 48), spd(t, m), a("Z", 8192 + 8 * m, 14336, 128)) for m in range(16)])
+        tt(a("OKA"), a("OH"), P(0, 0, 48), A.subtract)
+        send("OKA", 16, "AR", 0, 1, "al%d" % t, "la")
+        mms([(P(2, 0, 128, 1, 0, 64), h64("BX", 63 - 8 * q - 4 * s, 127 - 8 * q - 4 * s), h64(w[s], 16 + 256 * (q % 4) + q // 4, 272 + 256 * (q % 4), 2))
+             for s in range(2) for q in range(8)])
+        ts(h64("ZX"), P(2, 0, 128, 1, 0, 64), col("PX", t, 64), A.is_lt, 100.0, A.mult)
+        for s in range(2):
+            mms([(P(1), h64("BAND", 72 - 64 * s - 8 * b, 200 - 64 * s - 8 * b), h64(w[s], 16 + b, 1040, 2)) for b in range(2)], s == 0, s == 1)
+        act(a("STH"), P(1), F.Sign, col("PL", 12 + t), -1.0)
+        act(a("STH"), a("STH"), F.Relu)
+        scan(a("MN"), a("RST"), P(6), 0.0, A.mult, A.min)
+        ts(a("N1", 0, 64), a("MN", 7, 512, 8), 4096.0, A.add)
+        ts(a("N1", 0, 64), a("N1", 0, 64), 0x1807, A.bitwise_and)
+        cp(a("C0"), a("N1", 0, 64))
+        mm(P(4, 0, 128, 1, 0, 64), a("C0"), a("ID"))
+        tt(h64("CX"), h64("ZX"), P(4, 0, 128, 1, 0, 64), A.max)
+        for b2 in range(2):
+            mms([(P(2 + b2, 256 * bb + b, 256 * bb + 256, 2), h64("XR", 128 * (4 * b + 2 * b2 + bb), 128 * (4 * b + 2 * b2 + bb) + 128), h64("CX"))
+                 for b in range(2) for bb in range(2)])
+            both(a("WB", 16 + 512 * b2, 528 + 512 * b2), P(2 + b2))
+        tt(a("BO"), ix(a("WB", 0, 1040), a("LI")), a("TAB"), A.is_equal)
+        send("BO", 256, "WB", 1040, -1, "be%d" % t, "lb")
+        mms([(P(0), a("LBM", 128 * b, 128 * b + 128), a("WB", 16 + b, 1040, 2)) for b in range(2)])
+        act(a("K1"), P(0), F.Abs, col("COL", 10))
+        act(a("K1"), a("K1"), F.Relu, 1.0, -1.0)
+        tt(a("S2", 0, 48), a("IH"), a("AR"), A.is_gt)
+        tt(a("S2", 0, 48), a("S2", 0, 48), a("DIFI"), A.mult)
+        tt(a("S2", 0, 48), a("S2", 0, 48), a("DZ", 0, 48), A.add)
+        ts(a("LGI"), a("S2", 0, 48), -1.0, A.add)
+        scatter("Z", "LGI", 48, "ONEP")
+        tt(a("FG", 0, 48), a("AR"), a("IH"), A.is_gt)
+        mm(P(7, 0, 48), a("ONESB"), a("FG", 0, 48))
+        vop(col("NOP", 0), [P(7, 0, 48)], lambda q: q.tensor_reduce(ap(col("NOP", 0)), ap(P(7, 0, 48)), AxisListType.X, A.add))
+        mms([(P(1), a("ID"), a("VAC")), (P(1), a("ID"), a("K1"))], True, False)
+        for r0 in range(0, 16, 4):
+            mms([(P(1), spd(t, r), a("Z", r, 8192, 16)) for r in range(r0, r0 + 4)], False, r0 == 12)
+        tt(a("F1"), P(1), a("STH"), A.min)
+        both(P(1), P(1), F.Relu, 1.0, -1.0, (0.5, A.is_lt))
+        mm(P(2), a("ONESB"), a("F1"))
+        mm(P(3), a("TRIC"), a("F1"))
+        scan(a("REM", 1, 513), a("ONE", 0, 512), P(2), -3072.0, A.mult, A.subtract)
+        tt(a("FT", 0, 512), P(3), a("REM", 0, 512), A.is_lt)
+        tt(a("A1"), a("A1"), P(1), A.mult)
+        for i in range(16):
+            both(a("G%d" % (i // 8), 512 * (i % 8), 512 * (i % 8) + 512), ix(a("WB"), a("LB", 32 * i, 32 * i + 32)))
+        for q in range(4):
+            mms([(P(6, 128 * q, 128 * q + 128), spd(0, u), a("G%d" % (q // 2), 2048 * (q % 2) + u, 2048 * (q % 2) + 2048, 16)) for u in range(16)], q == 0, q == 3)
+        mms([(P(7, 0, 48), spd(0, m), a("WB", 1040 + m, 1808, 16)) for m in range(16)])
+        tt(a("OH"), a("OKA"), P(7, 0, 48), A.is_gt)
+        both(a("FR"), a("OH", 16 * t, 16 * t + 16), bias=1.0, scale=-1.0)
+        mm(P(4, 0, 16), a("ONESB"), a("FR"))
+        mm(P(4, 16, 32), a("TRIC"), a("FR"))
+        scan(a("RM2", 1, 17), a("ONE", 0, 16), P(4, 0, 16), -3968.0, A.mult, A.subtract)
+        tt(a("FT", 512, 528), P(4, 16, 32), a("RM2", 0, 16), A.is_lt)
+        tt(a("FB"), P(6), a("CB"), A.is_equal)
+        for b in range(2):
+            c0 = 32 * (8 * b + t)
+            tt(a("FB", c0, c0 + 32), a("FB", c0, c0 + 32), a("FLK", b, 64, 2), A.max)
+        mm(P(0), a("POW2"), a("FB"))
+        both(a("WD"), P(0))
+        both(a("WJ"), ix(a("WD"), a("LW%d" % t)))
+        mms([(P(7, 0, 32), view("BP", m), a("WJ", m, 512, 16)) for m in range(16)])
+        both(a("WF"), P(7, 0, 32), bias=0.25)
+        tt(a("T1"), ix(a("WF"), a("LM")), a("POW%d" % t), A.mult)
+        ts(P(7), a("T1"), 1.5 * 2 ** 23, A.add, 1.5 * 2 ** 23, A.subtract)
+        tt(a("FG", 48, 560), P(7), a("T1"), A.is_gt)
+        both(P(6), a("FB"), bias=1.0, scale=-1.0)
+        tt(a("BM"), a("B1"), P(6), A.mult)
+        mm(P(2), a("ID32"), a("TABT", 0, 512), True, False)
+        mm(P(2), a("TRIQ"), a("FT", 0, 512), False, True)
+        mm(P(3, 0, 32), a("TRIQ"), a("FT", 512, 544))
+        offsets("FT", 34, "T", 4, 5, True)
+        both(a("PAY", 0, 512), P(2))
+        tt(a("PAY", 512, 544), P(3, 0, 32), a("TABT", 512, 544), A.add)
+        ends("LE", 34, "T", 1152)
+        pack("T", 34, 1152)
+        both(a("HIT"), a("ZT"), F.Relu, 0.0, -32.0, (-32.0, A.mult, 0.0, A.max))
+        mms([(P(0, 0, 72), view("BS32", m), a("YT", 72 * m, 72 * m + 72)) for m in range(16)])
+        ts(a("N3", 0, 72), P(0, 0, 72), -1.0, A.mult)
+        ts(a("N4", 0, 72), a("N3", 0, 72), 0x3F80, A.bitwise_and)
+        cp(a("HI", 0, 72), a("N4", 0, 72))
+        ts(a("N5", 0, 72), a("N3", 0, 72), 127, A.bitwise_and)
+        cp(a("LO", 0, 72), a("N5", 0, 72))
+        for b, bank in enumerate((0, 1, 6)):
+            mr = range(7 * b, min(16, 7 * b + 7))
+            mms([(P(bank, 72 * (m - 7 * b), 72 * (m - 7 * b) + 72), spd(m, 2 + 2 * t + pl), a(("HI", "LO")[pl], 0, 72)) for m in mr for pl in range(2)])
+            both(a("VT", 504 * b, 504 * b + 72 * len(mr)), P(bank, 0, 72 * len(mr)))
+        mm(P(2), a("ID32"), a("TABG%d" % t, 0, 512), True, False)
+        mm(P(2), a("TRIQ"), a("FG", 0, 512), False, True)
+        mm(P(3, 0, 64), a("TRIQ"), a("FG", 512, 576))
+        offsets("FG", 36, "G", 4, 5)
+        both(a("PAYG", 0, 512), P(2))
+        tt(a("PAYG", 512, 576), P(3, 0, 64), a("TABG%d" % t, 512, 576), A.add)
+        if t == 0:
+            ends("LE2", 3, "G", 768)
+        pack("G", 36, 1152)
+        mms([(P(7, 0, 72), view("BS32", m), a("YG", m, 1152, 16)) for m in range(16)])
+        for b, (lo, hi) in enumerate(((0, 512), (512, 1024), (1024, 1152))):
+            mm(P(3 + b, 0, hi - lo), a("NID"), a("HIT", lo, hi), True, False)
+            mm(P(3 + b, 0, hi - lo), a("ONESB32"), a("YG", lo, hi), False, True)
+            scan(a("FL", lo, hi), a("HIT", lo, hi), P(3 + b, 0, hi - lo), 0.0 if b == 0 else col("FL", lo - 1), A.min, A.max)
+        both(P(2), a("A1"), bias=-1.0 * t)
+        tt(a("FGI"), ix(a("FL"), a("LE", 0, 34)), a("FT"), A.mult)
+        ts(a("FGI"), a("FGI"), MASK, A.bitwise_and)
+        tt(a("A1"), a("FGI", 0, 512), P(2), A.add)
+        if t == 0:
+            lists_a(0)
+        else:
+            dmas("S", [(T.yd[:], a("A1"))])
+        n = [a("N%d" % i, 0, 72) for i in (6, 7, 8)]
+        ts(n[0], P(7, 0, 72), -1.0, A.add)
+        ts(n[1], n[0], MASK, A.bitwise_and)
+        tt(n[0], n[1], a("DZ0"), A.min)
+        ts(n[1], n[0], 15, A.bitwise_and)
+        ts(n[2], n[0], 4, A.arith_shift_right, 31, A.bitwise_and)
+        ts(n[1], n[1], 31.0, A.mult)
+        ts(n[2], n[2], -15.0, A.mult)
+        tt(n[0], n[0], n[1], A.add)
+        tt(n[0], n[0], n[2], A.add)
+        cp(a("LZ"), n[0])
+        scatter("Z", "LZ", 72, "VT", 18)
+        for e, bank in enumerate((7, 6)):
+            lo, hi = 256 * e, 256 * e + 256
+            mms(([(P(bank, 0, 256), row("ONE", 0, 128), row("NEG1", 0, 256))] if t == 1 else [])
+                + [(P(bank, 0, 256), view("BP", u, 144 * (1 + t)), a("Z", 512 * u + lo, 512 * u + hi)) for u in range(16)])
+            tt(a("B1" if t == 0 else "YB", lo, hi), a("BM", lo, hi), P(bank, 0, 256), A.add)
+            if t == 1:
+                for c in range(2):
+                    dmas("YS"[c], [(T.ya[r::16, :], a("YB", 32 * r, 32 * r + 32)) for r in range(8 * e + 4 * c, 8 * e + 4 * c + 4)])
+        if t == 1:
+            return
+        ts(a("S3", 0, 16), a("FGI", 512, 528), 0.0, A.is_gt)
+        tt(a("OH", 0, 16), a("OH", 0, 16), a("S3", 0, 16), A.max)
+        both(a("YT", 0, 768), a("YT", 0, 768), bias=M20, scale=-1.0)
+        both(a("HIG"), a("ZG", 0, 768), F.Relu, 0.0, -32.0, (-32.0, A.mult, 0.0, A.max))
+        for b, (lo, hi) in enumerate(((0, 512), (512, 768))):
+            mms([(P(4 + b, 0, hi - lo), a("NID"), a("HIG", lo, hi)), (P(4 + b, 0, hi - lo), a("ONESB32"), a("YT", lo, hi))])
+            scan(a("FL2", lo, hi), a("HIG", lo, hi), P(4 + b, 0, hi - lo), 0.0 if b == 0 else col("FL2", lo - 1), A.min, A.max)
+        mms([(P(6, 0, 48), spd(0, m), a("BO", m, 768, 16)) for m in range(16)])
+        tt(a("N4", 0, 48), ix(a("FL2"), a("LE2", 0, 3)), a("FG", 0, 48), A.mult)
+        ts(a("N4", 0, 48), a("N4", 0, 48), MASK, A.bitwise_and)
+        tt(a("KEEP"), a("AR"), P(6, 0, 48), A.is_gt)
+        tt(a("IE1"), a("IE1"), a("KEEP"), A.mult)
+        tt(a("IE1"), a("IE1"), a("N4", 0, 48), A.add)
+        ts(a("IH"), a("IE1"), 0.0, A.is_gt)
+
+    ts(a("A1"), a("DEN"), 1.0, A.add)
+    lists_a(0)
+    for s in range(2):
+        both(a(Wn(s, 0), 16, 1040), a("XL%d" % s), bias=96.0)
+    invert("AXO", "OH")
+    ts(a("VO"), a("N2", 0, 48), 16.0, A.add)
+    for s in range(2):
+        mm(P(2 + s, 0, 48), h64("SUM32", s=s), h64("VO", s=s))
+        cp(a("LO%d" % s), P(2 + s, 0, 48))
+        outgoing(s, 0)
+    cp(row("PARF", 0, 6, 8), row("PARI", 0, 6, 8))
+    mm(P(7, 0, 6), row("R8", 0, 128, 8), row("PARF", 0, 6, 8))
+    mm(P(7, 8, 14, 1, 0, 64), row("R8X", 0, 64, 8), row("PARF", 0, 6, 8))
+    cp(a("PL", 0, 6), P(7, 0, 6))
+    ts(a("PL", 8, 11), P(7, 0, 3), 1536.0, A.add)
+    ts(col("PL", 12), P(7, 1, 2), 1535.5, A.add)
+    ts(col("PL", 13), P(7, 1, 2), -0.5, A.add)
+    cp(col("PX", 1, 64), P(7, 10, 11, 1, 0, 64))
+    ts(col("PX", 0, 64), P(7, 10, 11, 1, 0, 64), 1536.0, A.add)
+    invert("DEN", "IH")
+    act(a("SGA"), a("INV", 0, 784), F.Sign, bias=-0.5)
+    act(a("SGB"), a("INV", 0, 784), F.Sign, bias=M20 - 0.5, scale=-1.0)
+    mms([(P(4, 0, 48), view("BJ", m), a(n, 1 + m, 769, 16)) for n in ("SGA", "SGB") for m in range(16)])
+    ts(a("S1", 0, 48), a("N2", 0, 48), 8.0, A.mult, 1.0, A.add)
+    tt(a("S1", 0, 48), a("S1", 0, 48), P(4, 0, 48), A.add)
+    tt(a("IE1"), a("S1", 0, 48), a("IH"), A.mult)
+    ts(a("B1"), a("BH"), 1.0, A.add)
+    for t in range(2):
+        order_tables(t)
+        round_tables(t)
+        for k in range(4 * t, 4 * t + 4):
+            for s in range(2):
+                step(s, k)
+        if t == 1:
+            dmas("Y", [(T.yx[64 * s:64 * s + 64, :], h64(Wn(s, 0), 16, 1040)) for s in range(2)])
+        control(t)
+    emit()

@@ -4,21 +4,21 @@ from concourse.mybir import AluOpType as A, ActivationFunctionType as F, AxisLis
 
 B16, F32, I32, U16 = "bfloat16", "float32", "int32", "uint16"
 _SB = {
-    B16: dict(W00=1808, W01=1808, W10=1808, W11=1808, WB=1808, G0=4096, G1=4096, D=2048, OB0=768, OB1=768, BO=768, Z=15872, XL0=1024, XL1=1024,
-              Q0=512, Q1=512, ONE=576, DEC=1152, C15=512, NEG1=512, TIE=512, RST=512, ONESB=128, TRI=128, TRIQ=128, TRIC=128, DM=128, BW=208, BAND=208,
-              SPD=2304, SPR=2048, BP=432, BJ=144, SUM=128, S17=128, ID=128, NID=128, NBIG=128, SEL=16, PT=128, BX=128, XR=1024, LBM=256, POW2=128, TA=128, TB=128,
-              FT=544, FG=576, FI=512, F1=512, HELD=512, VAC=512, K1=512, STH=512, FB=512, WD=512, WJ=512, UH=512, POW0=512, POW1=512, ONEP=1024,
-              HIT=1152, HIG=768, VT=1152, TAB=768, SGA=784, SGB=784, C0=64, CX=128, CT=48, CG=48, OH=48, OKA=48, AR=48, IH=48, FR=16, HI=80, LO=80, TL=48,
-              FLK=64, KEEP=48, EX=16),
-    F32: dict(ONEF=144, ID32=128, ONESB32=128, BS32=144, SUM32=128, PA=136, R8=128, R8X=64, PARF=8, PL=16, PX=8, COL=16, J=512, TABV=512, DUM=72, DZ=72, DZ0=72,
-              DT=72, DG=72, DI=72, A1=512, BM=512, T1=512, T2=512, YB=512, MN=512, REM=528, PAY=544, PAYG=576, TABT=544, TABG0=576, TABG1=576, WT=2304, WG=10112,
-              INV=1936, ZT=1152, ZG=1152, YT=1152, YG=1152, FL=1168, FL2=784, ZX=128, WF=32, XT=48, PPT=48, ZZT=48, OOT=48, XG=48, PPG=48, ZZG=48, OOG=48,
-              ZZ=80, EQ=80, OO=80, IE1=48, DIFI=48, DIFK=64, S1=72, S2=72, S3=72, S4=72, NOP=8, RM2=32, VO=48),
-    I32: dict(DEN=512, AXO=512, BH=512, B1=512, CB=512, UI=512, FGI=544, PARI=8, PI=8, N1=80, N2=80, N3=80, N4=80, N5=80, N6=80, N7=80, N8=80),
+    B16: dict(W00=1808, W01=1808, W10=1808, W11=1808, WB=1808, G0=4096, G1=4096, D=2048, OB0=768, OB1=768, BO=768, Z=15488, XL0=1024, XL1=1024,
+              Q0=512, Q1=512, ONE=576, DEC=1152, C15=512, TIE=512, RST=512, BLK=208, TS=128, DMP=128, TRIQ=128, TRIC=128, PARD=128, NHM=128, BW=208,
+              BWP=144, BAND=208, SPD=288, SPR=2048, BJ=144, SUM=128, S17=128, ID=128, NID=128, NBIG=128, PBIG=128, HB=64, SEL=16, PT=128, BX=128,
+              XR=1024, LBM=256, TB=128, FT=544, FG=576, FI=512, F1=512, HELD=512, K1=512, STH=512, FB=512, WJ=512, UH=512, POW0=512, POW1=512,
+              ONEP=256, HIT=1152, SG=1152, HIG=768, TAB=768, SGA=768, SGB=768, C0=64, CX=128, CT=48, CG=48, OH=48, OKA=48, AR=48, IH=48, FR=16,
+              TL=48, FLK=64, KEEP=48, EX=16),
+    F32: dict(ONEF=144, ID32=128, ONES32=128, NID32=128, N8K=128, N16K=128, BS32=144, SUM32=128, PA=136, R8=128, R8X=64, E8=128, PARF=8, PL=16,
+              PX=8, COL=16, J=512, DS=72, DZ=72, DZ0=72, DT=72, DG=72, A1=512, B1=512, BM=512, T1=512, T2=512, MN=512, REM=528, PAY=544, PAYG=576,
+              TABT=544, TABG0=576, TABG1=576, CI=128, TLK=48, WT=1808, WG=10624, ROW=9472, INV=4096, ZT=1152, ZG=1152, YT=1152, YG=1152, FL=1152,
+              FL2=768, ZX=128, WF=32, D0=48, PPT=48, OOT=48, PPG=48, OOG=48, OO=80, IE1=48, S1=72, S2=72, S3=72, S4=72, RM2=32, VO=48),
+    I32: dict(DEN=512, AXO=512, BH=512, CB=512, UI=208, FGI=544, PARI=8, PI=8, N1=80, N2=80, N3=80, N4=80, N5=80, N6=80, N7=80, N8=80),
     U16: dict(LA=512, LB=512, LO0=48, LO1=48, LI=48, LKA=64, LGI=48, LST=48, LSG=48, LS=48, LE=48, LE2=8, LZ=72, LW0=32, LW1=32, LM=32),
 }
-_ALIAS = dict(XL0=("G0", 0), XL1=("G1", 0), SGA=("D", 0), SGB=("D", 784), ZG=("WG", 1152), YG=("WG", 2304), WT=("WG", 3456), INV=("WG", 5760),
-              T1=("WG", 7696), T2=("WG", 8208), MN=("WG", 8720), YB=("WG", 9232))
+_ALIAS = dict(XL0=("G0", 0), XL1=("G1", 0), SGA=("D", 0), SGB=("D", 784), ROW=("WG", 1152), WT=("WG", 1152), INV=("WG", 2960),
+              T1=("WG", 7056), T2=("WG", 7568), MN=("WG", 8080))
 PLACE, SCRATCH = {}, {}
 for _d, _t in _SB.items():
     _o = 0
@@ -35,12 +35,18 @@ for _d, _t in _SB.items():
 for _i in range(8):
     SCRATCH["P%d" % _i] = ("psum", [128, 512], F32)
     PLACE["P%d" % _i] = ("P%d" % _i, 0, 512)
-SEMAPHORES = (["cV", "cS", "cP", "cG", "l0", "l1", "la", "lb"] + ["x%d" % i for i in range(16)] + ["al0", "al1", "be0", "be1"] + ["d%d" % i for i in range(16)])
+PLACE["ONESB"] = (PLACE["BLK"][0], PLACE["BLK"][1] + 64, 128)
+SCRATCH["YS"] = ("dram", [128, 512], F32)
+PLACE["YS"] = ("YS", 0, 512)
+SEMAPHORES = (["cV", "cS", "cP", "cG", "cX", "l0", "l1", "la", "lb"] + ["x%d" % i for i in range(16)] + ["al0", "al1", "be0", "be1"]
+              + ["d%d" % i for i in range(16)])
 M20, M24 = float(2 ** 20), float(2 ** 24)
-MASK = 2 ** 20 - 1
-LN2 = math.log(2.0)
-CY, GCY, PECY, HOP, FAR, HALF, LOOK, GAP, PIECE, TURNS = 1.04e-3, 1.4e-3, 0.55e-3, 0.13, 4.3, 0.7, 0.8, 1.0, 128, 30
-SHY = ({"V": 6.0, "S": 3.0}, {"V": 12.0, "S": 12.0}, {"V": 2.0, "S": 1.0})
+MASK, FLAG = 2 ** 20 - 1, 3 * 2 ** 18
+LN2, RND = math.log(2.0), 1.5 * 2 ** 23
+COSTS = ((0.05, 0.83e-3, 1.3e-3, 3.15e-3, 0.42e-3, 0.08, 4.0, 1.0), (0.06, 1.04e-3, 1.6e-3, 4e-3, 0.53e-3, 0.1, 4.2, 1.0),
+         (0.05, 0.9e-3, 1.2e-3, 4.5e-3, 0.45e-3, 0.12, 6.5, 1.5), (0.06, 1.1e-3, 2.1e-3, 2.5e-3, 0.6e-3, 0.1, 5.0, 1.2))
+HALF, LOOK, GAP, PIECE, TURNS, MOVES, HEAT = 0.7, 0.7, 0.8, 128, 700, 8000, 0.001
+SHY, LIFT = {"V": 8.0, "S": 4.0}, (-8.0, -3.0, -1.0, 1.0, 3.0, 8.0)
 ORDER = []
 
 
@@ -50,11 +56,11 @@ def rank_program(g, core, T, topo):
         return
     N = len(T.cores)
     QU = {"V": g.vector, "S": g.scalar, "P": g.tensor, "G": g, "Y": g.sync}
-    nodes, rec, nd, lsum, chain = [], {}, [0], {}, []
+    nodes, rec, nd, lsum, chain, half, part = [], {}, [0], {}, [], [0], [0]
 
-    def a(n, lo=0, hi=None, st=1, p0=0, p1=128):
+    def a(n, lo=0, hi=None, st=1, p0=0, p1=128, ps=1):
         b, o, w = PLACE[n]
-        return (b, o + lo, o + (w if hi is None else hi), st, p0, p1)
+        return (b, o + lo, o + (w if hi is None else hi), st, p0, p1, ps)
 
     def h64(n, lo=0, hi=None, st=1, s=0):
         return a(n, lo, hi, st, 64 * s, 64 * s + 64)
@@ -64,6 +70,8 @@ def rank_program(g, core, T, topo):
             return x
         if x[0] == "@":
             return ap(x[1]).indirect(ap(x[2]))
+        if x[6] != 1:
+            return T[x[0]][x[4]:x[5]:x[6], x[1]:x[2]]
         return T[x[0]][x[4]:x[5], x[1]:x[2]:x[3]] if x[3] != 1 else T[x[0]][x[4]:x[5], x[1]:x[2]]
 
     def flat(xs):
@@ -76,7 +84,7 @@ def rank_program(g, core, T, topo):
     def psum(x):
         return SCRATCH[x[0]][0] == "psum"
 
-    def node(ways, rd, wr, lat=0.0, tok=None, after=()):
+    def node(ways, rd, wr, lat=(0, 0, 0), tok=None, after=()):
         me, dep = len(nodes), set(after)
         for kind, xs in (("r", rd), ("w", wr)):
             for x in xs:
@@ -88,11 +96,14 @@ def rank_program(g, core, T, topo):
                 old = rec.get(x[0], [])
                 if psum(x):
                     old = []
-                elif kind == "w" and x[3] == 1 and x[4] == 0 and x[5] == 128:
+                elif kind == "w" and x[3:] == (1, 0, 128, 1):
                     old = [r for r in old if not (x[1] <= r[0] and r[1] <= x[2])]
                 rec[x[0]] = old + [(x[1], x[2], kind, me)]
-        nodes.append(dict(ways=ways, dep=sorted(dep), lat=lat, tok=tok))
+        nodes.append(dict(ways=ways, part=part[0], dep=sorted(dep), lat=lat, tok=tok))
         return me
+
+    def mark():
+        part[0] += 1
 
     def size(x):
         return (x[2] - x[1] + x[3] - 1) // x[3]
@@ -101,16 +112,16 @@ def rank_program(g, core, T, topo):
         xs = [x for x in [out] + ins if isinstance(x, tuple)]
         ind = [x for x in xs if x[0] == "@"]
         if ind:
-            return 16 * size(ind[0][2]) * (3.8 if out[0] == "@" else 1.56) * CY + 0.06
+            return (1, 0, 0, 16 * size(ind[0][2]), 0) if out[0] == "@" else (1, 0, 16 * size(ind[0][2]), 0, 0)
         f = 1.0
         if e == "V" and two:
             f = 1.0 if any(psum(x) for x in xs[1:]) else 2.0
         elif e == "V" and all(SCRATCH[x[0]][2] in (B16, U16) for x in xs if size(x) > 1):
             f = 0.5
-        return max(64, max(size(x) for x in xs) * f) * CY + 0.06
+        return (1, max(64, max(size(x) for x in xs) * f), 0, 0, 0)
 
-    def op(out, ins, ways, lat=0.0):
-        node(ways, flat(ins) + ([out[2]] if out[0] == "@" else []), [out[1]] if out[0] == "@" else [out], lat)
+    def op(out, ins, ways):
+        node(ways, flat(ins) + ([out[2]] if out[0] == "@" else []), [out[1]] if out[0] == "@" else [out])
 
     def ix(w, o):
         return ("@", w, o)
@@ -153,43 +164,68 @@ def rank_program(g, core, T, topo):
             vf = tsf(o, i, scale, A.mult, bias, A.add)
         op(o, [i, bias, scale], {"S": (actf(o, i, f, bias, scale), est("S", o, [i])), "V": (vf, est("V", o, [i]))})
 
+    def pair(o, i, v, s1, s2, es="SV"):
+        def two(q):
+            half[0] += 1
+            actf(o, i, *s1)(q).then_inc(T.sem["cX"], 1)
+            q.wait_ge(T.sem["cX"], half[0])
+            return actf(o, o, *s2)(q)
+        c = est("S", o, [i])
+        ways = {"S": (two, (3, 2 * c[1], 0, 0, 0)), "V": (tsf(o, i, *v), est("V", o, [i]))}
+        op(o, [i] + list(v) + list(s1), {e: ways[e] for e in es})
+
+    def whole(o, i):
+        pair(o, i, (RND, A.add, RND, A.subtract), (F.Identity, RND, 1.0), (F.Identity, -RND, 1.0))
+
     def mms(items, start=True, stop=True):
         def fn(q):
             for i, (o, l, r) in enumerate(items):
                 last = q.matmul(ap(o), ap(l), ap(r), start and i == 0, stop and i == len(items) - 1)
             return last
-        c = sum(max(min(64, size(l)), size(r)) * (4 if SCRATCH[l[0]][2] == F32 else 1) * PECY + 0.005 for o, l, r in items)
-        node({"P": (fn, c)}, [x for o, l, r in items for x in (l, r)], [items[0][0]], 0.06)
+        c = sum(max(min(64, size(l)), size(r)) * (4 if SCRATCH[l[0]][2] == F32 else 1) + 8 for o, l, r in items)
+        node({"P": (fn, (0, 0, 0, 0, c))}, [x for o, l, r in items for x in (l, r)], [items[0][0]], (0.05, 0, 0))
 
     def mm(o, l, r, start=True, stop=True):
         mms([(o, l, r)], start, stop)
 
-    def scatter(win, lst, n, src, piece=16):
+    def scatter(win, lst, n, src, piece=16, same=False):
         for lo in range(0, n, piece):
             hi = min(n, lo + piece)
-            cp(ix(a(win), a(lst, lo, hi)), a(src, 16 * lo, 16 * hi))
+            cp(ix(a(win), a(lst, lo, hi)), a(src, 0, 16 * (hi - lo)) if same else a(src, 16 * lo, 16 * hi))
+
+    def iotaf(o, p, base, cm):
+        kw = {} if SCRATCH[o[0]][2] == I32 else {"allow_small_or_imprecise_dtypes": True}
+        return (lambda q: q.iota(ap(o), p, base, cm, **kw), (4, 2 * size(o), 0, 0, 0))
 
     def iota(o, p, base, cm):
-        kw = {} if SCRATCH[o[0]][2] == I32 else {"allow_small_or_imprecise_dtypes": True}
-        op(o, [], {"G": (lambda q: q.iota(ap(o), p, base, cm, **kw), 0.2 + 2 * size(o) * GCY)})
+        op(o, [], {"G": iotaf(o, p, base, cm)})
 
     def sel(o, i, p, base, cm, f=A.is_equal, fill=0.0):
-        op(o, [i], {"G": (lambda q: q.affine_select(ap(o), ap(i), p, f, fill, base, cm), 0.25 + 2 * size(o) * GCY)})
+        op(o, [i], {"G": (lambda q: q.affine_select(ap(o), ap(i), p, f, fill, base, cm), (5, 2 * size(o), 0, 0, 0))})
 
     def band(o, i, p, base, p2, base2):
         sel(o, i, p, base, 1, A.is_ge)
         sel(o, o, p2, base2, -1, A.is_ge)
 
-    def dmas(e, items):
+    def fill(n, lo, hi, c, piece=1024, st=1, es="SV", p1=128):
+        for l in range(lo, hi, piece * st):
+            o = a(n, l, min(hi, l + piece * st), st, 0, p1)
+            src = a("DEC", 0, size(o), 1, 0, p1)
+            ways = {"S": (actf(o, src, F.Identity, c, 0.0), est("S", o, [src])), "V": (lambda q, o=o: q.memset(ap(o), c), est("V", o, [])),
+                    "G": iotaf(o, [[0, size(o)]], int(c), 0)}
+            op(o, [src], {e: ways[e] for e in es})
+
+    def dmas(e, items, lat=2.3, after=()):
         sem = "d%d" % nd[0]
         nd[0] += 1
 
         def fn(q):
             for o, i in items:
                 q.dma_start(ap(o), ap(i)).then_inc(T.sem[sem], 16)
-        node({e: (fn, 0.1 * len(items))}, flat([i for o, i in items]), flat([o for o, i in items]), 2.5, (sem, 16 * len(items)))
+        return node({e: (fn, (2 * len(items), 0, 0, 0, 0))}, flat([i for o, i in items]), flat([o for o, i in items]), (0, 0, lat),
+                    (sem, 16 * len(items)), after)
 
-    def send(src, w, dst, off, sign, rsem, lsem):
+    def send(src, w, dst, off, sign, rsem, lsem, free=()):
         tr = []
         for h in range(1, N):
             d = T.cores[(rank + sign * h) % N]
@@ -199,72 +235,216 @@ def rank_program(g, core, T, topo):
             rid, pid = topo.addr(d, core)
             tr.append(RemoteDMATransfer(dst_ids=[DstId(rid=rid, pnc=pid)], dma_engine_mask=sum(1 << x for x in mine), remote_sem=T.sem[rsem],
                                         src=ap(a(src, w * (h - 1), w * h)), dst=ap(a(dst, off + w * (h - 1), off + w * h))))
+        first = 0.0 if lsum else 2.5
         lsum[lsem] = lsum.get(lsem, 0) + 4 * k
-        n = node({"G": (lambda q: q.remote_dma_fused(tr, local_sem=T.sem[lsem]), 0.8)}, [a(src)], [], FAR - 0.8, (lsem, lsum[lsem]))
-        node({"R": (None, 0.0)}, [], [a(dst, off, off + 3 * w)], 0.0, (rsem, 4 * k), [n])
+        n = node({"G": (lambda q: q.remote_dma_fused(tr, local_sem=T.sem[lsem]), (14 + 20 * first, 0, 0, 0, 0))}, [a(src)], list(free),
+                 (0, 0.8 if w > 64 else 0.6, 0), (lsem, lsum[lsem]))
+        node({"R": (None, (0, 0, 0, 0, 0))}, [], [a(dst, off, off + 3 * w)], (0, 0, 0), (rsem, 4 * k), [n])
 
     def schedule():
-        n = len(nodes)
-        fwd, bwd = [[] for _ in nodes], [[] for _ in nodes]
-        for u, x in enumerate(nodes):
-            for d in x["dep"]:
-                ways = nodes[d]["ways"]
-                gap = 0.0 if "P" in ways and "P" in x["ways"] else nodes[d]["lat"] + (0.0 if "R" in ways else HOP)
-                fwd[d].append((u, gap))
-                bwd[u].append((d, gap))
+        n, ES = len(nodes), "RPGYVS"
+        views = []
+        for m in COSTS:
+            cost = [{e: sum(x * y for x, y in zip(c, m)) for e, (f, c) in x["ways"].items()} for x in nodes]
+            lat = [x["lat"][0] + x["lat"][1] * m[6] + x["lat"][2] * m[7] for x in nodes]
+            fwd, bwd = [[] for _ in nodes], [[] for _ in nodes]
+            for u, x in enumerate(nodes):
+                for d in x["dep"]:
+                    gap = 0.0 if "P" in cost[d] and "P" in cost[u] else lat[d] + (0.0 if "R" in cost[d] else m[5])
+                    fwd[d].append((u, gap))
+                    bwd[u].append((d, gap))
+            views.append((cost, lat, fwd, bwd))
 
-        def run(out, into, link, prio, first, shy):
+        def replay(order, view):
+            cost, lat, fwd, bwd = view
+            free, fin = dict.fromkeys(ES, 0.0), [0.0] * n
+            for i, e in order:
+                t = free[e]
+                for d, gap in bwd[i]:
+                    if fin[d] + gap > t:
+                        t = fin[d] + gap
+                free[e] = fin[i] = t + cost[i][e]
+            return max(fin[i] + lat[i] for i in range(n))
+
+        def run(cost, out, into, link, prio, first, shy):
             nxt = dict(zip(link, link[1:]))
             left = [len(into[i]) for i in range(n)]
             for i in link[1:]:
                 left[i] += 1
             rdy = list(first)
-            ready = {e: set() for e in "RPGYVS"}
-            free = {e: 0.0 for e in "RPGYVS"}
+            ready = {e: set() for e in ES}
+            free = dict.fromkeys(ES, 0.0)
             order, fin = [], [0.0] * n
-            key = {e: [prio[i] - (shy.get(e, 0.0) if len(nodes[i]["ways"]) > 1 else 0.0) - 1e-7 * i for i in range(n)] for e in "RPGYVS"}
+            key = {e: [prio[i] - (shy.get(e, 0.0) if len(cost[i]) > 1 else 0.0) - 1e-7 * i for i in range(n)] for e in ES}
             for i in range(n):
                 if left[i] == 0:
-                    for e in nodes[i]["ways"]:
+                    for e in cost[i]:
                         ready[e].add(i)
             while len(order) < n:
-                t0, e = min((max(free[e], min(rdy[i] for i in ready[e])), j, e) for j, e in enumerate("RPGYVS") if ready[e])[::2]
+                t0, e = min((max(free[e], min(rdy[i] for i in ready[e])), j, e) for j, e in enumerate(ES) if ready[e])[::2]
                 ke = key[e]
                 i = max((i for i in ready[e] if rdy[i] <= t0 + 0.05), key=lambda j: ke[j])
-                soon = [j for j in ready[e] if t0 + 0.05 < rdy[j] <= t0 + min(LOOK, nodes[i]["ways"][e][1]) and ke[j] > ke[i] + GAP]
+                soon = [j for j in ready[e] if t0 + 0.05 < rdy[j] <= t0 + min(LOOK, cost[i][e]) and ke[j] > ke[i] + GAP]
                 if soon:
                     i = max(soon, key=lambda j: ke[j])
-                for x in nodes[i]["ways"]:
+                for x in cost[i]:
                     ready[x].discard(i)
-                free[e] = fin[i] = max(t0, rdy[i]) + nodes[i]["ways"][e][1]
+                free[e] = fin[i] = max(t0, rdy[i]) + cost[i][e]
                 order.append((i, e))
                 for u, t1 in [(u, fin[i] + gap) for u, gap in out[i]] + ([(nxt[i], t0)] if i in nxt else []):
                     rdy[u] = max(rdy[u], t1)
                     left[u] -= 1
                     if left[u] == 0:
-                        for x in nodes[u]["ways"]:
+                        for x in cost[u]:
                             ready[x].add(u)
-            return max(fin[i] + nodes[i]["lat"] for i in range(n)), order, fin
+            return order, fin
 
-        level = [0.0] * n
+        seed, unit = 1, [1.0] * len(views)
         nxt = dict(zip(chain, chain[1:]))
+        cost, lat, fwd, bwd = views[0]
+        level = [0.0] * n
         for i in range(n - 1, -1, -1):
-            level[i] = min(c for f, c in nodes[i]["ways"].values()) + max([level[u] + gap for u, gap in fwd[i]] + [nodes[i]["lat"]])
+            level[i] = min(cost[i].values()) + max([level[u] + gap for u, gap in fwd[i]] + [lat[i]])
             if i in nxt:
-                level[i] = max(level[i], level[nxt[i]] + HALF * nodes[i]["ways"]["S"][1])
-        best, seed = None, 1
-        for shy in SHY:
-            prio = level
-            for it in range(TURNS):
-                got = run(fwd, bwd, chain, prio, [0.0] * n, shy)
-                if best is None or got[0] < best[0]:
-                    best = got
-                back = run(bwd, fwd, chain[::-1], (best if it % 3 == 2 else got)[2], [x["lat"] for x in nodes], shy)[2]
-                prio = []
-                for x in back:
+                level[i] = max(level[i], level[nxt[i]] + HALF * cost[i]["S"])
+
+        def forward(prio):
+            order, fin = run(cost, fwd, bwd, chain, prio, [0.0] * n, SHY)
+            ends = [replay(order, v) for v in views]
+            return sum(x / y for x, y in zip(ends, unit)), order, ends, fin
+        unit = forward(level)[2]
+        best, base, lift = forward(level), level, [0.0] * (part[0] + 1)
+        for it in range(TURNS):
+            seed = seed * 48271 % 2147483647
+            if it % 12 == 11:
+                prio, new = run(cost, bwd, fwd, chain[::-1], best[3], lat, SHY)[1], [0.0] * len(lift)
+            else:
+                prio, new = base, list(lift)
+                for k in range(1 + seed % 2):
                     seed = seed * 48271 % 2147483647
-                    prio.append(x + seed / 2147483647)
-        return best[1]
+                    new[seed % len(new)] += LIFT[(seed >> 10) % len(LIFT)]
+            got = forward([prio[i] + new[nodes[i]["part"]] for i in range(n)])
+            if got[0] <= best[0]:
+                best, base, lift = got, prio, new
+        order, eng = [i for i, e in best[1]], [None] * n
+        for i, e in best[1]:
+            eng[i] = e
+        deps = [[d for d, gap in bwd[i]] for i in range(n)]
+        subs = [[u for u, gap in fwd[i]] for i in range(n)]
+
+        def times():
+            out = []
+            for cost, lat, fwd, bwd in views:
+                fin, rest, free = [0.0] * n, [0.0] * n, dict.fromkeys(ES, 0.0)
+                for i in order:
+                    e = eng[i]
+                    t = free[e]
+                    for d, gap in bwd[i]:
+                        if fin[d] + gap > t:
+                            t = fin[d] + gap
+                    free[e] = fin[i] = t + cost[i][e]
+                free = dict.fromkeys(ES, 0.0)
+                for i in reversed(order):
+                    e = eng[i]
+                    t = max(free[e], lat[i])
+                    for u, gap in fwd[i]:
+                        if rest[u] + gap > t:
+                            t = rest[u] + gap
+                    free[e] = rest[i] = t + cost[i][e]
+                out.append((fin, rest, max(rest)))
+            return sum(x[2] / w for x, w in zip(out, unit)), out
+
+        def guess(lo, hi, span):
+            before, after, rise = {}, {}, 0.0
+            for p in range(lo - 1, -1, -1):
+                before.setdefault(eng[order[p]], order[p])
+                if len(before) == 4 and lo - p > 60:
+                    break
+            for p in range(hi + 1, n):
+                after.setdefault(eng[order[p]], order[p])
+                if len(after) == 4 and p - hi > 60:
+                    break
+            for (cost, lat, fwd, bwd), (fin, rest, end), w in zip(views, fins, unit):
+                free, new, far = {e: fin[i] for e, i in before.items()}, {}, 0.0
+                for i in span:
+                    e = eng[i]
+                    t = free.get(e, 0.0)
+                    for d, gap in bwd[i]:
+                        f = new.get(d, fin[d]) + gap
+                        if f > t:
+                            t = f
+                    free[e] = new[i] = t = t + cost[i][e]
+                    for u, gap in fwd[i]:
+                        if pos[u] > hi and t + gap + rest[u] > far:
+                            far = t + gap + rest[u]
+                for e, u in after.items():
+                    far = max(far, free.get(e, 0.0) + rest[u])
+                rise += (far - end) / w if far > end else 0.0
+            return rise
+
+        def waits(v, fin):
+            cost, lat, fwd, bwd = views[v]
+            before, last = [None] * n, {}
+            for i in order:
+                before[i], last[eng[i]] = last.get(eng[i]), i
+            i, out = max(tail, key=lambda j: fin[j] + lat[j]), []
+            while i is not None:
+                t, j = fin[i] - cost[i][eng[i]] - 1e-9, before[i]
+                tight = [d for d, gap in bwd[i] if fin[d] + gap >= t]
+                if j is not None and fin[j] >= t and j not in deps[i]:
+                    out.append((j, i))
+                    i = j
+                else:
+                    i = tight[0] if tight else None
+            return out
+        tail = [i for i in range(n) if not subs[i]]
+        score, fins = times()
+        arcs, pos = None, [0] * n
+        top = (score, list(order), list(eng))
+        for it in range(MOVES):
+            seed = seed * 48271 % 2147483647
+            if not arcs:
+                arcs = [x for v in range(len(views)) for x in waits(v, fins[v][0])]
+                for p, i in enumerate(order):
+                    pos[i] = p
+            j, i = arcs[(seed >> 8) % len(arcs)]
+            kind, pj, pi = (seed >> 4) % 4, pos[j], pos[i]
+            x = (i, j)[kind % 2]
+            e0, heat = eng[x], HEAT * (1 - it / MOVES) * (seed >> 5 & 255) / 255
+            if kind < 2:
+                step = 1 if kind else -1
+                for far in range((seed >> 16) % 8 - 3):
+                    p = (pi if kind else pj) + step
+                    while 0 <= p < n and eng[order[p]] != e0:
+                        p += step
+                    if 0 <= p < n:
+                        pj, pi = (pj, p) if kind else (p, pi)
+                span, tied = order[pj:pi + 1], {x}
+                for u in (span if kind else span[::-1]):
+                    if any(d in tied for d in (deps[u] if kind else subs[u])):
+                        tied.add(u)
+                if (order[pi] if kind else order[pj]) in tied:
+                    continue
+                one, two = [u for u in span if u in tied], [u for u in span if u not in tied]
+                span = two + one if kind else one + two
+            else:
+                other = [e for e in cost[x] if e != e0]
+                if not other:
+                    continue
+                eng[x], pj = other[(seed >> 16) % len(other)], pos[x]
+                pi, span = pj, [x]
+            if guess(pj, pi, span) <= heat:
+                was = order[pj:pi + 1]
+                order[pj:pi + 1] = span
+                new, nf = times()
+                if new <= score + heat:
+                    score, fins, arcs = new, nf, None
+                    if score < top[0]:
+                        top = (score, list(order), list(eng))
+                    continue
+                order[pj:pi + 1] = was
+            eng[x] = e0
+        return [(i, top[2][i]) for i in top[1]]
 
     def emit():
         if not ORDER:
@@ -318,61 +498,63 @@ def rank_program(g, core, T, topo):
     def Wn(s, k):
         return "W%d%d" % (s, k % 2)
 
-    dmas("Y", [(a("AXO"), T.axo[:])])
-    dmas("S", [(a("DEN"), T.den[:])])
-    dmas("Y", [(h64("XL%d" % s, s=hh), T.x0[64 * s:64 * s + 64, :]) for s in range(2) for hh in range(2)])
-    dmas("Y", [(row("PARI", 0, 6, 8), T.par[:])])
-    dmas("Y", [(a("BH", 32 * r, 32 * r + 32), T.axo[r::16, :]) for r in range(16)])
+    first = dmas("Y", [(a("AXO"), T.axo[:])])
+    dmas("S", [(a("DEN"), T.den[:])], 3.0)
+    second = dmas("Y", [(h64("XL%d" % s, s=hh), T.x0[64 * s:64 * s + 64, :]) for s in range(2) for hh in range(2)]
+                  + [(row("PARI", 0, 6, 8), T.par[:])], 2.6, [first])
+    dmas("Y", [(a("BH", 32 * r, 32 * r + 32), T.axo[r::16, :]) for r in range(16)], 4.0, [second])
 
-    ms(a("ONE"), 1.0)
-    ms(a("ONEF"), 1.0)
-    ms(a("TA"), M20)
-    ms(a("TB"), -2064.0)
-    ms(a("SEL", 8, 16), -8.0)
+    mark()
     ms(a("DEC"), -M20)
+    ms(a("ONE"), 1.0)
+    ms(a("BW"), 0.0)
+    ms(row("E8", 0, 128), 0.125)
+    fill("ONEF", 0, 144, 1.0)
+    fill("TB", 0, 128, -2064.0)
+    fill("SEL", 8, 16, -8.0)
+    iota(a("UI", 0, 208), [[-16, 13], [0, 16]], 64, 1)
+    iota(a("CI"), [[1, 128]], 0, -1)
     iota(col("PI", 0), [[0, 1]], 0, 1)
-    blk, blk2 = [[-16, 8], [0, 16]], [[16, 8], [0, 16]]
-    band(a("TRIQ"), a("TA"), blk, 0, blk2, 15)
-    sel(a("TRIQ"), a("TRIQ"), [[1, 128]], 0, -1, A.is_ge)
+    iota(a("J"), [[16, 512]], 0, 1)
+    ts(a("UI", 0, 208), a("UI", 0, 208), 4, A.arith_shift_right)
+    ts(a("BLK"), a("UI", 0, 208), 0.0, A.is_equal)
+    cp(a("BW", 15, 208, 16), a("BLK", 15, 208, 16))
+    ts(a("ID"), a("CI"), 0.0, A.is_equal)
+    sel(a("TS"), a("ONESB"), [[1, 128]], 0, -1, A.is_gt)
+    sel(a("PARD"), a("ID"), [[0, 8], [1, 2], [0, 8]], 0, 0, A.is_gt)
+    tt(a("DMP"), a("ONESB"), a("TS"), A.subtract)
+    both(a("TRIQ"), a("TS"), scale=M20)
     sel(a("TRIQ"), a("TRIQ"), [[1, 128]], 0, -1, A.not_equal, M24)
-    band(a("BW"), a("ONE", 0, 208), [[-16, 13], [1000, 16]], 64 - 15000, [[16, 13], [0, 16]], 15 - 64)
-    band(a("ONESB"), a("ONE", 0, 128), blk, 0, blk2, 15)
-    iota(a("DUM"), [[1, 72]], 0, 72)
-    iota(a("TABV"), [[2, 512]], 0, 0)
     ts(col("PI", 1), col("PI", 0), 15, A.bitwise_and)
     ts(col("PI", 2), col("PI", 0), 112, A.bitwise_and)
-    ts(col("PI", 3), col("PI", 0), 3, A.arith_shift_right, 1, A.bitwise_and)
     ts(col("PI", 6), col("PI", 0), 1, A.add)
-    ts(col("PI", 4), col("PI", 6), 7, A.bitwise_and)
-    ts(col("PI", 5), col("PI", 0), 7, A.bitwise_and)
-    cp(a("COL", 0, 5), a("PI", 1, 6))
-    ts(col("COL", 4), col("COL", 4), 0.5, A.mult)
-    ts(col("COL", 8), col("COL", 1), -72.0, A.mult)
-    ts(col("COL", 10), col("COL", 3), -1.0, A.mult)
-    ts(col("COL", 11), col("COL", 1), -1.0, A.mult)
-    ts(a("DUM"), a("DUM"), col("COL", 8), A.add)
-    both(a("TABV"), a("TABV"), bias=col("COL", 2), v=(col("COL", 2), A.add))
-    ts(a("DM"), a("ONESB"), -1.0, A.mult)
-    sel(a("DM"), a("DM"), [[-1, 128]], 0, 1, A.is_ge)
-    cp(a("BS32"), a("BW", 64, 208))
-    for n, c in (("DT", 1152.0), ("DI", 784.0), ("DZ", 14337.0), ("DG", 8960.0), ("DZ0", 14336.0)):
-        ts(a(n), a("DUM"), c, A.add)
-    ms(a("PA", 0, 8), 0.0)
+    ts(col("PI", 3), col("PI", 6), 7, A.bitwise_and)
+    ts(col("PI", 4), col("PI", 0), 7, A.bitwise_and)
+    cp(a("COL", 0, 4), a("PI", 1, 5))
+    both(col("COL", 4), col("COL", 3), scale=0.5)
+    both(a("COL", 10, 12), a("COL", 1, 3), scale=-1.0)
+    both(a("BS32"), a("BW", 64, 208))
+    for n, c in (("DT", 1152.0), ("DS", 0.0), ("DZ", 14337.0 - 16384), ("DG", 8960.0), ("DZ0", 8192.0)):
+        both(a(n), a("J", 0, 72), bias=c)
+    fill("PA", 0, 8, 0.0)
     for s in range(2):
         sel(h64("SUM", s=s), h64("ONE", 0, 128, s=s), [[0, 2], [-1, 64]], 0, 1)
-        sel(h64("SUM32", s=s), h64("ONEF", 0, 128, s=s), [[0, 2], [-1, 64]], 0, 1)
         for hh in range(2):
             sel(h64("PA", 8 + 64 * hh, 72 + 64 * hh, s=s), h64("ONEF", 0, 64, s=s), [[-16, 4], [-8, 4], [-1, 4]], -4 * hh, 1)
+    both(a("SUM32"), a("SUM"))
     sel(a("PA", 8, 136), a("PA", 8, 136), [[0, 8], [-1, 4], [0, 4]], 1, 0, A.is_ge)
-    sel(a("ID"), a("ONE", 0, 128), [[-1, 128]], 0, 1)
+    mark()
     sel(row("R8", 0, 128, 8), row("ONEF", 0, 128, 8), [[-1, 8], [0, 16]], 0, 1)
     sel(row("R8X", 0, 64, 8), row("ONEF", 0, 64, 8), [[0, 8], [-1, 8]], 0, 1)
-    iota(a("J"), [[16, 512]], 0, 1)
+    mark()
+    sel(a("SPD"), a("ONE", 0, 288), [[-1, 2], [-16, 9], [1000, 16]], -15000, 1)
     for i in range(8):
-        sel(a("SPD", 288 * i, 288 * i + 288), a("ONE", 0, 288), [[-1, 2], [-16, 9], [1000, 16]], -2 * i - 15000, 1)
         sel(a("SPR", 256 * i, 256 * i + 256), a("ONE", 0, 256), [[-1, 2], [-16, 8], [0, 16]], -2 * i, 1)
-    iota(row("TIE", 0, 512), [[0, 64], [1, 8]], -7, 0)
-    sel(a("RST"), a("ONE", 0, 512), [[0, 64], [1, 8]], 0, 0, A.not_equal)
+    for i in range(2):
+        iota(row("TIE", 256 * i, 256 * i + 256), [[0, 32], [1, 8]], -7, 0)
+    mark()
+    fill("RST", 0, 512, 1.0)
+    fill("RST", 0, 512, 0.0, 64, 8)
     band(a("SEL", 0, 8), a("SEL", 8, 16), [[-16, 4], [-64, 2]], 0, [[16, 4], [64, 2]], 15)
     sel(a("PT"), a("TB"), [[-8, 2], [-16, 8], [-1, 8]], 0, 1)
     band(h64("BAND"), h64("ONE", 0, 208), [[-16, 13], [1000, 2], [0, 8]], 64 - 1000, [[16, 13], [0, 2], [0, 8]], 15 - 64)
@@ -381,132 +563,119 @@ def rank_program(g, core, T, topo):
         sel(h64("XR", 256 * i, 256 * i + 256), h64("ONE", 0, 256), [[-8, 2], [-1, 8], [0, 16]], -16 * i, 1)
     for b in range(2):
         sel(a("LBM", 128 * b, 128 * b + 128), a("ONE", 0, 128), [[-16, 8], [1000, 2], [0, 8]], -1000 * b, 1)
-    sel(a("TRI"), a("ONESB"), [[1, 128]], 0, -1, A.is_ge)
-    sel(a("TRIC"), a("TRI"), [[1, 128]], 0, -1, A.not_equal, -4096.0)
-    band(a("POW2"), a("ONE", 0, 128), [[-16, 8], [-1000, 8], [-8, 2]], 0, [[16, 8], [0, 8], [8, 2]], 7)
-    iota(a("TABG0", 0, 48), [[128, 48]], 8193, 8)
+    sel(a("TRIC"), a("TS"), [[1, 128]], 0, -1, A.not_equal, -4096.0)
     iota(a("S4", 0, 32), [[0, 16], [16, 2]], 0, 0)
-    ts(h64("S17"), h64("SUM"), 17.0, A.mult)
-    ms(h64("C15"), 1536.0)
-    ts(a("NID"), a("ID"), -1.0, A.mult)
-    cp(a("ID32"), a("ID"))
-    ts(a("NBIG"), a("ID"), -16384.0, A.mult)
-    both(a("J"), a("J"), bias=col("COL", 11), v=(col("COL", 11), A.add))
+    both(h64("S17"), h64("SUM"), scale=17.0)
+    fill("C15", 0, 512, 1536.0, p1=64)
+    for n, c in (("NID", -1.0), ("ID32", 1.0), ("NBIG", -16384.0), ("PBIG", 16384.0), ("NID32", -1.0), ("N8K", -8192.0), ("N16K", -16384.0)):
+        both(a(n), a("ID"), scale=c)
     act(col("EX", 0), col("COL", 0), F.Exp, scale=LN2)
     cp(col("COL", 5), col("EX", 0))
-    ts(a("POW2"), a("POW2"), col("COL", 5), A.mult)
+    both(a("BWP"), a("BW", 64, 208), scale=col("COL", 5), v=(col("COL", 5), A.mult))
     for t in range(2):
-        ts(col("COL", 6 + t), col("COL", 0), float(t), A.is_equal, -1.0 / M20, A.mult)
-    for i in range(3):
-        tt(a("BP", 144 * i, 144 * i + 144), a("SPD", 288 * i, 288 * i + 144), a("SPD", 288 * i + 144, 288 * i + 288), A.add)
-    cp(a("ONESB32"), a("ONESB"))
-    ts(a("BJ"), a("BW", 64, 208), col("COL", 4), A.mult)
-    ts(col("COL", 9), col("COL", 1), -8.0, A.mult, -M24, A.add)
-    ts(a("TABG0", 0, 48), a("TABG0", 0, 48), col("COL", 9), A.add)
-    cp(a("TABG1", 0, 48), a("TABG0", 0, 48))
+        ts(col("COL", 6 + t), col("COL", 0), float(t), A.is_equal, -16384.0 / M20, A.mult)
+    both(a("ONES32"), a("ONESB"))
+    both(a("NHM"), a("ONESB"), scale=-M20 / 2)
+    both(a("BJ"), a("BW", 64, 208), scale=col("COL", 4), v=(col("COL", 4), A.mult))
     ts(a("LM"), a("S4", 0, 32), col("COL", 0), A.add)
-    both(a("TABT", 0, 512), a("J"), bias=1.0 - M24)
-    for n, lo, hi, c in (("TABT", 528, 544, -M24), ("TABG0", 560, 576, -M24), ("TABG1", 560, 576, -M24), ("FT", 528, 544, 0.0), ("FG", 560, 576, 0.0),
-                         ("FL", 1152, 1168, 0.0), ("FL2", 768, 784, 0.0), ("WB", 0, 16, 0.0), ("REM", 0, 1, -3072.0), ("RM2", 0, 1, -3968.0),
+    for n, lo, hi, c in (("TABT", 512, 528, -8 * M20), ("TABG0", 560, 576, -8 * M20), ("TABG1", 560, 576, -8 * M20), ("FT", 512, 528, 0.0),
+                         ("FG", 560, 576, 0.0), ("D0", 0, 48, 0.0), ("CT", 0, 1, 0.0), ("CG", 0, 1, 0.0), ("WB", 0, 16, 0.0),
+                         ("REM", 0, 1, -3072.0), ("RM2", 0, 1, -3968.0),
                          ("W00", 0, 16, 96.0), ("W01", 0, 16, 96.0), ("W10", 0, 16, 96.0), ("W11", 0, 16, 96.0)):
-        ms(a(n, lo, hi), c)
-    ms(row("NEG1", 0, 512), -1.0)
-    for i in range(8):
-        both(a("Z", 1024 * i, 1024 * i + 1024), a("DEC", 0, 1024), scale=0.0)
-    both(a("Z", 8192, 14336, 8), a("DEC", 0, 768), scale=0.0)
+        fill(n, lo, hi, c, es="SVG")
 
-    def offsets(fl, nl, x, b0, b1, linkcol=False):
-        c, xx, pp, oo = [a(n + x, 0, nl) for n in ("C", "X", "PP", "OO")]
+    def offsets(fl, nl, x, b0, b1, floor=False):
+        c, pp, oo = a("C" + x, 1, nl + 1), a("PP" + x, 0, nl), a("OO" + x, 0, nl)
         mms([(P(b0, 0, nl), view("BW", m, 64), a(fl, m, 16 * nl, 16)) for m in range(16)])
         both(c, P(b0, 0, nl))
-        mm(P(b1, 0, nl), a("ONESB"), c)
-        mm(P(b1, 64, 64 + nl), a("DM"), c)
+        mms([(P(b1, 128, 128 + nl), a("TS"), c), (P(b1, 128, 128 + nl), a("DMP"), a("C" + x, 0, nl))])
         mms([(P(b0, 64, 64 + nl), a("ID32"), a("D" + x, 0, nl)), (P(b0, 64, 64 + nl), a("NBIG"), c)])
-        scan(xx, a("ONE", 0, nl), P(b1, 0, nl), 0.0, A.mult, A.add)
-        tt(pp, xx, P(b1, 64, 64 + nl), A.add)
-        if linkcol:
-            ts(col("NOP", 1), col("XT", 31), -1.0, A.mult, col("NOP", 0), A.add)
-            ts(col("PPT", 32), col("NOP", 1), 0.0, A.max, col("PPT", 32), A.add)
+        scan(pp, a("D0" if floor else "ONE", 0, nl), P(b1, 128, 128 + nl), 0.0, A.max if floor else A.mult, A.add)
         tt(oo, pp, P(b0, 64, 64 + nl), A.max)
         cp(a("LS" + x, 0, nl), oo)
 
-    def ends(le, nl, x, zero):
-        c, zz, xx, pp = [a(n + x, 0, nl) for n in ("C", "ZZ", "X", "PP")]
-        tt(xx, pp, c, A.add)
-        both(zz, c, bias=zero + 1.0, scale=-16384.0)
-        tt(xx, xx, zz, A.max)
-        ts(a(le, 0, nl), xx, -1.0, A.add)
+    def ends(le, nl, x, b):
+        mms([(P(b, 0, nl), a("ID32"), a("PP" + x, 0, nl)), (P(b, 0, nl), a("ID"), a("C" + x, 1, nl + 1))])
+        ts(a(le, 0, nl), P(b, 0, nl), -1.0, A.add)
 
-    def pack(x, nl, n):
+    def pack(x, nl, cuts):
         scatter("W" + x, "LS" + x, nl, "PAYG" if x == "G" else "PAY", 18)
-        scan(a("Z" + x, 0, n), a("DEC", 0, n), a("W" + x, 0, n), -2 * M24, A.add, A.max)
-        if x == "T" and n == 1152:
-            act(a("YT"), a("ZT"), F.Relu)
-            act(a("YT"), a("YT"), F.Relu, M20, -1.0)
-        else:
-            ts(a("Y" + x, 0, n), a("Z" + x, 0, n), 0.0, A.max, M20, A.min)
+        for lo, hi in cuts:
+            scan(a("Z" + x, lo, hi), a("DEC", lo, hi), a("W" + x, lo, hi), -2 * M24 if lo == 0 else col("Z" + x, lo - 1), A.add, A.max)
+            pair(a("Y" + x, lo, hi), a("Z" + x, lo, hi), (0.0, A.max, M20, A.min), (F.Relu, M20, -1.0), (F.Relu, M20, -1.0))
 
     def invert(src, held):
-        ts(a("FI"), a(src), 8192.0, A.is_ge)
-        both(a("WT", 0, 768), a("DEC", 0, 768), scale=32.0)
-        both(a("INV", 0, 784), a("DEC", 0, 784), scale=0.0)
+        mark()
+        one = 1.0 if src == "A1" else 0.0
+        pair(a("FI"), a(src), (8192.0 + one, A.is_ge), (F.Sign, -8192.5, 1.0), (F.Relu, 0.0, 1.0), "SV" if one else "V")
+        fill("WT", 0, 768, -8 * M20, 384, es="SVG")
+        fill("INV", 1024, 4096, 0.0, 768, 4)
         offsets("FI", 32, "T", 4, 5)
-        mm(P(7), a("TRIQ"), a("FI"))
-        ts(P(6), a(src), -8184.0 - 131072.0, A.add, 128.0, A.mult)
-        tt(a("T2"), a("TABV"), P(6), A.add)
+        mms([(P(7), row("E8", 0, 128), row("J", 0, 512)), (P(7), row("ONE", 0, 128, 16), row("DEC", 0, 512, 16))], True, False)
+        mms([(P(7), a("PARD"), a("FI")), (P(7), a("TRIQ"), a("FI"))], False, True)
+        if one:
+            both(a("T2"), a(src), bias=-6145.0 * 128, scale=128.0)
+        else:
+            ts(a("T2"), a(src), -6144.0, A.add, 128.0, A.mult)
         tt(a("PAY", 0, 512), a("T2"), P(7), A.add)
-        pack("T", 32, 768)
+        pack("T", 32, ((0, 384), (384, 768)))
         mms([(P(4, 0, 48), view("BS32", m), a("YT", m, 768, 16)) for m in range(16)])
         cp(a("N1", 0, 48), P(4, 0, 48))
-        ts(a("N2", 0, 48), a("N1", 0, 48), MASK, A.bitwise_and, 10, A.arith_shift_right)
-        ts(a("EQ", 0, 48), a("N2", 0, 48), 0.0, A.is_equal)
-        tt(a("ZZ", 0, 48), a("EQ", 0, 48), a("DI", 0, 48), A.mult)
-        tt(a("OO", 0, 48), a("ZZ", 0, 48), a("N2", 0, 48), A.max)
+        ts(a("N2", 0, 48), a("N1", 0, 48), MASK - 1023, A.bitwise_and, 8, A.arith_shift_right)
+        tt(a("OO", 0, 48), a("N2", 0, 48), a("DS", 0, 48), A.max)
         cp(a("LS"), a("OO", 0, 48))
-        scatter("INV", "LS", 48, "YT")
-        mms([(P(5, 0, 48), view("BS32", m), a("INV", 1 + m, 769, 16)) for m in range(16)])
+        mark()
+        scatter("INV", "LS", 48, "YT", 24)
+        mms([(P(5, 0, 48), view("BS32", m), a("INV", 1024 + 4 * m, 4096, 64)) for m in range(16)])
         cp(a("N1", 0, 48), P(5, 0, 48))
         ts(a("N2", 0, 48), a("N1", 0, 48), 1023, A.bitwise_and)
         ts(a("N3", 0, 48), a("N1", 0, 48), MASK, A.bitwise_and)
         ts(a(held), a("N3", 0, 48), 0.0, A.is_gt)
 
-    def lists_a(b):
-        for s in range(2):
-            mms([(P(b + s, 0, 256), h64("PA", 8 - 8 * a0, 136 - 8 * a0, s=s), h64("A1", a0, 512, 2, s=s)) for a0 in range(2)])
-            ts(a("LA", 256 * s, 256 * s + 256), P(b + s, 0, 256), 0.125, A.mult, 15.4375, A.add)
+    def lists_a(banks):
+        for e in range(2):
+            for s in range(2):
+                b, lo = banks[2 * e + s], 256 * s + 128 * e
+                mms([(P(b, 0, 128), h64("PA", 8 - 8 * a0, 136 - 8 * a0, s=s), h64("A1", 256 * e + a0, 256 * e + 256, 2, s=s)) for a0 in range(2)])
+                ts(a("LA", lo, lo + 128), P(b, 0, 128), 0.125, A.mult, 15.4375, A.add)
 
     def outgoing(s, k):
         w = Wn(s, k)
         for lo, hi in ((0, 24), (24, 48)):
             both(a("OB%d" % s, 16 * lo, 16 * hi), ix(a(w, 0, 1040), a("LO%d" % s, lo, hi)))
-        send("OB%d" % s, 256, w, 1040, 1, "x%d" % (2 * k + s), "l%d" % s)
+        send("OB%d" % s, 256, w, 1040, 1, "x%d" % (2 * k + s), "l%d" % s, [a("AR"), a("WB", 1040, 1808)] if (s, k) == (1, 7) else [])
 
-    def order_tables(t):
-        ts(a("UI"), a("J"), col("PL", 3), A.mult, col("PL", 4 + t), A.add)
-        ts(a("UI"), a("UI"), 8191, A.bitwise_and)
-        ts(a("UH"), a("UI"), 1.0 / 512, A.mult, 191.5009765625, A.add)
+    def order_tables(t, b):
+        mark()
+        x, r = (a("T1"), a("MN")) if t == 0 else (a("T2"), a("T1"))
+        both(x, a("J"), bias=col("PL", 14 + t), scale=col("PL", 3), v=(col("PL", 3), A.mult, col("PL", 14 + t), A.add))
+        both(r, x, bias=2.0 ** -14, scale=2.0 ** -13)
+        whole(r, r)
+        mms([(P(b), a("ID32"), x), (P(b), a("N8K"), r)])
+        ts(a("UI", 0, 32), P(b, 0, 32), 4096.0, A.add)
+        both(a("UH"), P(b), bias=199.5009765625, scale=1.0 / 512)
         act(a("POW%d" % t), a("UH"), F.Exp, bias=191 * LN2, scale=-LN2)
-        ts(a("TABG%d" % t, 48, 560), a("UI"), 1.0 - M24, A.add)
         ts(a("N5", 0, 32), a("UI", 0, 32), 15, A.bitwise_and)
+        ts(col("COL", 12), col("N5", 0), 16384.0, A.mult, 4097.0 - M24, A.add)
+        both(a("TABG%d" % t, 48, 560), P(b), bias=col("COL", 12), v=(col("COL", 12), A.add))
         ts(a("N6", 0, 32), a("UI", 0, 32), 4, A.arith_shift_right, 31, A.bitwise_and)
         ts(a("N5", 0, 32), a("N5", 0, 32), 32.0, A.mult)
         tt(a("N5", 0, 32), a("N5", 0, 32), a("N6", 0, 32), A.add)
         cp(a("LW%d" % t), a("N5", 0, 32))
 
     def round_tables(t):
+        mark()
         ts(a("LB"), a("B1"), 0.125, A.mult, 15.4375, A.add)
-        ts(a("CB"), a("B1"), 7, A.bitwise_and)
+        cp(a("BH"), a("B1"))
+        ts(a("CB"), a("BH"), 7, A.bitwise_and)
         both(a("HELD"), a("A1"), F.Sign, v=(0.0, A.is_gt))
-        both(a("VAC"), a("HELD"), bias=1.0, scale=-1.0)
         for b in range(2):
             c0 = 32 * (8 * b + t)
-            tt(a("S1", 0, 32), a("B1", c0, c0 + 32), a("DZ", b, 64, 2), A.subtract)
-            ts(a("S2", 0, 32), a("B1", c0, c0 + 32), 0.0, A.is_gt)
-            tt(a("DIFK", b, 64, 2), a("S1", 0, 32), a("S2", 0, 32), A.mult)
-        cp(a("TABT", 512, 528), a("TABG0", 16 * t, 16 * t + 16))
-        both(a("ONEP"), a("DEC", 0, 1024), scale=col("COL", 6 + t), v=(col("COL", 6 + t), A.mult))
+            both(a("HB", b, 64, 2), a("B1", c0, c0 + 32), F.Sign, v=(0.0, A.is_gt))
+        mark()
+        both(a("TABT", 528, 544), a("TLK", 16 * t, 16 * t + 16))
+        both(a("ONEP"), a("DEC", 0, 256), scale=col("COL", 6 + t), v=(col("COL", 6 + t), A.mult))
         ts(a("LI"), a("IE1"), 0.125, A.mult, 15.4375, A.add)
-        tt(a("DIFI"), a("IE1"), a("DZ", 0, 48), A.subtract)
         cp(a("N1", 0, 48), a("IE1"))
         ts(a("N1", 0, 48), a("N1", 0, 48), 7, A.bitwise_and)
         both(a("S3", 0, 48), a("IH"), bias=99.0, scale=-99.0)
@@ -515,13 +684,16 @@ def rank_program(g, core, T, topo):
         mms([(P(5, m, 256, 16), a("SPR", 128 * m, 128 * m + 128), a("TL", 32, 48)) for m in range(16)])
         both(a("TAB", 0, 512), P(4))
         both(a("TAB", 512, 768), P(5, 0, 256))
-        both(a("WT", 0, 1152), a("DEC"), scale=32.0)
-        both(a("WG", 0, 1152), a("DEC"), scale=32.0)
+        mark()
+        fill("WT", 0, 1152, -8 * M20, 288, es="SVG")
+        fill("WG", 0, 1152, -8 * M20, 288, es="SVG")
+        mark()
         mms([(P(6), row("ONE", 0, 128), row("TIE", 0, 512))]
             + [(P(6, 256 * b + 64 * bl, 256 * b + 64 * bl + 64), a("HELD", 128 * bl, 128 * bl + 128), a("PT", 64 * b, 64 * b + 64)) for b in range(2) for bl in range(4)],
             True, False)
 
     def step(s, k):
+        mark()
         w, gs = Wn(s, k), "G%d" % s
         for hv in range(2):
             b, o = 2 * s + hv, a(Wn(s, k + 1), 16 + 512 * hv, 528 + 512 * hv)
@@ -538,8 +710,10 @@ def rank_program(g, core, T, topo):
             else:
                 both(a("Q%d" % hv), P(b), bias=-7.5 if k == 7 else -103.5)
                 tt(o, P(b), a("Q%d" % hv), A.subtract)
+        mark()
         if k < 7:
             outgoing(s, k + 1)
+        mark()
         if k % 4 == 3:
             for hv in range(2):
                 for j in range(4):
@@ -550,26 +724,38 @@ def rank_program(g, core, T, topo):
                     mms([(P(6, c0 + 256 * pb + 64 * bb, c0 + 256 * pb + 64 * bb + 32 - j, 4), a("D", 512 * j + 256 * bb + pb, 512 * j + 256 * bb + 256, 2),
                           a("SEL", 0, 8)) for bb in range(2) for pb in range(2)], False, s == 1 and hv == 1 and j == 3)
 
+    CUTS, FINE = ((0, 512), (512, 1024), (1024, 1152)), ((0, 288), (288, 576), (576, 864), (864, 1152))
+    rows = a("ROW", 0, 8192, 1, 0, 128, 16)
+
+    def partners(t, banks):
+        for b, (lo, hi) in zip(banks, CUTS):
+            mms([(P(b, 0, hi - lo), a("ONES32"), a("YT", lo, hi)), (P(b, 0, hi - lo), a("NHM"), a("SG", lo, hi))])
+            both(a("YT", lo, hi), P(b, 0, hi - lo), bias=-8 * M20 - t)
+
     def control(t):
         w = [Wn(s, 0) for s in range(2)]
         th = 8 if t == 0 else 0
-        for s in range(2):
-            mms([(P(0, 0, 64), h64("BW", 79 - 64 * s - u, 207 - 64 * s - u), h64(w[s], 16 + 64 * u, 80 + 64 * u)) for u in range(16)], s == 0, s == 1)
-        ts(a("FLK"), P(0, 0, 64), col("PL", th), A.is_lt)
-        tt(a("S1", 0, 64), a("FLK"), a("DIFK"), A.mult)
-        tt(a("S1", 0, 64), a("S1", 0, 64), a("DZ", 0, 64), A.add)
-        ts(a("LKA"), a("S1", 0, 64), -1.0, A.add)
-        scatter("Z", "LKA", 64, "ONEP")
-        mms([(P(0, 0, 48), spd(t, m), a("Z", 8192 + 8 * m, 14336, 128)) for m in range(16)])
-        tt(a("OKA"), a("OH"), P(0, 0, 48), A.subtract)
+        mark()
+        for i in range(4):
+            s, u0 = i // 2, 8 * (i % 2)
+            mms([(P(0, 0, 64), h64("BW", 79 - 64 * s - u, 207 - 64 * s - u), h64(w[s], 16 + 64 * u, 80 + 64 * u)) for u in range(u0, u0 + 8)], i == 0, i == 3)
+        mms([(P(3, 0, 64), a("NBIG"), a("HB"))] + [(P(3, b, 64, 2), a("ID32"), a("B1", 32 * (8 * b + t), 32 * (8 * b + t) + 32)) for b in range(2)], True, False)
+        ts(a("FLK"), P(0, 0, 64), col("PL", th), A.is_ge)
+        mm(P(3, 0, 64), a("PBIG"), a("FLK"), False, True)
+        tt(a("S1", 0, 64), P(3, 0, 64), a("DZ", 0, 64), A.min)
+        ts(a("LKA"), a("S1", 0, 64), 16383.0, A.add)
+        scatter("Z", "LKA", 64, "ONEP", 16, True)
+        mms([(P(0, 0, 48), a("NID"), a("OH"))] + [(P(0, 0, 48), spd(t, m), a("Z", 8192 + 8 * m, 14336, 128)) for m in range(16)])
+        both(a("OKA"), P(0, 0, 48), F.Relu, 0.0, -1.0, (-1.0, A.mult, 0.0, A.max))
         send("OKA", 16, "AR", 0, 1, "al%d" % t, "la")
+        mark()
         mms([(P(2, 0, 128, 1, 0, 64), h64("BX", 63 - 8 * q - 4 * s, 127 - 8 * q - 4 * s), h64(w[s], 16 + 256 * (q % 4) + q // 4, 272 + 256 * (q % 4), 2))
              for s in range(2) for q in range(8)])
         ts(h64("ZX"), P(2, 0, 128, 1, 0, 64), col("PX", t, 64), A.is_lt, 100.0, A.mult)
         for s in range(2):
             mms([(P(1), h64("BAND", 72 - 64 * s - 8 * b, 200 - 64 * s - 8 * b), h64(w[s], 16 + b, 1040, 2)) for b in range(2)], s == 0, s == 1)
-        act(a("STH"), P(1), F.Sign, col("PL", 12 + t), -1.0)
-        act(a("STH"), a("STH"), F.Relu)
+        both(a("STH"), P(1), F.Relu, col("PL", 12 + t), M20, (col("PL", th + 1), A.is_ge, M20, A.mult))
+        mark()
         scan(a("MN"), a("RST"), P(6), 0.0, A.mult, A.min)
         ts(a("N1", 0, 64), a("MN", 7, 512, 8), 4096.0, A.add)
         ts(a("N1", 0, 64), a("N1", 0, 64), 0x1807, A.bitwise_and)
@@ -582,132 +768,148 @@ def rank_program(g, core, T, topo):
             both(a("WB", 16 + 512 * b2, 528 + 512 * b2), P(2 + b2))
         tt(a("BO"), ix(a("WB", 0, 1040), a("LI")), a("TAB"), A.is_equal)
         send("BO", 256, "WB", 1040, -1, "be%d" % t, "lb")
+        if t == 0:
+            order_tables(1, 5)
+        mark()
         mms([(P(0), a("LBM", 128 * b, 128 * b + 128), a("WB", 16 + b, 1040, 2)) for b in range(2)])
-        act(a("K1"), P(0), F.Abs, col("COL", 10))
-        act(a("K1"), a("K1"), F.Relu, 1.0, -1.0)
-        tt(a("S2", 0, 48), a("IH"), a("AR"), A.is_gt)
-        tt(a("S2", 0, 48), a("S2", 0, 48), a("DIFI"), A.mult)
-        tt(a("S2", 0, 48), a("S2", 0, 48), a("DZ", 0, 48), A.add)
-        ts(a("LGI"), a("S2", 0, 48), -1.0, A.add)
-        scatter("Z", "LGI", 48, "ONEP")
+        pair(a("K1"), P(0), (col("COL", 2), A.is_equal, 16384.0, A.mult), (F.Abs, col("COL", 11), 1.0), (F.Relu, 16384.0, -16384.0))
+        mark()
+        mms([(P(7, 0, 48), a("ID32"), a("IE1")), (P(7, 0, 48), a("NBIG"), a("IH")), (P(7, 0, 48), a("PBIG"), a("AR"))])
+        tt(a("S2", 0, 48), P(7, 0, 48), a("DZ", 0, 48), A.min)
+        ts(a("LGI"), a("S2", 0, 48), 16383.0, A.add)
+        scatter("Z", "LGI", 48, "ONEP", 16, True)
         tt(a("FG", 0, 48), a("AR"), a("IH"), A.is_gt)
         mm(P(7, 0, 48), a("ONESB"), a("FG", 0, 48))
-        vop(col("NOP", 0), [P(7, 0, 48)], lambda q: q.tensor_reduce(ap(col("NOP", 0)), ap(P(7, 0, 48)), AxisListType.X, A.add))
-        mms([(P(1), a("ID"), a("VAC")), (P(1), a("ID"), a("K1"))], True, False)
+        node({"V": (lambda q: q.tensor_reduce(ap(col("D0", 33)), ap(P(7, 0, 48)), AxisListType.X, A.add), (1, 64, 0, 0, 0)),
+              "S": (lambda q: q.activation(ap(a("S2", 0, 48)), ap(P(7, 0, 48)), F.Identity, accum_out=ap(col("D0", 33))), (1.4, 64, 0, 0, 0))},
+             [P(7, 0, 48)], [col("D0", 33), a("S2", 0, 48)])
+        mark()
+        mm(P(1), a("NID32"), a("A1"), True, False)
+        mm(P(1), a("ID"), a("K1"), False, False)
         for r0 in range(0, 16, 4):
             mms([(P(1), spd(t, r), a("Z", r, 8192, 16)) for r in range(r0, r0 + 4)], False, r0 == 12)
-        tt(a("F1"), P(1), a("STH"), A.min)
-        both(P(1), P(1), F.Relu, 1.0, -1.0, (0.5, A.is_lt))
+        tt(a("F1"), P(1), a("STH"), A.is_ge)
+        both(P(1) if t == 0 else a("A1"), P(1), F.Relu, 0.0, -1.0, (-1.0, A.mult, 0.0, A.max))
         mm(P(2), a("ONESB"), a("F1"))
         mm(P(3), a("TRIC"), a("F1"))
         scan(a("REM", 1, 513), a("ONE", 0, 512), P(2), -3072.0, A.mult, A.subtract)
         tt(a("FT", 0, 512), P(3), a("REM", 0, 512), A.is_lt)
-        tt(a("A1"), a("A1"), P(1), A.mult)
+        mark()
         for i in range(16):
             both(a("G%d" % (i // 8), 512 * (i % 8), 512 * (i % 8) + 512), ix(a("WB"), a("LB", 32 * i, 32 * i + 32)))
-        for q in range(4):
-            mms([(P(6, 128 * q, 128 * q + 128), spd(0, u), a("G%d" % (q // 2), 2048 * (q % 2) + u, 2048 * (q % 2) + 2048, 16)) for u in range(16)], q == 0, q == 3)
+        for lo, hi in ((0, 128), (128, 256), (256, 384), (384, 448), (448, 512)):
+            e = lo // 256
+            mms([(P(6 * e, lo - 256 * e, hi - 256 * e), spd(0, u), a("G%d" % e, 16 * lo - 4096 * e + u, 16 * hi - 4096 * e, 16)) for u in range(16)],
+                lo % 256 == 0, hi % 256 == 0)
+        mark()
         mms([(P(7, 0, 48), spd(0, m), a("WB", 1040 + m, 1808, 16)) for m in range(16)])
         tt(a("OH"), a("OKA"), P(7, 0, 48), A.is_gt)
         both(a("FR"), a("OH", 16 * t, 16 * t + 16), bias=1.0, scale=-1.0)
         mm(P(4, 0, 16), a("ONESB"), a("FR"))
         mm(P(4, 16, 32), a("TRIC"), a("FR"))
         scan(a("RM2", 1, 17), a("ONE", 0, 16), P(4, 0, 16), -3968.0, A.mult, A.subtract)
-        tt(a("FT", 512, 528), P(4, 16, 32), a("RM2", 0, 16), A.is_lt)
-        tt(a("FB"), P(6), a("CB"), A.is_equal)
+        tt(a("FT", 528, 544), P(4, 16, 32), a("RM2", 0, 16), A.is_lt)
+        mark()
         for b in range(2):
             c0 = 32 * (8 * b + t)
-            tt(a("FB", c0, c0 + 32), a("FB", c0, c0 + 32), a("FLK", b, 64, 2), A.max)
-        mm(P(0), a("POW2"), a("FB"))
-        both(a("WD"), P(0))
-        both(a("WJ"), ix(a("WD"), a("LW%d" % t)))
-        mms([(P(7, 0, 32), view("BP", m), a("WJ", m, 512, 16)) for m in range(16)])
+            tt(a("FB", 256 * b, 256 * b + 256), P(6 * b, 0, 256), a("CB", 256 * b, 256 * b + 256), A.is_equal)
+            tt(a("FB", c0, c0 + 32), a("FB", c0, c0 + 32), a("FLK", b, 64, 2), A.is_ge)
+        for lo in (0, 16):
+            both(a("WJ", 16 * lo, 16 * lo + 256), ix(a("FB"), a("LW%d" % t, lo, lo + 16)))
+        mms([(P(7, 0, 32), view("BWP", m), a("WJ", m, 512, 16)) for m in range(16)])
         both(a("WF"), P(7, 0, 32), bias=0.25)
         tt(a("T1"), ix(a("WF"), a("LM")), a("POW%d" % t), A.mult)
-        ts(P(7), a("T1"), 1.5 * 2 ** 23, A.add, 1.5 * 2 ** 23, A.subtract)
+        whole(P(7), a("T1"))
         tt(a("FG", 48, 560), P(7), a("T1"), A.is_gt)
-        both(P(6), a("FB"), bias=1.0, scale=-1.0)
-        tt(a("BM"), a("B1"), P(6), A.mult)
-        mm(P(2), a("ID32"), a("TABT", 0, 512), True, False)
-        mm(P(2), a("TRIQ"), a("FT", 0, 512), False, True)
+        mark()
+        mms([(P(6), a("ID32"), a("B1")), (P(6), a("NBIG"), a("FB"))])
+        both(a("BM"), P(6), F.Relu, v=(0.0, A.max))
+        if t == 1:
+            both(a("BM"), a("BM"), bias=-1.0)
+            dmas("Y", [(a("YS", 0, 512, 1, r, 128, 16), a("BM", 32 * r, 32 * r + 32)) for r in range(16)], 4.0)
+        mark()
+        mm(P(5), a("ID32"), a("TABT", 0, 512), True, False)
+        mm(P(5), a("TRIQ"), a("FT", 0, 512), False, True)
         mm(P(3, 0, 32), a("TRIQ"), a("FT", 512, 544))
-        offsets("FT", 34, "T", 4, 5, True)
-        both(a("PAY", 0, 512), P(2))
+        offsets("FT", 34, "T", 4, 4, True)
+        both(a("PAY", 0, 512), P(5))
         tt(a("PAY", 512, 544), P(3, 0, 32), a("TABT", 512, 544), A.add)
-        ends("LE", 34, "T", 1152)
-        pack("T", 34, 1152)
+        ends("LE", 34, "T", 3)
+        pack("T", 34, ((0, 576), (576, 1152)))
+        mark()
         both(a("HIT"), a("ZT"), F.Relu, 0.0, -32.0, (-32.0, A.mult, 0.0, A.max))
-        mms([(P(0, 0, 72), view("BS32", m), a("YT", 72 * m, 72 * m + 72)) for m in range(16)])
-        ts(a("N3", 0, 72), P(0, 0, 72), -1.0, A.mult)
-        ts(a("N4", 0, 72), a("N3", 0, 72), 0x3F80, A.bitwise_and)
-        cp(a("HI", 0, 72), a("N4", 0, 72))
-        ts(a("N5", 0, 72), a("N3", 0, 72), 127, A.bitwise_and)
-        cp(a("LO", 0, 72), a("N5", 0, 72))
-        for b, bank in enumerate((0, 1, 6)):
-            mr = range(7 * b, min(16, 7 * b + 7))
-            mms([(P(bank, 72 * (m - 7 * b), 72 * (m - 7 * b) + 72), spd(m, 2 + 2 * t + pl), a(("HI", "LO")[pl], 0, 72)) for m in mr for pl in range(2)])
-            both(a("VT", 504 * b, 504 * b + 72 * len(mr)), P(bank, 0, 72 * len(mr)))
+        act(a("SG"), a("ZT"), F.Sign, 0.5 - M20)
+        if t == 1:
+            partners(t, (0, 1, 6))
+        mark()
         mm(P(2), a("ID32"), a("TABG%d" % t, 0, 512), True, False)
         mm(P(2), a("TRIQ"), a("FG", 0, 512), False, True)
         mm(P(3, 0, 64), a("TRIQ"), a("FG", 512, 576))
-        offsets("FG", 36, "G", 4, 5)
+        offsets("FG", 36, "G", 4, 4)
         both(a("PAYG", 0, 512), P(2))
         tt(a("PAYG", 512, 576), P(3, 0, 64), a("TABG%d" % t, 512, 576), A.add)
         if t == 0:
-            ends("LE2", 3, "G", 768)
-        pack("G", 36, 1152)
+            ends("LE2", 3, "G", 2)
+        pack("G", 36, FINE)
+        dmas("Y", [(rows, a("YS" if t == 1 else "BM"))])
         mms([(P(7, 0, 72), view("BS32", m), a("YG", m, 1152, 16)) for m in range(16)])
-        for b, (lo, hi) in enumerate(((0, 512), (512, 1024), (1024, 1152))):
-            mm(P(3 + b, 0, hi - lo), a("NID"), a("HIT", lo, hi), True, False)
-            mm(P(3 + b, 0, hi - lo), a("ONESB32"), a("YG", lo, hi), False, True)
-            scan(a("FL", lo, hi), a("HIT", lo, hi), P(3 + b, 0, hi - lo), 0.0 if b == 0 else col("FL", lo - 1), A.min, A.max)
-        both(P(2), a("A1"), bias=-1.0 * t)
-        tt(a("FGI"), ix(a("FL"), a("LE", 0, 34)), a("FT"), A.mult)
-        ts(a("FGI"), a("FGI"), MASK, A.bitwise_and)
-        tt(a("A1"), a("FGI", 0, 512), P(2), A.add)
+        mark()
+        for b, (lo, hi) in zip((5, 3, 4, 2), FINE):
+            mm(P(b, 0, hi - lo), a("NID"), a("HIT", lo, hi), True, False)
+            mm(P(b, 0, hi - lo), a("ONES32"), a("YG", lo, hi), False, True)
+            scan(a("FL", lo, hi), a("HIT", lo, hi), P(b, 0, hi - lo), 0.0 if lo == 0 else col("FL", lo - 1), A.min, A.max)
         if t == 0:
-            lists_a(0)
+            for lo, hi in ((0, 256), (256, 544)):
+                tt(a("FGI", lo, hi), ix(a("FL"), a("LE", lo // 16, hi // 16)), a("FT", lo, hi), A.mult)
+                ts(a("FGI", lo, hi), a("FGI", lo, hi), 0x3FFF, A.bitwise_and)
+                tt(a("A1", lo, lo + 256), a("FGI", lo, lo + 256), P(1, lo, lo + 256), A.add)
+            lists_a((0, 2, 3, 1))
+            mark()
+            partners(t, (4, 5, 6))
         else:
+            x, r = a("PAY", 0, 512), a("REM", 16, 528)
+            tt(x, ix(a("FL"), a("LE", 0, 32)), a("FT", 0, 512), A.mult)
+            both(r, x, bias=-0.4375, scale=2.0 ** -14)
+            whole(r, r)
+            mms([(P(1), a("ID32"), a("A1")), (P(1), a("N16K"), r), (P(1), a("ID32"), x)])
+            both(a("A1"), P(1), bias=-1.0)
             dmas("S", [(T.yd[:], a("A1"))])
-        n = [a("N%d" % i, 0, 72) for i in (6, 7, 8)]
+        mark()
+        n = [a("N%d" % i, 0, 72) for i in (5, 6, 7, 8)]
         ts(n[0], P(7, 0, 72), -1.0, A.add)
-        ts(n[1], n[0], MASK, A.bitwise_and)
-        tt(n[0], n[1], a("DZ0"), A.min)
-        ts(n[1], n[0], 15, A.bitwise_and)
-        ts(n[2], n[0], 4, A.arith_shift_right, 31, A.bitwise_and)
-        ts(n[1], n[1], 31.0, A.mult)
-        ts(n[2], n[2], -15.0, A.mult)
-        tt(n[0], n[0], n[1], A.add)
-        tt(n[0], n[0], n[2], A.add)
-        cp(a("LZ"), n[0])
-        scatter("Z", "LZ", 72, "VT", 18)
-        for e, bank in enumerate((7, 6)):
-            lo, hi = 256 * e, 256 * e + 256
-            mms(([(P(bank, 0, 256), row("ONE", 0, 128), row("NEG1", 0, 256))] if t == 1 else [])
-                + [(P(bank, 0, 256), view("BP", u, 144 * (1 + t)), a("Z", 512 * u + lo, 512 * u + hi)) for u in range(16)])
-            tt(a("B1" if t == 0 else "YB", lo, hi), a("BM", lo, hi), P(bank, 0, 256), A.add)
-            if t == 1:
-                for c in range(2):
-                    dmas("YS"[c], [(T.ya[r::16, :], a("YB", 32 * r, 32 * r + 32)) for r in range(8 * e + 4 * c, 8 * e + 4 * c + 4)])
+        if t == 0:
+            ts(n[1], n[0], 9, A.arith_shift_right, 0x1E0, A.bitwise_and)
+            ts(n[2], n[0], 4, A.arith_shift_right, 31, A.bitwise_and)
+            ts(n[3], n[0], FLAG + 0x1E00, A.bitwise_and)
+            tt(n[1], n[1], n[3], A.add)
+        else:
+            ts(n[1], n[0], 5, A.arith_shift_right, 0x7E00, A.bitwise_and)
+            ts(n[2], n[0], 4, A.arith_shift_right, 511, A.bitwise_and)
+        tt(n[1], n[1], n[2], A.add)
+        tt(n[1], n[1], a("DZ0"), A.min)
+        cp(a("LZ"), n[1])
+        scatter("ROW", "LZ", 72, "YT", 18)
         if t == 1:
+            dmas("Y", [(T.ya[:], rows)])
             return
-        ts(a("S3", 0, 16), a("FGI", 512, 528), 0.0, A.is_gt)
+        dmas("Y", [(a("B1"), rows)])
+        mark()
+        ts(a("S3", 0, 16), a("FGI", 528, 544), 0.0, A.is_gt)
         tt(a("OH", 0, 16), a("OH", 0, 16), a("S3", 0, 16), A.max)
-        both(a("YT", 0, 768), a("YT", 0, 768), bias=M20, scale=-1.0)
         both(a("HIG"), a("ZG", 0, 768), F.Relu, 0.0, -32.0, (-32.0, A.mult, 0.0, A.max))
         for b, (lo, hi) in enumerate(((0, 512), (512, 768))):
-            mms([(P(4 + b, 0, hi - lo), a("NID"), a("HIG", lo, hi)), (P(4 + b, 0, hi - lo), a("ONESB32"), a("YT", lo, hi))])
+            mms([(P(4 + b, 0, hi - lo), a("NID"), a("HIG", lo, hi)), (P(4 + b, 0, hi - lo), a("ID32"), a("YT", lo, hi))])
             scan(a("FL2", lo, hi), a("HIG", lo, hi), P(4 + b, 0, hi - lo), 0.0 if b == 0 else col("FL2", lo - 1), A.min, A.max)
         mms([(P(6, 0, 48), spd(0, m), a("BO", m, 768, 16)) for m in range(16)])
-        tt(a("N4", 0, 48), ix(a("FL2"), a("LE2", 0, 3)), a("FG", 0, 48), A.mult)
-        ts(a("N4", 0, 48), a("N4", 0, 48), MASK, A.bitwise_and)
+        tt(a("S4", 0, 48), ix(a("FL2"), a("LE2", 0, 3)), a("FG", 0, 48), A.mult)
         tt(a("KEEP"), a("AR"), P(6, 0, 48), A.is_gt)
         tt(a("IE1"), a("IE1"), a("KEEP"), A.mult)
-        tt(a("IE1"), a("IE1"), a("N4", 0, 48), A.add)
+        tt(a("IE1"), a("IE1"), a("S4", 0, 48), A.add)
         ts(a("IH"), a("IE1"), 0.0, A.is_gt)
 
+    mark()
     ts(a("A1"), a("DEN"), 1.0, A.add)
-    lists_a(0)
+    lists_a((0, 1, 2, 3))
     for s in range(2):
         both(a(Wn(s, 0), 16, 1040), a("XL%d" % s), bias=96.0)
     invert("AXO", "OH")
@@ -716,25 +918,37 @@ def rank_program(g, core, T, topo):
         mm(P(2 + s, 0, 48), h64("SUM32", s=s), h64("VO", s=s))
         cp(a("LO%d" % s), P(2 + s, 0, 48))
         outgoing(s, 0)
+    mark()
+    fill("Z", 0, 8192, 0.0, 512, es="SVG")
+    fill("Z", 8192, 14336, 0.0, 768, 8)
+    mark()
     cp(row("PARF", 0, 6, 8), row("PARI", 0, 6, 8))
-    mm(P(7, 0, 6), row("R8", 0, 128, 8), row("PARF", 0, 6, 8))
-    mm(P(7, 8, 14, 1, 0, 64), row("R8X", 0, 64, 8), row("PARF", 0, 6, 8))
-    cp(a("PL", 0, 6), P(7, 0, 6))
-    ts(a("PL", 8, 11), P(7, 0, 3), 1536.0, A.add)
-    ts(col("PL", 12), P(7, 1, 2), 1535.5, A.add)
-    ts(col("PL", 13), P(7, 1, 2), -0.5, A.add)
-    cp(col("PX", 1, 64), P(7, 10, 11, 1, 0, 64))
-    ts(col("PX", 0, 64), P(7, 10, 11, 1, 0, 64), 1536.0, A.add)
-    invert("DEN", "IH")
-    act(a("SGA"), a("INV", 0, 784), F.Sign, bias=-0.5)
-    act(a("SGB"), a("INV", 0, 784), F.Sign, bias=M20 - 0.5, scale=-1.0)
-    mms([(P(4, 0, 48), view("BJ", m), a(n, 1 + m, 769, 16)) for n in ("SGA", "SGB") for m in range(16)])
+    mm(P(6, 0, 6), row("R8", 0, 128, 8), row("PARF", 0, 6, 8))
+    mm(P(6, 8, 14, 1, 0, 64), row("R8X", 0, 64, 8), row("PARF", 0, 6, 8))
+    both(a("PL", 0, 6), P(6, 0, 6))
+    both(a("PL", 8, 11), P(6, 0, 3), bias=1536.0)
+    both(col("PL", 12), P(6, 1, 2), bias=-1535.5 * M20, scale=-M20)
+    both(col("PL", 13), P(6, 1, 2), bias=0.5 * M20, scale=-M20)
+    both(a("PL", 14, 16), P(6, 4, 6), bias=-1023.5 * 8192)
+    both(col("PX", 1, 64), P(6, 10, 11, 1, 0, 64))
+    both(col("PX", 0, 64), P(6, 10, 11, 1, 0, 64), bias=1536.0)
+    invert("A1", "IH")
+    mark()
+    both(a("J"), a("J"), bias=col("COL", 10), v=(col("COL", 10), A.add))
+    both(a("TLK"), a("J", 0, 48), bias=8193.0 - M24, scale=8.0)
+    for t in range(2):
+        both(a("TABG%d" % t, 0, 48), a("TLK"), bias=float(FLAG))
+    both(a("TABT", 0, 512), a("J"), bias=1.0 - M24)
+    mark()
+    act(a("SGA"), a("INV", 1024, 4096, 4), F.Sign, bias=-0.5)
+    act(a("SGB"), a("INV", 1024, 4096, 4), F.Sign, bias=M20 - 0.5, scale=-1.0)
+    mms([(P(4, 0, 48), view("BJ", m), a(n, m, 768, 16)) for n in ("SGA", "SGB") for m in range(16)])
     ts(a("S1", 0, 48), a("N2", 0, 48), 8.0, A.mult, 1.0, A.add)
     tt(a("S1", 0, 48), a("S1", 0, 48), P(4, 0, 48), A.add)
     tt(a("IE1"), a("S1", 0, 48), a("IH"), A.mult)
     ts(a("B1"), a("BH"), 1.0, A.add)
+    order_tables(0, 7)
     for t in range(2):
-        order_tables(t)
         round_tables(t)
         for k in range(4 * t, 4 * t + 4):
             for s in range(2):

@@ -4,27 +4,28 @@ from concourse.mybir import AluOpType as A, ActivationFunctionType as F, AxisLis
 
 B16, F32, I32, U16 = "bfloat16", "float32", "int32", "uint16"
 _SB = {
-    B16: dict(W00=1808, W01=1808, W10=1808, W11=1808, WB=1808, G0=4096, G1=4096, D=2048, OB0=768, OB1=768, BO=768, Z=15488, XL0=1024, XL1=1024,
-              Q0=512, Q1=512, ONE=576, DEC=1152, C15=512, TIE=512, RST=512, BLK=208, TS=128, DMP=128, TRIQ=128, TRIC=128, PARD=128, NHM=128, BW=208,
-              BWP=144, BAND=208, SPD=288, SPR=2048, BJ=144, SUM=128, S17=128, ID=128, NID=128, NBIG=128, PBIG=128, HB=64, SEL=16, PT=128, BX=128,
+    B16: dict(W00=1808, W01=1808, W10=1808, W11=1808, WB=1808, G0=4096, G1=4096, D=2048, OB0=768, OB1=768, BO=768, OWN0=2048, OWN1=2048,
+              Q0=512, Q1=512, ONE=576, DEC=1152, TIE=512, RST=512, BLK=208, TS=128, DMP=128, TRIQ=128, TRIC=128, PARD=128, NHM=128, BW=208,
+              BWP=144, BAND=208, SPD=144, SPR=2048, BJ=144, SUM=128, S17=128, S25=128, ID=128, NID=128, NBIG=128, PBIG=128, SEL=16, PT=128, BX=128,
               XR=1024, LBM=256, TB=128, FT=544, FG=576, FI=512, F1=512, HELD=512, K1=512, STH=512, FB=512, WJ=512, UH=512, POW0=512, POW1=512,
-              ONEP=256, HIT=1152, SG=1152, HIG=768, TAB=768, SGA=768, SGB=768, C0=64, CX=128, CT=48, CG=48, OH=48, OKA=48, AR=48, IH=48, FR=16,
+              MO=48, HIT=1152, SG=1152, HIG=768, TAB=768, SGA=768, SGB=768, C0=64, CX=128, CT=48, CG=48, OH=48, OKA=48, AR=48, IH=48, FR=16,
               TL=48, FLK=64, KEEP=48, EX=16),
     F32: dict(ONEF=144, ID32=128, ONES32=128, NID32=128, N8K=128, N16K=128, BS32=144, SUM32=128, PA=136, R8=128, R8X=64, E8=128, PARF=8, PL=16,
-              PX=8, COL=16, J=512, DS=72, DZ=72, DZ0=72, DT=72, DG=72, A1=512, B1=512, BM=512, T1=512, T2=512, MN=512, REM=528, PAY=544, PAYG=576,
-              TABT=544, TABG0=576, TABG1=576, CI=128, TLK=48, WT=1808, WG=10624, ROW=9472, INV=4096, ZT=1152, ZG=1152, YT=1152, YG=1152, FL=1152,
-              FL2=768, ZX=128, WF=32, D0=48, PPT=48, OOT=48, PPG=48, OOG=48, OO=80, IE1=48, S1=72, S2=72, S3=72, S4=72, RM2=32, VO=48),
-    I32: dict(DEN=512, AXO=512, BH=512, CB=512, UI=208, FGI=544, PARI=8, PI=8, N1=80, N2=80, N3=80, N4=80, N5=80, N6=80, N7=80, N8=80),
+              PX=8, COL=16, J=512, DS=72, DZ=72, DZ0=72, DT=72, DG=72, A1=512, B1=512, BM=512, REM=528, PAY=544, PAYG=576, TABT=544, TABG0=576,
+              TABG1=576, CI=128, TLK=48, WG=16784, WT=1808, ROW=9472, Z=13824, INV=4096, T1=512, T2=512, MN=512, ZT=1152, ZG=1152, YT=1152,
+              YG=1152, FL=1152, ZD=512, ONEP=256, SPD32=144, P16K=128, PO=8,
+              FL2=768, ZX=128, WF=32, D0=48, PPT=48, OOT=48, PPG=48, OOG=48, OO=80, IE1=48, TG=64, TI=48, S1=72, S2=72, S3=72, S4=72, RM2=32, VO=48),
+    I32: dict(DEN=544, AXO=512, BH=512, CB=512, UI=208, FGI=544, UJ=512, PARI=8, PI=8, N1=80, N2=80, N3=80, N4=80, N5=80, N6=80, N7=80, N8=80),
     U16: dict(LA=512, LB=512, LO0=48, LO1=48, LI=48, LKA=64, LGI=48, LST=48, LSG=48, LS=48, LE=48, LE2=8, LZ=72, LW0=32, LW1=32, LM=32),
 }
-_ALIAS = dict(XL0=("G0", 0), XL1=("G1", 0), SGA=("D", 0), SGB=("D", 784), ROW=("WG", 1152), WT=("WG", 1152), INV=("WG", 2960),
-              T1=("WG", 7056), T2=("WG", 7568), MN=("WG", 8080))
+_ALIAS = dict(SGA=("D", 0), SGB=("D", 784), WT=("WG", 1152), ROW=("WG", 2960), INV=("WG", 2960),
+              Z=("WG", 2960), CB=("AXO", 0), FGI=("DEN", 0), UJ=("DEN", 0), T2=("BM", 0))
 PLACE, SCRATCH = {}, {}
 for _d, _t in _SB.items():
     _o = 0
     for _n, _w in _t.items():
         if _n in _ALIAS:
-            PLACE[_n] = _ALIAS[_n] + (_w,)
+            PLACE[_n] = (PLACE[_ALIAS[_n][0]][0], PLACE[_ALIAS[_n][0]][1] + _ALIAS[_n][1], _w)
         elif _w > 600:
             PLACE[_n] = (_n, 0, _w)
             SCRATCH[_n] = ("sbuf", [128, _w], _d)
@@ -36,17 +37,21 @@ for _i in range(8):
     SCRATCH["P%d" % _i] = ("psum", [128, 512], F32)
     PLACE["P%d" % _i] = ("P%d" % _i, 0, 512)
 PLACE["ONESB"] = (PLACE["BLK"][0], PLACE["BLK"][1] + 64, 128)
-SCRATCH["YS"] = ("dram", [128, 512], F32)
-PLACE["YS"] = ("YS", 0, 512)
+for _n, _w in (("YS", 512), ("LOW", 1152), ("NIL", 792)):
+    SCRATCH[_n] = ("dram", [128, _w], F32)
+    PLACE[_n] = (_n, 0, _w)
 SEMAPHORES = (["cV", "cS", "cP", "cG", "cX", "l0", "l1", "la", "lb"] + ["x%d" % i for i in range(16)] + ["al0", "al1", "be0", "be1"]
-              + ["d%d" % i for i in range(16)])
+              + ["d%d" % i for i in range(24)])
 M20, M24 = float(2 ** 20), float(2 ** 24)
 MASK, FLAG = 2 ** 20 - 1, 3 * 2 ** 18
 LN2, RND = math.log(2.0), 1.5 * 2 ** 23
-COSTS = ((0.05, 0.83e-3, 1.3e-3, 3.15e-3, 0.42e-3, 0.08, 4.0, 1.0), (0.06, 1.04e-3, 1.6e-3, 4e-3, 0.53e-3, 0.1, 4.2, 1.0),
-         (0.05, 0.9e-3, 1.2e-3, 4.5e-3, 0.45e-3, 0.12, 6.5, 1.5), (0.06, 1.1e-3, 2.1e-3, 2.5e-3, 0.6e-3, 0.1, 5.0, 1.2))
-HALF, LOOK, GAP, PIECE, TURNS, MOVES, HEAT = 0.7, 0.7, 0.8, 128, 700, 8000, 0.001
+COSTS = ((0.05, 0.83e-3, 1.3e-3, 3.15e-3, 0.45e-3, 0.1, 4.5, 1.1), (0.06, 1.04e-3, 1.6e-3, 4e-3, 0.53e-3, 0.1, 4.2, 1.0),
+         (0.05, 0.9e-3, 1.2e-3, 4.5e-3, 0.5e-3, 0.14, 6.0, 1.5), (0.06, 1.1e-3, 2.0e-3, 2.5e-3, 0.66e-3, 0.1, 5.0, 1.2))
+CALL = {"V": 1.0, "S": 1.3}
+HALF, LOOK, GAP, TURNS, MOVES, HEAT = 0.7, 0.7, 0.8, 800, 16000, 0.002
+PIECES = (0, 192, 384, 512, 640, 768, 896, 1024)
 SHY, LIFT = {"V": 8.0, "S": 4.0}, (-8.0, -3.0, -1.0, 1.0, 3.0, 8.0)
+DIF = 1
 ORDER = []
 
 
@@ -112,13 +117,13 @@ def rank_program(g, core, T, topo):
         xs = [x for x in [out] + ins if isinstance(x, tuple)]
         ind = [x for x in xs if x[0] == "@"]
         if ind:
-            return (1, 0, 0, 16 * size(ind[0][2]), 0) if out[0] == "@" else (1, 0, 16 * size(ind[0][2]), 0, 0)
+            return (1, 0, 0, 16 * size(ind[0][2]), 0) if out[0] == "@" else (CALL[e], 0, 16 * size(ind[0][2]), 0, 0)
         f = 1.0
         if e == "V" and two:
             f = 1.0 if any(psum(x) for x in xs[1:]) else 2.0
         elif e == "V" and all(SCRATCH[x[0]][2] in (B16, U16) for x in xs if size(x) > 1):
             f = 0.5
-        return (1, max(64, max(size(x) for x in xs) * f), 0, 0, 0)
+        return (CALL[e], max(64, max(size(x) for x in xs) * f), 0, 0, 0)
 
     def op(out, ins, ways):
         node(ways, flat(ins) + ([out[2]] if out[0] == "@" else []), [out[1]] if out[0] == "@" else [out])
@@ -171,7 +176,7 @@ def rank_program(g, core, T, topo):
             q.wait_ge(T.sem["cX"], half[0])
             return actf(o, o, *s2)(q)
         c = est("S", o, [i])
-        ways = {"S": (two, (3, 2 * c[1], 0, 0, 0)), "V": (tsf(o, i, *v), est("V", o, [i]))}
+        ways = {"S": (two, (2 + 2 * c[0], 2 * c[1], 0, 0, 0)), "V": (tsf(o, i, *v), est("V", o, [i]))}
         op(o, [i] + list(v) + list(s1), {e: ways[e] for e in es})
 
     def whole(o, i):
@@ -193,15 +198,21 @@ def rank_program(g, core, T, topo):
             hi = min(n, lo + piece)
             cp(ix(a(win), a(lst, lo, hi)), a(src, 0, 16 * (hi - lo)) if same else a(src, 16 * lo, 16 * hi))
 
+    def marks(lst, n):
+        for lo in range(0, n, 16):
+            o, c = ix(a("Z"), a(lst, lo, lo + 16)), (0, 0, 256, 0)
+            op(o, [a("ONEP")], {"V": (tsf(o, a("ONEP"), 1.0 / 64, A.mult, 0.5, A.add), (1,) + c),
+                                "S": (lambda q, o=o: q.activation(ap(o), ap(a("ONEP")), F.Sigmoid), (CALL["S"],) + c)})
+
     def iotaf(o, p, base, cm):
         kw = {} if SCRATCH[o[0]][2] == I32 else {"allow_small_or_imprecise_dtypes": True}
-        return (lambda q: q.iota(ap(o), p, base, cm, **kw), (4, 2 * size(o), 0, 0, 0))
+        return (lambda q: q.iota(ap(o), p, base, cm, **kw), (6, 2 * size(o), 0, 0, 0))
 
     def iota(o, p, base, cm):
         op(o, [], {"G": iotaf(o, p, base, cm)})
 
     def sel(o, i, p, base, cm, f=A.is_equal, fill=0.0):
-        op(o, [i], {"G": (lambda q: q.affine_select(ap(o), ap(i), p, f, fill, base, cm), (5, 2 * size(o), 0, 0, 0))})
+        op(o, [i], {"G": (lambda q: q.affine_select(ap(o), ap(i), p, f, fill, base, cm), (7, 2 * size(o), 0, 0, 0))})
 
     def band(o, i, p, base, p2, base2):
         sel(o, i, p, base, 1, A.is_ge)
@@ -231,7 +242,7 @@ def rank_program(g, core, T, topo):
             d = T.cores[(rank + sign * h) % N]
             eng = topo.engines(core, d)
             k = len(eng) // 4
-            mine = eng[:2 * k] if h == 1 else eng[h * k:(h + 1) * k]
+            mine = eng[0::2] if h == 1 else eng[1::2][(h - 2) * k:(h - 1) * k]
             rid, pid = topo.addr(d, core)
             tr.append(RemoteDMATransfer(dst_ids=[DstId(rid=rid, pnc=pid)], dma_engine_mask=sum(1 << x for x in mine), remote_sem=T.sem[rsem],
                                         src=ap(a(src, w * (h - 1), w * h)), dst=ap(a(dst, off + w * (h - 1), off + w * h))))
@@ -299,7 +310,7 @@ def rank_program(g, core, T, topo):
                             ready[x].add(u)
             return order, fin
 
-        seed, unit = 1, [1.0] * len(views)
+        seed, unit = 2, [1.0] * len(views)
         nxt = dict(zip(chain, chain[1:]))
         cost, lat, fwd, bwd = views[0]
         level = [0.0] * n
@@ -332,27 +343,37 @@ def rank_program(g, core, T, topo):
         deps = [[d for d, gap in bwd[i]] for i in range(n)]
         subs = [[u for u, gap in fwd[i]] for i in range(n)]
 
-        def times():
-            out = []
-            for cost, lat, fwd, bwd in views:
-                fin, rest, free = [0.0] * n, [0.0] * n, dict.fromkeys(ES, 0.0)
-                for i in order:
+        def times(lo, old):
+            out, last = [], {}
+            for i in order[:lo]:
+                last[eng[i]] = i
+            for (cost, lat, fwd, bwd), x in zip(views, old):
+                fin = list(x[0])
+                free = {e: fin[last[e]] if e in last else 0.0 for e in ES}
+                for i in order[lo:]:
                     e = eng[i]
                     t = free[e]
                     for d, gap in bwd[i]:
                         if fin[d] + gap > t:
                             t = fin[d] + gap
                     free[e] = fin[i] = t + cost[i][e]
-                free = dict.fromkeys(ES, 0.0)
-                for i in reversed(order):
+                out.append([fin, x[1], max(fin[i] + lat[i] for i in tail)])
+            return sum(x[2] / w for x, w in zip(out, unit)), out
+
+        def rests(hi, out):
+            first = {}
+            for i in reversed(order[hi + 1:]):
+                first[eng[i]] = i
+            for (cost, lat, fwd, bwd), x in zip(views, out):
+                rest = x[1] = list(x[1])
+                free = {e: rest[first[e]] if e in first else 0.0 for e in ES}
+                for i in reversed(order[:hi + 1]):
                     e = eng[i]
                     t = max(free[e], lat[i])
                     for u, gap in fwd[i]:
                         if rest[u] + gap > t:
                             t = rest[u] + gap
                     free[e] = rest[i] = t + cost[i][e]
-                out.append((fin, rest, max(rest)))
-            return sum(x[2] / w for x, w in zip(out, unit)), out
 
         def guess(lo, hi, span):
             before, after, rise = {}, {}, 0.0
@@ -398,13 +419,14 @@ def rank_program(g, core, T, topo):
                     i = tight[0] if tight else None
             return out
         tail = [i for i in range(n) if not subs[i]]
-        score, fins = times()
+        score, fins = times(0, [[[0.0] * n, [0.0] * n] for v in views])
+        rests(n - 1, fins)
         arcs, pos = None, [0] * n
         top = (score, list(order), list(eng))
         for it in range(MOVES):
             seed = seed * 48271 % 2147483647
-            if not arcs:
-                arcs = [x for v in range(len(views)) for x in waits(v, fins[v][0])]
+            if not arcs or it % 64 == 0:
+                arcs = waits(it % len(views), fins[it % len(views)][0])
                 for p, i in enumerate(order):
                     pos[i] = p
             j, i = arcs[(seed >> 8) % len(arcs)]
@@ -436,8 +458,9 @@ def rank_program(g, core, T, topo):
             if guess(pj, pi, span) <= heat:
                 was = order[pj:pi + 1]
                 order[pj:pi + 1] = span
-                new, nf = times()
+                new, nf = times(pj, fins)
                 if new <= score + heat:
+                    rests(pi, nf)
                     score, fins, arcs = new, nf, None
                     if score < top[0]:
                         top = (score, list(order), list(eng))
@@ -499,10 +522,10 @@ def rank_program(g, core, T, topo):
         return "W%d%d" % (s, k % 2)
 
     first = dmas("Y", [(a("AXO"), T.axo[:])])
-    dmas("S", [(a("DEN"), T.den[:])], 3.0)
-    second = dmas("Y", [(h64("XL%d" % s, s=hh), T.x0[64 * s:64 * s + 64, :]) for s in range(2) for hh in range(2)]
-                  + [(row("PARI", 0, 6, 8), T.par[:])], 2.6, [first])
-    dmas("Y", [(a("BH", 32 * r, 32 * r + 32), T.axo[r::16, :]) for r in range(16)], 4.0, [second])
+    dmas("S", [(a("DEN", 0, 512), T.den[:])], 3.0)
+    dmas("Y", [(h64(Wn(s, 0), 16, 1040, s=hh), T.x0[64 * s:64 * s + 64, :]) for s in range(2) for hh in range(2)]
+         + [(row("PARI", 0, 6, 8), T.par[:])], 2.6, [first])
+    dmas("Y", [(a("BH", 32 * r, 32 * r + 32), T.axo[r::16, :]) for r in range(16)], 6.0, [first])
 
     mark()
     ms(a("DEC"), -M20)
@@ -527,14 +550,12 @@ def rank_program(g, core, T, topo):
     sel(a("TRIQ"), a("TRIQ"), [[1, 128]], 0, -1, A.not_equal, M24)
     ts(col("PI", 1), col("PI", 0), 15, A.bitwise_and)
     ts(col("PI", 2), col("PI", 0), 112, A.bitwise_and)
-    ts(col("PI", 6), col("PI", 0), 1, A.add)
-    ts(col("PI", 3), col("PI", 6), 7, A.bitwise_and)
-    ts(col("PI", 4), col("PI", 0), 7, A.bitwise_and)
-    cp(a("COL", 0, 4), a("PI", 1, 5))
-    both(col("COL", 4), col("COL", 3), scale=0.5)
+    ts(col("PI", 3), col("PI", 0), 7, A.bitwise_and)
+    cp(a("COL", 0, 3), a("PI", 1, 4))
+    both(col("COL", 4), col("COL", 2), scale=0.5)
     both(a("COL", 10, 12), a("COL", 1, 3), scale=-1.0)
     both(a("BS32"), a("BW", 64, 208))
-    for n, c in (("DT", 1152.0), ("DS", 0.0), ("DZ", 14337.0 - 16384), ("DG", 8960.0), ("DZ0", 8192.0)):
+    for n, c in (("DT", 1152.0), ("DS", 0.0), ("DZ", 12672.0), ("DG", 8960.0), ("DZ0", 8192.0)):
         both(a(n), a("J", 0, 72), bias=c)
     fill("PA", 0, 8, 0.0)
     for s in range(2):
@@ -547,11 +568,12 @@ def rank_program(g, core, T, topo):
     sel(row("R8", 0, 128, 8), row("ONEF", 0, 128, 8), [[-1, 8], [0, 16]], 0, 1)
     sel(row("R8X", 0, 64, 8), row("ONEF", 0, 64, 8), [[0, 8], [-1, 8]], 0, 1)
     mark()
-    sel(a("SPD"), a("ONE", 0, 288), [[-1, 2], [-16, 9], [1000, 16]], -15000, 1)
+    sel(a("SPD"), a("ONE", 0, 144), [[-16, 9], [1000, 16]], -15000, 1)
+    both(a("SPD32"), a("SPD"), scale=2.0)
     for i in range(8):
         sel(a("SPR", 256 * i, 256 * i + 256), a("ONE", 0, 256), [[-1, 2], [-16, 8], [0, 16]], -2 * i, 1)
     for i in range(2):
-        iota(row("TIE", 256 * i, 256 * i + 256), [[0, 32], [1, 8]], -7, 0)
+        iota(row("TIE", 256 * i, 256 * i + 256), [[0, 32], [1, 8]], -8, 0)
     mark()
     fill("RST", 0, 512, 1.0)
     fill("RST", 0, 512, 0.0, 64, 8)
@@ -566,23 +588,24 @@ def rank_program(g, core, T, topo):
     sel(a("TRIC"), a("TS"), [[1, 128]], 0, -1, A.not_equal, -4096.0)
     iota(a("S4", 0, 32), [[0, 16], [16, 2]], 0, 0)
     both(h64("S17"), h64("SUM"), scale=17.0)
-    fill("C15", 0, 512, 1536.0, p1=64)
-    for n, c in (("NID", -1.0), ("ID32", 1.0), ("NBIG", -16384.0), ("PBIG", 16384.0), ("NID32", -1.0), ("N8K", -8192.0), ("N16K", -16384.0)):
+    both(h64("S25"), h64("SUM"), scale=25.0)
+    for n, c in (("NID", -1.0), ("ID32", 1.0), ("NBIG", -16384.0), ("PBIG", 16384.0), ("NID32", -1.0), ("N8K", -8192.0), ("N16K", -16384.0),
+                 ("P16K", 16384.0)):
         both(a(n), a("ID"), scale=c)
-    act(col("EX", 0), col("COL", 0), F.Exp, scale=LN2)
+    act(col("EX", 0), col("COL", 0), F.Sigmoid, -36 * LN2, LN2)
     cp(col("COL", 5), col("EX", 0))
     both(a("BWP"), a("BW", 64, 208), scale=col("COL", 5), v=(col("COL", 5), A.mult))
-    for t in range(2):
-        ts(col("COL", 6 + t), col("COL", 0), float(t), A.is_equal, -16384.0 / M20, A.mult)
+    ts(col("COL", 6), col("COL", 0), 0.0, A.is_equal, -64.0 / M20, A.mult)
+    both(a("ONEP"), a("DEC", 0, 256), bias=-32.0, scale=col("COL", 6), v=(col("COL", 6), A.mult, -32.0, A.add))
     both(a("ONES32"), a("ONESB"))
     both(a("NHM"), a("ONESB"), scale=-M20 / 2)
     both(a("BJ"), a("BW", 64, 208), scale=col("COL", 4), v=(col("COL", 4), A.mult))
     ts(a("LM"), a("S4", 0, 32), col("COL", 0), A.add)
     for n, lo, hi, c in (("TABT", 512, 528, -8 * M20), ("TABG0", 560, 576, -8 * M20), ("TABG1", 560, 576, -8 * M20), ("FT", 512, 528, 0.0),
-                         ("FG", 560, 576, 0.0), ("D0", 0, 48, 0.0), ("CT", 0, 1, 0.0), ("CG", 0, 1, 0.0), ("WB", 0, 16, 0.0),
+                         ("FG", 560, 576, 0.0), ("D0", 0, 48, 0.0), ("CT", 0, 1, 0.0), ("CG", 0, 1, 0.0), ("WB", 0, 16, 7.0),
                          ("REM", 0, 1, -3072.0), ("RM2", 0, 1, -3968.0),
-                         ("W00", 0, 16, 96.0), ("W01", 0, 16, 96.0), ("W10", 0, 16, 96.0), ("W11", 0, 16, 96.0)):
-        fill(n, lo, hi, c, es="SVG")
+                         ("W00", 0, 16, 0.0), ("W01", 0, 16, 96.0), ("W10", 0, 16, 0.0), ("W11", 0, 16, 96.0)):
+        fill(n, lo, hi, c)
 
     def offsets(fl, nl, x, b0, b1, floor=False):
         c, pp, oo = a("C" + x, 1, nl + 1), a("PP" + x, 0, nl), a("OO" + x, 0, nl)
@@ -608,7 +631,12 @@ def rank_program(g, core, T, topo):
         mark()
         one = 1.0 if src == "A1" else 0.0
         pair(a("FI"), a(src), (8192.0 + one, A.is_ge), (F.Sign, -8192.5, 1.0), (F.Relu, 0.0, 1.0), "SV" if one else "V")
-        fill("WT", 0, 768, -8 * M20, 384, es="SVG")
+        if one:
+            dmas("Y", [(a("WT", 0, 768), a("WG", 0, 768))], 3.0)
+        else:
+            fill("WT", 0, 768, -8 * M20)
+            fill("WG", 0, 1152, -8 * M20, 576)
+            dmas("Y", [(a("LOW"), a("WG", 0, 1152))], 3.0, [first])
         fill("INV", 1024, 4096, 0.0, 768, 4)
         offsets("FI", 32, "T", 4, 5)
         mms([(P(7), row("E8", 0, 128), row("J", 0, 512)), (P(7), row("ONE", 0, 128, 16), row("DEC", 0, 512, 16))], True, False)
@@ -632,6 +660,11 @@ def rank_program(g, core, T, topo):
         ts(a("N3", 0, 48), a("N1", 0, 48), MASK, A.bitwise_and)
         ts(a(held), a("N3", 0, 48), 0.0, A.is_gt)
 
+    def slots():
+        act(a("SGA"), a("INV", 1024, 4096, 4), F.Sign, bias=-0.5)
+        act(a("SGB"), a("INV", 1024, 4096, 4), F.Sign, bias=M20 - 0.5, scale=-1.0)
+        mms([(P(4, 0, 48), view("BJ", m), a(n, m, 768, 16)) for n in ("SGA", "SGB") for m in range(16)])
+
     def lists_a(banks):
         for e in range(2):
             for s in range(2):
@@ -647,46 +680,65 @@ def rank_program(g, core, T, topo):
 
     def order_tables(t, b):
         mark()
-        x, r = (a("T1"), a("MN")) if t == 0 else (a("T2"), a("T1"))
-        both(x, a("J"), bias=col("PL", 14 + t), scale=col("PL", 3), v=(col("PL", 3), A.mult, col("PL", 14 + t), A.add))
-        both(r, x, bias=2.0 ** -14, scale=2.0 ** -13)
-        whole(r, r)
-        mms([(P(b), a("ID32"), x), (P(b), a("N8K"), r)])
-        ts(a("UI", 0, 32), P(b, 0, 32), 4096.0, A.add)
-        both(a("UH"), P(b), bias=199.5009765625, scale=1.0 / 512)
-        act(a("POW%d" % t), a("UH"), F.Exp, bias=191 * LN2, scale=-LN2)
+        if t == 0:
+            u, c = a("UJ"), 0.0
+            ts(u, a("J"), col("PL", 3), A.mult, col("PL", 4), A.add)
+            ts(u, u, 8191, A.bitwise_and)
+            cp(a("UI", 0, 32), a("UJ", 0, 32))
+            ts(a("UH"), u, 1.0 / 512, A.mult, 191.5009765625, A.add)
+        else:
+            x, r, u, c = a("T2"), a("T1"), P(b), 4096.0
+            both(x, a("J"), bias=col("PL", 15), scale=col("PL", 3), v=(col("PL", 3), A.mult, col("PL", 15), A.add))
+            both(r, x, bias=2.0 ** -14, scale=2.0 ** -13)
+            whole(r, r)
+            mms([(u, a("ID32"), x), (u, a("N8K"), r)])
+            ts(a("UI", 0, 32), P(b, 0, 32), c, A.add)
+            both(a("UH"), u, bias=199.5009765625, scale=1.0 / 512)
+        act(a("POW%d" % t), a("UH"), F.Sigmoid, bias=171 * LN2, scale=-LN2)
         ts(a("N5", 0, 32), a("UI", 0, 32), 15, A.bitwise_and)
-        ts(col("COL", 12), col("N5", 0), 16384.0, A.mult, 4097.0 - M24, A.add)
-        both(a("TABG%d" % t, 48, 560), P(b), bias=col("COL", 12), v=(col("COL", 12), A.add))
+        ts(col("COL", 12), col("N5", 0), 16384.0, A.mult, c + 1 - M24, A.add)
+        if t == 0:
+            ts(a("TABG0", 48, 560), u, col("COL", 12), A.add)
+        else:
+            both(a("TABG1", 48, 560), u, bias=col("COL", 12), v=(col("COL", 12), A.add))
         ts(a("N6", 0, 32), a("UI", 0, 32), 4, A.arith_shift_right, 31, A.bitwise_and)
         ts(a("N5", 0, 32), a("N5", 0, 32), 32.0, A.mult)
         tt(a("N5", 0, 32), a("N5", 0, 32), a("N6", 0, 32), A.add)
         cp(a("LW%d" % t), a("N5", 0, 32))
 
+    def place(out, nl):
+        x, n3, n4 = a("N2", 0, nl), a("N3", 0, nl), a("N4", 0, nl)
+        ts(n3, x, 15, A.bitwise_and)
+        ts(n4, x, 4, A.arith_shift_right, 511, A.bitwise_and)
+        ts(x, x, 0x6000, A.bitwise_and)
+        ts(n3, n3, 512.0, A.mult)
+        tt(n4, n4, x, A.add)
+        tt(a(out), n3, n4, A.add)
+
     def round_tables(t):
         mark()
         ts(a("LB"), a("B1"), 0.125, A.mult, 15.4375, A.add)
-        cp(a("BH"), a("B1"))
+        if t == 1:
+            ts(a("BH"), a("B1"), -1.0, A.add)
         ts(a("CB"), a("BH"), 7, A.bitwise_and)
         both(a("HELD"), a("A1"), F.Sign, v=(0.0, A.is_gt))
         for b in range(2):
             c0 = 32 * (8 * b + t)
-            both(a("HB", b, 64, 2), a("B1", c0, c0 + 32), F.Sign, v=(0.0, A.is_gt))
+            ts(a("N2", b, 64, 2), a("B1", c0, c0 + 32), -1.0, A.add)
+        place("TG", 64)
         mark()
         both(a("TABT", 528, 544), a("TLK", 16 * t, 16 * t + 16))
-        both(a("ONEP"), a("DEC", 0, 256), scale=col("COL", 6 + t), v=(col("COL", 6 + t), A.mult))
+        dmas("Y", [(a("Z", 0, 12672, 1, 0, 128, 16), a("NIL"))], 3.0)
         ts(a("LI"), a("IE1"), 0.125, A.mult, 15.4375, A.add)
-        cp(a("N1", 0, 48), a("IE1"))
-        ts(a("N1", 0, 48), a("N1", 0, 48), 7, A.bitwise_and)
-        both(a("S3", 0, 48), a("IH"), bias=99.0, scale=-99.0)
-        tt(a("TL"), a("S3", 0, 48), a("N1", 0, 48), A.add)
+        ts(a("N2", 0, 48), a("IE1"), -1.0, A.add)
+        ts(a("N1", 0, 48), a("N2", 0, 48), 0x4007, A.bitwise_and)
+        cp(a("TL"), a("N1", 0, 48))
+        place("TI", 48)
         mms([(P(4, m, 512, 16), a("SPR", 128 * m, 128 * m + 128), a("TL", 0, 32)) for m in range(16)])
         mms([(P(5, m, 256, 16), a("SPR", 128 * m, 128 * m + 128), a("TL", 32, 48)) for m in range(16)])
         both(a("TAB", 0, 512), P(4))
         both(a("TAB", 512, 768), P(5, 0, 256))
         mark()
-        fill("WT", 0, 1152, -8 * M20, 288, es="SVG")
-        fill("WG", 0, 1152, -8 * M20, 288, es="SVG")
         mark()
         mms([(P(6), row("ONE", 0, 128), row("TIE", 0, 512))]
             + [(P(6, 256 * b + 64 * bl, 256 * b + 64 * bl + 64), a("HELD", 128 * bl, 128 * bl + 128), a("PT", 64 * b, 64 * b + 64)) for b in range(2) for bl in range(4)],
@@ -695,21 +747,30 @@ def rank_program(g, core, T, topo):
     def step(s, k):
         mark()
         w, gs = Wn(s, k), "G%d" % s
+        if k % 4 == 3:
+            for j in range(4):
+                sel(a("OWN%d" % s, j, 2048, 4), a(w, 16 + 512 * DIF, 528 + 512 * DIF), [[0, 512]], 0, 0)
         for hv in range(2):
-            b, o = 2 * s + hv, a(Wn(s, k + 1), 16 + 512 * hv, 528 + 512 * hv)
-            mm(P(b), h64("SUM" if k % 4 < 2 else "S17"), h64(w, 16 + 512 * hv, 528 + 512 * hv), True, False)
-            if k % 4 == 1:
-                mm(P(b), h64("SUM"), h64("C15"), False, False)
-            for q in (2 * hv, 2 * hv + 1):
-                for lo in range(256 * q, 256 * q + 256, PIECE):
-                    both(a(gs, 4 * lo, 4 * (lo + PIECE)), ix(a(w), a("LA", 256 * s + lo // 4, 256 * s + (lo + PIECE) // 4)))
+            b, v0, o = 2 * s + hv, 512 * hv, a(Wn(s, k + 1), 16 + 512 * hv, 528 + 512 * hv)
+            dif = k % 4 == 3 and hv == DIF
+            mm(P(b), h64("SUM" if k % 4 == 0 else "S25" if dif else "S17"), h64(w, 16 + v0, 528 + v0), True, False)
+            for lo, hi in zip(PIECES, PIECES[1:]):
+                if lo // 512 != hv:
+                    continue
+                out, got = a(gs, 4 * lo, 4 * hi), ix(a(w), a("LA", 256 * s + lo // 4, 256 * s + hi // 4))
+                if dif:
+                    tt(out, got, a("OWN%d" % s, 4 * (lo - v0), 4 * (hi - v0)), A.subtract)
+                else:
+                    both(out, got)
                     chain.append(len(nodes) - 1)
-                mms([(P(b, 256 * (q % 2), 256 * (q % 2) + 256), a("SUM"), a(gs, 1024 * q + j, 1024 * q + 1024, 4)) for j in range(4)], False, q % 2 == 1)
+                mms([(P(b, lo - v0, hi - v0), a("SUM"), a(gs, 4 * lo + j, 4 * hi, 4)) for j in range(4)], False, hi == v0 + 512)
             if k % 4 == 0:
-                both(o, P(b), bias=-768.0)
+                both(o, P(b), bias=-768.0 if k else 96.0)
             else:
                 both(a("Q%d" % hv), P(b), bias=-7.5 if k == 7 else -103.5)
                 tt(o, P(b), a("Q%d" % hv), A.subtract)
+        if k == 0:
+            fill(w, 0, 16, 96.0)
         mark()
         if k < 7:
             outgoing(s, k + 1)
@@ -718,8 +779,11 @@ def rank_program(g, core, T, topo):
             for hv in range(2):
                 for j in range(4):
                     b = (4, 5, 7)[(8 * s + 4 * hv + j) % 3]
-                    mms([(P(b), a("NID"), a(w, 16 + 512 * hv, 528 + 512 * hv)), (P(b), a("ID"), a(gs, 2048 * hv + j, 2048 * hv + 2048, 4))])
-                    act(a("D", 512 * j, 512 * j + 512), P(b), F.Abs)
+                    if hv == DIF:
+                        act(a("D", 512 * j, 512 * j + 512), a(gs, 2048 * hv + j, 2048 * hv + 2048, 4), F.Abs)
+                    else:
+                        mms([(P(b), a("NID"), a(w, 16 + 512 * hv, 528 + 512 * hv)), (P(b), a("ID"), a(gs, 2048 * hv + j, 2048 * hv + 2048, 4))])
+                        act(a("D", 512 * j, 512 * j + 512), P(b), F.Abs)
                     c0 = 128 * hv + 32 * s + j
                     mms([(P(6, c0 + 256 * pb + 64 * bb, c0 + 256 * pb + 64 * bb + 32 - j, 4), a("D", 512 * j + 256 * bb + pb, 512 * j + 256 * bb + 256, 2),
                           a("SEL", 0, 8)) for bb in range(2) for pb in range(2)], False, s == 1 and hv == 1 and j == 3)
@@ -739,19 +803,27 @@ def rank_program(g, core, T, topo):
         for i in range(4):
             s, u0 = i // 2, 8 * (i % 2)
             mms([(P(0, 0, 64), h64("BW", 79 - 64 * s - u, 207 - 64 * s - u), h64(w[s], 16 + 64 * u, 80 + 64 * u)) for u in range(u0, u0 + 8)], i == 0, i == 3)
-        mms([(P(3, 0, 64), a("NBIG"), a("HB"))] + [(P(3, b, 64, 2), a("ID32"), a("B1", 32 * (8 * b + t), 32 * (8 * b + t) + 32)) for b in range(2)], True, False)
+        mm(P(3, 0, 64), a("ID32"), a("TG"), True, False)
         ts(a("FLK"), P(0, 0, 64), col("PL", th), A.is_ge)
         mm(P(3, 0, 64), a("PBIG"), a("FLK"), False, True)
         tt(a("S1", 0, 64), P(3, 0, 64), a("DZ", 0, 64), A.min)
-        ts(a("LKA"), a("S1", 0, 64), 16383.0, A.add)
-        scatter("Z", "LKA", 64, "ONEP", 16, True)
-        mms([(P(0, 0, 48), a("NID"), a("OH"))] + [(P(0, 0, 48), spd(t, m), a("Z", 8192 + 8 * m, 14336, 128)) for m in range(16)])
-        both(a("OKA"), P(0, 0, 48), F.Relu, 0.0, -1.0, (-1.0, A.mult, 0.0, A.max))
+        cp(a("LKA"), a("S1", 0, 64))
+        marks("LKA", 64)
+        mark()
+        if t == 0:
+            mms([(P(7, 0, 48), a("NBIG"), a("MO")), (P(7, 0, 48), a("PBIG"), a("OH")), (P(7, 0, 48), a("PBIG"), a("OH"))], True, False)
+            for s in range(2):
+                mms([(P(7, 0, 48), h64("BW", 79 - 64 * s - m, 207 - 64 * s - m), h64("OB%d" % s, m, 768, 16)) for m in range(16)], False, s == 1)
+            ts(a("OKA"), P(7, 0, 48), col("PO", 0), A.is_ge)
+        else:
+            mms([(P(0, 0, 48), a("NID"), a("OH"))]
+                + [(P(0, 0, 48), view("SPD32", m), a("Z", 8192 + 4096 * (m % 2) + m // 2, 8576 + 4096 * (m % 2), 8)) for m in range(16)])
+            both(a("OKA"), P(0, 0, 48), F.Relu, 0.0, -1.0, (-1.0, A.mult, 0.0, A.max))
         send("OKA", 16, "AR", 0, 1, "al%d" % t, "la")
         mark()
         mms([(P(2, 0, 128, 1, 0, 64), h64("BX", 63 - 8 * q - 4 * s, 127 - 8 * q - 4 * s), h64(w[s], 16 + 256 * (q % 4) + q // 4, 272 + 256 * (q % 4), 2))
              for s in range(2) for q in range(8)])
-        ts(h64("ZX"), P(2, 0, 128, 1, 0, 64), col("PX", t, 64), A.is_lt, 100.0, A.mult)
+        both(h64("ZX"), P(2, 0, 128, 1, 0, 64), F.Relu, col("PX", 2 + t, 64), -200.0, (col("PX", t, 64), A.is_lt, 100.0, A.mult))
         for s in range(2):
             mms([(P(1), h64("BAND", 72 - 64 * s - 8 * b, 200 - 64 * s - 8 * b), h64(w[s], 16 + b, 1040, 2)) for b in range(2)], s == 0, s == 1)
         both(a("STH"), P(1), F.Relu, col("PL", 12 + t), M20, (col("PL", th + 1), A.is_ge, M20, A.mult))
@@ -766,18 +838,21 @@ def rank_program(g, core, T, topo):
             mms([(P(2 + b2, 256 * bb + b, 256 * bb + 256, 2), h64("XR", 128 * (4 * b + 2 * b2 + bb), 128 * (4 * b + 2 * b2 + bb) + 128), h64("CX"))
                  for b in range(2) for bb in range(2)])
             both(a("WB", 16 + 512 * b2, 528 + 512 * b2), P(2 + b2))
-        tt(a("BO"), ix(a("WB", 0, 1040), a("LI")), a("TAB"), A.is_equal)
+        tt(a("BO"), ix(a("WB", 0, 1040), a("LI")), a("TAB"), A.not_equal)
         send("BO", 256, "WB", 1040, -1, "be%d" % t, "lb")
         if t == 0:
+            sent = len(nodes) - 2
+            fill("WT", 0, 1152, -8 * M20, 1152, es="G")
+            nodes[-1]["dep"].append(sent)
             order_tables(1, 5)
         mark()
         mms([(P(0), a("LBM", 128 * b, 128 * b + 128), a("WB", 16 + b, 1040, 2)) for b in range(2)])
         pair(a("K1"), P(0), (col("COL", 2), A.is_equal, 16384.0, A.mult), (F.Abs, col("COL", 11), 1.0), (F.Relu, 16384.0, -16384.0))
         mark()
-        mms([(P(7, 0, 48), a("ID32"), a("IE1")), (P(7, 0, 48), a("NBIG"), a("IH")), (P(7, 0, 48), a("PBIG"), a("AR"))])
+        mms([(P(7, 0, 48), a("ID32"), a("TI")), (P(7, 0, 48), a("PBIG"), a("AR"))])
         tt(a("S2", 0, 48), P(7, 0, 48), a("DZ", 0, 48), A.min)
-        ts(a("LGI"), a("S2", 0, 48), 16383.0, A.add)
-        scatter("Z", "LGI", 48, "ONEP", 16, True)
+        cp(a("LGI"), a("S2", 0, 48))
+        marks("LGI", 48)
         tt(a("FG", 0, 48), a("AR"), a("IH"), A.is_gt)
         mm(P(7, 0, 48), a("ONESB"), a("FG", 0, 48))
         node({"V": (lambda q: q.tensor_reduce(ap(col("D0", 33)), ap(P(7, 0, 48)), AxisListType.X, A.add), (1, 64, 0, 0, 0)),
@@ -786,8 +861,8 @@ def rank_program(g, core, T, topo):
         mark()
         mm(P(1), a("NID32"), a("A1"), True, False)
         mm(P(1), a("ID"), a("K1"), False, False)
-        for r0 in range(0, 16, 4):
-            mms([(P(1), spd(t, r), a("Z", r, 8192, 16)) for r in range(r0, r0 + 4)], False, r0 == 12)
+        dmas("Y", [(a("ZD"), a("Z", 0, 8192, 1, 0, 128, 16))])
+        mm(P(1), a("P16K"), a("ZD"), False, True)
         tt(a("F1"), P(1), a("STH"), A.is_ge)
         both(P(1) if t == 0 else a("A1"), P(1), F.Relu, 0.0, -1.0, (-1.0, A.mult, 0.0, A.max))
         mm(P(2), a("ONESB"), a("F1"))
@@ -803,7 +878,7 @@ def rank_program(g, core, T, topo):
                 lo % 256 == 0, hi % 256 == 0)
         mark()
         mms([(P(7, 0, 48), spd(0, m), a("WB", 1040 + m, 1808, 16)) for m in range(16)])
-        tt(a("OH"), a("OKA"), P(7, 0, 48), A.is_gt)
+        tt(a("OH"), a("OKA"), P(7, 0, 48), A.min)
         both(a("FR"), a("OH", 16 * t, 16 * t + 16), bias=1.0, scale=-1.0)
         mm(P(4, 0, 16), a("ONESB"), a("FR"))
         mm(P(4, 16, 32), a("TRIC"), a("FR"))
@@ -817,7 +892,7 @@ def rank_program(g, core, T, topo):
         for lo in (0, 16):
             both(a("WJ", 16 * lo, 16 * lo + 256), ix(a("FB"), a("LW%d" % t, lo, lo + 16)))
         mms([(P(7, 0, 32), view("BWP", m), a("WJ", m, 512, 16)) for m in range(16)])
-        both(a("WF"), P(7, 0, 32), bias=0.25)
+        both(a("WF"), P(7, 0, 32), bias=0.25 * M20, scale=2.0 ** 56)
         tt(a("T1"), ix(a("WF"), a("LM")), a("POW%d" % t), A.mult)
         whole(P(7), a("T1"))
         tt(a("FG", 48, 560), P(7), a("T1"), A.is_gt)
@@ -826,7 +901,7 @@ def rank_program(g, core, T, topo):
         both(a("BM"), P(6), F.Relu, v=(0.0, A.max))
         if t == 1:
             both(a("BM"), a("BM"), bias=-1.0)
-            dmas("Y", [(a("YS", 0, 512, 1, r, 128, 16), a("BM", 32 * r, 32 * r + 32)) for r in range(16)], 4.0)
+            dmas("Y", [(a("YS", 0, 512, 1, r, 128, 16), a("BM", 32 * r, 32 * r + 32)) for r in range(16)], 6.0)
         mark()
         mm(P(5), a("ID32"), a("TABT", 0, 512), True, False)
         mm(P(5), a("TRIQ"), a("FT", 0, 512), False, True)
@@ -839,8 +914,7 @@ def rank_program(g, core, T, topo):
         mark()
         both(a("HIT"), a("ZT"), F.Relu, 0.0, -32.0, (-32.0, A.mult, 0.0, A.max))
         act(a("SG"), a("ZT"), F.Sign, 0.5 - M20)
-        if t == 1:
-            partners(t, (0, 1, 6))
+        partners(t, (0, 6, 0) if t == 0 else (0, 1, 6))
         mark()
         mm(P(2), a("ID32"), a("TABG%d" % t, 0, 512), True, False)
         mm(P(2), a("TRIQ"), a("FG", 0, 512), False, True)
@@ -852,7 +926,11 @@ def rank_program(g, core, T, topo):
             ends("LE2", 3, "G", 2)
         pack("G", 36, FINE)
         dmas("Y", [(rows, a("YS" if t == 1 else "BM"))])
-        mms([(P(7, 0, 72), view("BS32", m), a("YG", m, 1152, 16)) for m in range(16)])
+        if t == 0:
+            dmas("Y", [(a(n, 0, 1152), a("LOW")) for n in ("WT", "WG")], 4.0)
+        halves = ((7, 0, 72),) if t == 0 else ((7, 0, 36), (6, 36, 72))
+        for b, lo, hi in halves:
+            mms([(P(b, lo, hi), view("BS32", m), a("YG", 16 * lo + m, 16 * hi, 16)) for m in range(16)])
         mark()
         for b, (lo, hi) in zip((5, 3, 4, 2), FINE):
             mm(P(b, 0, hi - lo), a("NID"), a("HIT", lo, hi), True, False)
@@ -864,30 +942,31 @@ def rank_program(g, core, T, topo):
                 ts(a("FGI", lo, hi), a("FGI", lo, hi), 0x3FFF, A.bitwise_and)
                 tt(a("A1", lo, lo + 256), a("FGI", lo, lo + 256), P(1, lo, lo + 256), A.add)
             lists_a((0, 2, 3, 1))
-            mark()
-            partners(t, (4, 5, 6))
         else:
             x, r = a("PAY", 0, 512), a("REM", 16, 528)
             tt(x, ix(a("FL"), a("LE", 0, 32)), a("FT", 0, 512), A.mult)
             both(r, x, bias=-0.4375, scale=2.0 ** -14)
             whole(r, r)
-            mms([(P(1), a("ID32"), a("A1")), (P(1), a("N16K"), r), (P(1), a("ID32"), x)])
+            mm(P(1), a("ID32"), a("A1"), True, False)
+            mm(P(1), a("ID32"), x, False, False)
+            mm(P(1), a("N16K"), r, False, True)
             both(a("A1"), P(1), bias=-1.0)
             dmas("S", [(T.yd[:], a("A1"))])
         mark()
-        n = [a("N%d" % i, 0, 72) for i in (5, 6, 7, 8)]
-        ts(n[0], P(7, 0, 72), -1.0, A.add)
-        if t == 0:
-            ts(n[1], n[0], 9, A.arith_shift_right, 0x1E0, A.bitwise_and)
-            ts(n[2], n[0], 4, A.arith_shift_right, 31, A.bitwise_and)
-            ts(n[3], n[0], FLAG + 0x1E00, A.bitwise_and)
-            tt(n[1], n[1], n[3], A.add)
-        else:
-            ts(n[1], n[0], 5, A.arith_shift_right, 0x7E00, A.bitwise_and)
-            ts(n[2], n[0], 4, A.arith_shift_right, 511, A.bitwise_and)
-        tt(n[1], n[1], n[2], A.add)
-        tt(n[1], n[1], a("DZ0"), A.min)
-        cp(a("LZ"), n[1])
+        for b, lo, hi in halves:
+            n = [a("N%d" % i, lo, hi) for i in (5, 6, 7, 8)]
+            ts(n[0], P(b, lo, hi), -1.0, A.add)
+            if t == 0:
+                ts(n[1], n[0], 9, A.arith_shift_right, 0x1E0, A.bitwise_and)
+                ts(n[2], n[0], 4, A.arith_shift_right, 31, A.bitwise_and)
+                ts(n[3], n[0], FLAG + 0x1E00, A.bitwise_and)
+                tt(n[1], n[1], n[3], A.add)
+            else:
+                ts(n[1], n[0], 5, A.arith_shift_right, 0x7E00, A.bitwise_and)
+                ts(n[2], n[0], 4, A.arith_shift_right, 511, A.bitwise_and)
+            tt(n[1], n[1], n[2], A.add)
+            tt(n[1], n[1], a("DZ0", lo, hi), A.min)
+            cp(a("LZ", lo, hi), n[1])
         scatter("ROW", "LZ", 72, "YT", 18)
         if t == 1:
             dmas("Y", [(T.ya[:], rows)])
@@ -902,16 +981,14 @@ def rank_program(g, core, T, topo):
             scan(a("FL2", lo, hi), a("HIG", lo, hi), P(4 + b, 0, hi - lo), 0.0 if b == 0 else col("FL2", lo - 1), A.min, A.max)
         mms([(P(6, 0, 48), spd(0, m), a("BO", m, 768, 16)) for m in range(16)])
         tt(a("S4", 0, 48), ix(a("FL2"), a("LE2", 0, 3)), a("FG", 0, 48), A.mult)
-        tt(a("KEEP"), a("AR"), P(6, 0, 48), A.is_gt)
+        tt(a("KEEP"), a("AR"), P(6, 0, 48), A.min)
         tt(a("IE1"), a("IE1"), a("KEEP"), A.mult)
         tt(a("IE1"), a("IE1"), a("S4", 0, 48), A.add)
         ts(a("IH"), a("IE1"), 0.0, A.is_gt)
 
     mark()
-    ts(a("A1"), a("DEN"), 1.0, A.add)
+    ts(a("A1"), a("DEN", 0, 512), 1.0, A.add)
     lists_a((0, 1, 2, 3))
-    for s in range(2):
-        both(a(Wn(s, 0), 16, 1040), a("XL%d" % s), bias=96.0)
     invert("AXO", "OH")
     ts(a("VO"), a("N2", 0, 48), 16.0, A.add)
     for s in range(2):
@@ -919,8 +996,13 @@ def rank_program(g, core, T, topo):
         cp(a("LO%d" % s), P(2 + s, 0, 48))
         outgoing(s, 0)
     mark()
-    fill("Z", 0, 8192, 0.0, 512, es="SVG")
-    fill("Z", 8192, 14336, 0.0, 768, 8)
+    slots()
+    ts(a("MO"), P(4, 0, 48), 0.0, A.is_equal)
+    mark()
+    fill("ZG", 0, 792, 0.0)
+    dmas("Y", [(a("NIL"), a("ZG", 0, 792))], 3.0, [first])
+    for lo in (8192, 12288):
+        fill("Z", lo, lo + 384, 0.0)
     mark()
     cp(row("PARF", 0, 6, 8), row("PARI", 0, 6, 8))
     mm(P(6, 0, 6), row("R8", 0, 128, 8), row("PARF", 0, 6, 8))
@@ -929,9 +1011,11 @@ def rank_program(g, core, T, topo):
     both(a("PL", 8, 11), P(6, 0, 3), bias=1536.0)
     both(col("PL", 12), P(6, 1, 2), bias=-1535.5 * M20, scale=-M20)
     both(col("PL", 13), P(6, 1, 2), bias=0.5 * M20, scale=-M20)
-    both(a("PL", 14, 16), P(6, 4, 6), bias=-1023.5 * 8192)
+    both(col("PO", 0), P(6, 0, 1), bias=1536.0 + 16384)
+    both(col("PL", 15), P(6, 5, 6), bias=-1023.5 * 8192)
     both(col("PX", 1, 64), P(6, 10, 11, 1, 0, 64))
     both(col("PX", 0, 64), P(6, 10, 11, 1, 0, 64), bias=1536.0)
+    both(a("PX", 2, 4, 1, 0, 64), a("PX", 0, 2, 1, 0, 64), bias=-100.0, scale=200.0)
     invert("A1", "IH")
     mark()
     both(a("J"), a("J"), bias=col("COL", 10), v=(col("COL", 10), A.add))
@@ -940,9 +1024,7 @@ def rank_program(g, core, T, topo):
         both(a("TABG%d" % t, 0, 48), a("TLK"), bias=float(FLAG))
     both(a("TABT", 0, 512), a("J"), bias=1.0 - M24)
     mark()
-    act(a("SGA"), a("INV", 1024, 4096, 4), F.Sign, bias=-0.5)
-    act(a("SGB"), a("INV", 1024, 4096, 4), F.Sign, bias=M20 - 0.5, scale=-1.0)
-    mms([(P(4, 0, 48), view("BJ", m), a(n, m, 768, 16)) for n in ("SGA", "SGB") for m in range(16)])
+    slots()
     ts(a("S1", 0, 48), a("N2", 0, 48), 8.0, A.mult, 1.0, A.add)
     tt(a("S1", 0, 48), a("S1", 0, 48), P(4, 0, 48), A.add)
     tt(a("IE1"), a("S1", 0, 48), a("IH"), A.mult)

import math
from concourse.bass import DstId, RemoteDMATransfer
from concourse.mybir import AluOpType as A, ActivationFunctionType as F, AxisListType

B16, F32, I32, U16 = "bfloat16", "float32", "int32", "uint16"
_SB = {
    B16: dict(W00=1808, W01=1808, W10=1808, W11=1808, WB=1808, G0=4096, G1=4096, D=2048, OB0=768, OB1=768, BO=768, OWN0=2048, OWN1=2048,
              Q0=512, Q1=512, ONE=576, DEC=1152, TIE=512, RST=512, BLK=208, TS=128, DMP=128, TRIQ=128, TRIC=128, PARD=128, NHM=128, BW=208,
              BWP=144, BAND=208, SPD=144, SPR=2048, BJ=144, SUM=128, S17=128, S25=128, ID=128, NID=128, NBIG=128, PBIG=128, SEL=16, PT=128, BX=128,
              XR=1024, LBM=256, TB=128, FT=544, FG=576, FI=512, F1=512, HELD=512, K1=512, STH=512, FB=512, WJ=512, UH=512, POW0=512, POW1=512,
              MO=48, HIT=1152, SG=1152, HIG=768, TAB=768, SGA=768, SGB=768, C0=64, CX=128, CT=48, CG=48, OH=48, OKA=48, AR=48, IH=48, FR=16,
              TL=48, FLK=64, KEEP=48, EX=16),
    F32: dict(ONEF=144, ID32=128, ONES32=128, NID32=128, N8K=128, N16K=128, BS32=144, SUM32=128, PA=136, R8=128, R8X=64, E8=128, PARF=8, PL=16,
              PX=8, COL=16, J=512, DS=72, DZ=72, DZ0=72, DT=72, DG=72, A1=512, B1=512, BM=512, REM=528, PAY=544, PAYG=576, TABT=544, TABG0=576,
              TABG1=576, CI=128, TLK=48, WG=16784, WT=1808, ROW=9472, Z=13824, INV=4096, T1=512, T2=512, MN=512, ZT=1152, ZG=1152, YT=1152,
              YG=1152, FL=1152, ZD=512, ONEP=256, SPD32=144, P16K=128, PO=8,
              FL2=768, ZX=128, WF=32, D0=48, PPT=48, OOT=48, PPG=48, OOG=48, OO=80, IE1=48, TG=64, TI=48, S1=72, S2=72, S3=72, S4=72, RM2=32, VO=48),
    I32: dict(DEN=544, AXO=512, BH=512, CB=512, UI=208, FGI=544, UJ=512, PARI=8, PI=8, N1=80, N2=80, N3=80, N4=80, N5=80, N6=80, N7=80, N8=80),
    U16: dict(LA=512, LB=512, LO0=48, LO1=48, LI=48, LKA=64, LGI=48, LST=48, LSG=48, LS=48, LE=48, LE2=8, LZ=72, LW0=32, LW1=32, LM=32),
}
_ALIAS = dict(SGA=("D", 0), SGB=("D", 784), WT=("WG", 1152), ROW=("WG", 2960), INV=("WG", 2960),
              Z=("WG", 2960), CB=("AXO", 0), FGI=("DEN", 0), UJ=("DEN", 0), T2=("BM", 0))
PLACE, SCRATCH = {}, {}
for _d, _t in _SB.items():
    _o = 0
    for _n, _w in _t.items():
        if _n in _ALIAS:
            PLACE[_n] = (PLACE[_ALIAS[_n][0]][0], PLACE[_ALIAS[_n][0]][1] + _ALIAS[_n][1], _w)
        elif _w > 600:
            PLACE[_n] = (_n, 0, _w)
            SCRATCH[_n] = ("sbuf", [128, _w], _d)
        else:
            PLACE[_n] = ("pool" + _d, _o, _w)
            _o += (_w + 15) // 16 * 16
    SCRATCH["pool" + _d] = ("sbuf", [128, _o], _d)
for _i in range(8):
    SCRATCH["P%d" % _i] = ("psum", [128, 512], F32)
    PLACE["P%d" % _i] = ("P%d" % _i, 0, 512)
PLACE["ONESB"] = (PLACE["BLK"][0], PLACE["BLK"][1] + 64, 128)
for _n, _w in (("YS", 512), ("LOW", 1152), ("NIL", 792)):
    SCRATCH[_n] = ("dram", [128, _w], F32)
    PLACE[_n] = (_n, 0, _w)
SEMAPHORES = (["cV", "cS", "cP", "cG", "cX", "l0", "l1", "la", "lb"] + ["x%d" % i for i in range(16)] + ["al0", "al1", "be0", "be1"]
              + ["d%d" % i for i in range(24)])
M20, M24 = float(2 ** 20), float(2 ** 24)
MASK, FLAG = 2 ** 20 - 1, 3 * 2 ** 18
LN2, RND = math.log(2.0), 1.5 * 2 ** 23
COSTS = ((0.05, 0.83e-3, 1.3e-3, 3.15e-3, 0.45e-3, 0.1, 4.5, 1.1), (0.06, 1.04e-3, 1.6e-3, 4e-3, 0.53e-3, 0.1, 4.2, 1.0),
         (0.05, 0.9e-3, 1.2e-3, 4.5e-3, 0.5e-3, 0.14, 6.0, 1.5), (0.06, 1.1e-3, 2.0e-3, 2.5e-3, 0.66e-3, 0.1, 5.0, 1.2))
CALL = {"V": 1.0, "S": 1.3}
HALF, LOOK, GAP, TURNS, MOVES, HEAT = 0.7, 0.7, 0.8, 800, 16000, 0.002
PIECES = (0, 192, 384, 512, 640, 768, 896, 1024)
SHY, LIFT = {"V": 8.0, "S": 4.0}, (-8.0, -3.0, -1.0, 1.0, 3.0, 8.0)
DIF = 1
ORDER = []


def rank_program(g, core, T, topo):
    rank = T.rank_of(core)
    if rank is None:
        return
    N = len(T.cores)
    QU = {"V": g.vector, "S": g.scalar, "P": g.tensor, "G": g, "Y": g.sync}
    nodes, rec, nd, lsum, chain, half, part = [], {}, [0], {}, [], [0], [0]

    def a(n, lo=0, hi=None, st=1, p0=0, p1=128, ps=1):
        b, o, w = PLACE[n]
        return (b, o + lo, o + (w if hi is None else hi), st, p0, p1, ps)

    def h64(n, lo=0, hi=None, st=1, s=0):
        return a(n, lo, hi, st, 64 * s, 64 * s + 64)

    def ap(x):
        if not isinstance(x, tuple):
            return x
        if x[0] == "@":
            return ap(x[1]).indirect(ap(x[2]))
        if x[6] != 1:
            return T[x[0]][x[4]:x[5]:x[6], x[1]:x[2]]
        return T[x[0]][x[4]:x[5], x[1]:x[2]:x[3]] if x[3] != 1 else T[x[0]][x[4]:x[5], x[1]:x[2]]

    def flat(xs):
        o = []
        for x in xs:
            if isinstance(x, tuple):
                o += [x[1], x[2]] if x[0] == "@" else [x]
        return o

    def psum(x):
        return SCRATCH[x[0]][0] == "psum"

    def node(ways, rd, wr, lat=(0, 0, 0), tok=None, after=()):
        me, dep = len(nodes), set(after)
        for kind, xs in (("r", rd), ("w", wr)):
            for x in xs:
                for (lo, hi, k, n) in rec.get(x[0], []):
                    if psum(x) or (lo < x[2] and x[1] < hi and (kind == "w" or k == "w")):
                        dep.add(n)
        for kind, xs in (("r", rd), ("w", wr)):
            for x in xs:
                old = rec.get(x[0], [])
                if psum(x):
                    old = []
                elif kind == "w" and x[3:] == (1, 0, 128, 1):
                    old = [r for r in old if not (x[1] <= r[0] and r[1] <= x[2])]
                rec[x[0]] = old + [(x[1], x[2], kind, me)]
        nodes.append(dict(ways=ways, part=part[0], dep=sorted(dep), lat=lat, tok=tok))
        return me

    def mark():
        part[0] += 1

    def size(x):
        return (x[2] - x[1] + x[3] - 1) // x[3]

    def est(e, out, ins, two=False):
        xs = [x for x in [out] + ins if isinstance(x, tuple)]
        ind = [x for x in xs if x[0] == "@"]
        if ind:
            return (1, 0, 0, 16 * size(ind[0][2]), 0) if out[0] == "@" else (CALL[e], 0, 16 * size(ind[0][2]), 0, 0)
        f = 1.0
        if e == "V" and two:
            f = 1.0 if any(psum(x) for x in xs[1:]) else 2.0
        elif e == "V" and all(SCRATCH[x[0]][2] in (B16, U16) for x in xs if size(x) > 1):
            f = 0.5
        return (CALL[e], max(64, max(size(x) for x in xs) * f), 0, 0, 0)

    def op(out, ins, ways):
        node(ways, flat(ins) + ([out[2]] if out[0] == "@" else []), [out[1]] if out[0] == "@" else [out])

    def ix(w, o):
        return ("@", w, o)

    def vop(o, ins, fn, two=False):
        op(o, ins, {"V": (fn, est("V", o, ins, two))})

    def cp(o, i):
        vop(o, [i], lambda q: q.tensor_copy(ap(o), ap(i)))

    def ms(o, c):
        vop(o, [], lambda q: q.memset(ap(o), c))

    def tt(o, x, y, f):
        vop(o, [x, y], lambda q: q.tensor_tensor(ap(o), ap(x), ap(y), f), True)

    def tsf(o, x, s1, f1, s2=None, f2=None):
        if f2 is None:
            return lambda q: q.tensor_scalar(ap(o), ap(x), ap(s1), None, f1)
        return lambda q: q.tensor_scalar(ap(o), ap(x), ap(s1), ap(s2), f1, f2)

    def ts(o, x, s1, f1, s2=None, f2=None):
        vop(o, [x, s1, s2], tsf(o, x, s1, f1, s2, f2))

    def scan(o, d0, d1, ini, f0, f1):
        vop(o, [d0, d1, ini], lambda q: q.tensor_tensor_scan(ap(o), ap(d0), ap(d1), ap(ini), f0, f1))

    def actf(o, i, f, bias, scale):
        return lambda q: q.activation(ap(o), ap(i), f, bias=ap(bias), scale=ap(scale))

    def act(o, i, f=F.Identity, bias=0.0, scale=1.0):
        op(o, [i, bias, scale], {"S": (actf(o, i, f, bias, scale), est("S", o, [i]))})

    def both(o, i, f=F.Identity, bias=0.0, scale=1.0, v=None):
        if v is not None:
            vf = tsf(o, i, *v)
        elif bias == 0.0 and scale == 1.0:
            vf = lambda q: q.tensor_copy(ap(o), ap(i))
        else:
            vf = tsf(o, i, scale, A.mult, bias, A.add)
        op(o, [i, bias, scale], {"S": (actf(o, i, f, bias, scale), est("S", o, [i])), "V": (vf, est("V", o, [i]))})

    def pair(o, i, v, s1, s2, es="SV"):
        def two(q):
            half[0] += 1
            actf(o, i, *s1)(q).then_inc(T.sem["cX"], 1)
            q.wait_ge(T.sem["cX"], half[0])
            return actf(o, o, *s2)(q)
        c = est("S", o, [i])
        ways = {"S": (two, (2 + 2 * c[0], 2 * c[1], 0, 0, 0)), "V": (tsf(o, i, *v), est("V", o, [i]))}
        op(o, [i] + list(v) + list(s1), {e: ways[e] for e in es})

    def whole(o, i):
        pair(o, i, (RND, A.add, RND, A.subtract), (F.Identity, RND, 1.0), (F.Identity, -RND, 1.0))

    def mms(items, start=True, stop=True):
        def fn(q):
            for i, (o, l, r) in enumerate(items):
                last = q.matmul(ap(o), ap(l), ap(r), start and i == 0, stop and i == len(items) - 1)
            return last
        c = sum(max(min(64, size(l)), size(r)) * (4 if SCRATCH[l[0]][2] == F32 else 1) + 8 for o, l, r in items)
        node({"P": (fn, (0, 0, 0, 0, c))}, [x for o, l, r in items for x in (l, r)], [items[0][0]], (0.05, 0, 0))

    def mm(o, l, r, start=True, stop=True):
        mms([(o, l, r)], start, stop)

    def scatter(win, lst, n, src, piece=16, same=False):
        for lo in range(0, n, piece):
            hi = min(n, lo + piece)
            cp(ix(a(win), a(lst, lo, hi)), a(src, 0, 16 * (hi - lo)) if same else a(src, 16 * lo, 16 * hi))

    def marks(lst, n):
        for lo in range(0, n, 16):
            o, c = ix(a("Z"), a(lst, lo, lo + 16)), (0, 0, 256, 0)
            op(o, [a("ONEP")], {"V": (tsf(o, a("ONEP"), 1.0 / 64, A.mult, 0.5, A.add), (1,) + c),
                                "S": (lambda q, o=o: q.activation(ap(o), ap(a("ONEP")), F.Sigmoid), (CALL["S"],) + c)})

    def iotaf(o, p, base, cm):
        kw = {} if SCRATCH[o[0]][2] == I32 else {"allow_small_or_imprecise_dtypes": True}
        return (lambda q: q.iota(ap(o), p, base, cm, **kw), (6, 2 * size(o), 0, 0, 0))

    def iota(o, p, base, cm):
        op(o, [], {"G": iotaf(o, p, base, cm)})

    def sel(o, i, p, base, cm, f=A.is_equal, fill=0.0):
        op(o, [i], {"G": (lambda q: q.affine_select(ap(o), ap(i), p, f, fill, base, cm), (7, 2 * size(o), 0, 0, 0))})

    def band(o, i, p, base, p2, base2):
        sel(o, i, p, base, 1, A.is_ge)
        sel(o, o, p2, base2, -1, A.is_ge)

    def fill(n, lo, hi, c, piece=1024, st=1, es="SV", p1=128):
        for l in range(lo, hi, piece * st):
            o = a(n, l, min(hi, l + piece * st), st, 0, p1)
            src = a("DEC", 0, size(o), 1, 0, p1)
            ways = {"S": (actf(o, src, F.Identity, c, 0.0), est("S", o, [src])), "V": (lambda q, o=o: q.memset(ap(o), c), est("V", o, [])),
                    "G": iotaf(o, [[0, size(o)]], int(c), 0)}
            op(o, [src], {e: ways[e] for e in es})

    def dmas(e, items, lat=2.3, after=()):
        sem = "d%d" % nd[0]
        nd[0] += 1

        def fn(q):
            for o, i in items:
                q.dma_start(ap(o), ap(i)).then_inc(T.sem[sem], 16)
        return node({e: (fn, (2 * len(items), 0, 0, 0, 0))}, flat([i for o, i in items]), flat([o for o, i in items]), (0, 0, lat),
                    (sem, 16 * len(items)), after)

    def send(src, w, dst, off, sign, rsem, lsem, free=()):
        tr = []
        for h in range(1, N):
            d = T.cores[(rank + sign * h) % N]
            eng = topo.engines(core, d)
            k = len(eng) // 4
            mine = eng[0::2] if h == 1 else eng[1::2][(h - 2) * k:(h - 1) * k]
            rid, pid = topo.addr(d, core)
            tr.append(RemoteDMATransfer(dst_ids=[DstId(rid=rid, pnc=pid)], dma_engine_mask=sum(1 << x for x in mine), remote_sem=T.sem[rsem],
                                        src=ap(a(src, w * (h - 1), w * h)), dst=ap(a(dst, off + w * (h - 1), off + w * h))))
        first = 0.0 if lsum else 2.5
        lsum[lsem] = lsum.get(lsem, 0) + 4 * k
        n = node({"G": (lambda q: q.remote_dma_fused(tr, local_sem=T.sem[lsem]), (14 + 20 * first, 0, 0, 0, 0))}, [a(src)], list(free),
                 (0, 0.8 if w > 64 else 0.6, 0), (lsem, lsum[lsem]))
        node({"R": (None, (0, 0, 0, 0, 0))}, [], [a(dst, off, off + 3 * w)], (0, 0, 0), (rsem, 4 * k), [n])

    def schedule():
        n, ES = len(nodes), "RPGYVS"
        views = []
        for m in COSTS:
            cost = [{e: sum(x * y for x, y in zip(c, m)) for e, (f, c) in x["ways"].items()} for x in nodes]
            lat = [x["lat"][0] + x["lat"][1] * m[6] + x["lat"][2] * m[7] for x in nodes]
            fwd, bwd = [[] for _ in nodes], [[] for _ in nodes]
            for u, x in enumerate(nodes):
                for d in x["dep"]:
                    gap = 0.0 if "P" in cost[d] and "P" in cost[u] else lat[d] + (0.0 if "R" in cost[d] else m[5])
                    fwd[d].append((u, gap))
                    bwd[u].append((d, gap))
            views.append((cost, lat, fwd, bwd))

        def replay(order, view):
            cost, lat, fwd, bwd = view
            free, fin = dict.fromkeys(ES, 0.0), [0.0] * n
            for i, e in order:
                t = free[e]
                for d, gap in bwd[i]:
                    if fin[d] + gap > t:
                        t = fin[d] + gap
                free[e] = fin[i] = t + cost[i][e]
            return max(fin[i] + lat[i] for i in range(n))

        def run(cost, out, into, link, prio, first, shy):
            nxt = dict(zip(link, link[1:]))
            left = [len(into[i]) for i in range(n)]
            for i in link[1:]:
                left[i] += 1
            rdy = list(first)
            ready = {e: set() for e in ES}
            free = dict.fromkeys(ES, 0.0)
            order, fin = [], [0.0] * n
            key = {e: [prio[i] - (shy.get(e, 0.0) if len(cost[i]) > 1 else 0.0) - 1e-7 * i for i in range(n)] for e in ES}
            for i in range(n):
                if left[i] == 0:
                    for e in cost[i]:
                        ready[e].add(i)
            while len(order) < n:
                t0, e = min((max(free[e], min(rdy[i] for i in ready[e])), j, e) for j, e in enumerate(ES) if ready[e])[::2]
                ke = key[e]
                i = max((i for i in ready[e] if rdy[i] <= t0 + 0.05), key=lambda j: ke[j])
                soon = [j for j in ready[e] if t0 + 0.05 < rdy[j] <= t0 + min(LOOK, cost[i][e]) and ke[j] > ke[i] + GAP]
                if soon:
                    i = max(soon, key=lambda j: ke[j])
                for x in cost[i]:
                    ready[x].discard(i)
                free[e] = fin[i] = max(t0, rdy[i]) + cost[i][e]
                order.append((i, e))
                for u, t1 in [(u, fin[i] + gap) for u, gap in out[i]] + ([(nxt[i], t0)] if i in nxt else []):
                    rdy[u] = max(rdy[u], t1)
                    left[u] -= 1
                    if left[u] == 0:
                        for x in cost[u]:
                            ready[x].add(u)
            return order, fin

        seed, unit = 2, [1.0] * len(views)
        nxt = dict(zip(chain, chain[1:]))
        cost, lat, fwd, bwd = views[0]
        level = [0.0] * n
        for i in range(n - 1, -1, -1):
            level[i] = min(cost[i].values()) + max([level[u] + gap for u, gap in fwd[i]] + [lat[i]])
            if i in nxt:
                level[i] = max(level[i], level[nxt[i]] + HALF * cost[i]["S"])

        def forward(prio):
            order, fin = run(cost, fwd, bwd, chain, prio, [0.0] * n, SHY)
            ends = [replay(order, v) for v in views]
            return sum(x / y for x, y in zip(ends, unit)), order, ends, fin
        unit = forward(level)[2]
        best, base, lift = forward(level), level, [0.0] * (part[0] + 1)
        for it in range(TURNS):
            seed = seed * 48271 % 2147483647
            if it % 12 == 11:
                prio, new = run(cost, bwd, fwd, chain[::-1], best[3], lat, SHY)[1], [0.0] * len(lift)
            else:
                prio, new = base, list(lift)
                for k in range(1 + seed % 2):
                    seed = seed * 48271 % 2147483647
                    new[seed % len(new)] += LIFT[(seed >> 10) % len(LIFT)]
            got = forward([prio[i] + new[nodes[i]["part"]] for i in range(n)])
            if got[0] <= best[0]:
                best, base, lift = got, prio, new
        order, eng = [i for i, e in best[1]], [None] * n
        for i, e in best[1]:
            eng[i] = e
        deps = [[d for d, gap in bwd[i]] for i in range(n)]
        subs = [[u for u, gap in fwd[i]] for i in range(n)]

        def times(lo, old):
            out, last = [], {}
            for i in order[:lo]:
                last[eng[i]] = i
            for (cost, lat, fwd, bwd), x in zip(views, old):
                fin = list(x[0])
                free = {e: fin[last[e]] if e in last else 0.0 for e in ES}
                for i in order[lo:]:
                    e = eng[i]
                    t = free[e]
                    for d, gap in bwd[i]:
                        if fin[d] + gap > t:
                            t = fin[d] + gap
                    free[e] = fin[i] = t + cost[i][e]
                out.append([fin, x[1], max(fin[i] + lat[i] for i in tail)])
            return sum(x[2] / w for x, w in zip(out, unit)), out

        def rests(hi, out):
            first = {}
            for i in reversed(order[hi + 1:]):
                first[eng[i]] = i
            for (cost, lat, fwd, bwd), x in zip(views, out):
                rest = x[1] = list(x[1])
                free = {e: rest[first[e]] if e in first else 0.0 for e in ES}
                for i in reversed(order[:hi + 1]):
                    e = eng[i]
                    t = max(free[e], lat[i])
                    for u, gap in fwd[i]:
                        if rest[u] + gap > t:
                            t = rest[u] + gap
                    free[e] = rest[i] = t + cost[i][e]

        def guess(lo, hi, span):
            before, after, rise = {}, {}, 0.0
            for p in range(lo - 1, -1, -1):
                before.setdefault(eng[order[p]], order[p])
                if len(before) == 4 and lo - p > 60:
                    break
            for p in range(hi + 1, n):
                after.setdefault(eng[order[p]], order[p])
                if len(after) == 4 and p - hi > 60:
                    break
            for (cost, lat, fwd, bwd), (fin, rest, end), w in zip(views, fins, unit):
                free, new, far = {e: fin[i] for e, i in before.items()}, {}, 0.0
                for i in span:
                    e = eng[i]
                    t = free.get(e, 0.0)
                    for d, gap in bwd[i]:
                        f = new.get(d, fin[d]) + gap
                        if f > t:
                            t = f
                    free[e] = new[i] = t = t + cost[i][e]
                    for u, gap in fwd[i]:
                        if pos[u] > hi and t + gap + rest[u] > far:
                            far = t + gap + rest[u]
                for e, u in after.items():
                    far = max(far, free.get(e, 0.0) + rest[u])
                rise += (far - end) / w if far > end else 0.0
            return rise

        def waits(v, fin):
            cost, lat, fwd, bwd = views[v]
            before, last = [None] * n, {}
            for i in order:
                before[i], last[eng[i]] = last.get(eng[i]), i
            i, out = max(tail, key=lambda j: fin[j] + lat[j]), []
            while i is not None:
                t, j = fin[i] - cost[i][eng[i]] - 1e-9, before[i]
                tight = [d for d, gap in bwd[i] if fin[d] + gap >= t]
                if j is not None and fin[j] >= t and j not in deps[i]:
                    out.append((j, i))
                    i = j
                else:
                    i = tight[0] if tight else None
            return out
        tail = [i for i in range(n) if not subs[i]]
        score, fins = times(0, [[[0.0] * n, [0.0] * n] for v in views])
        rests(n - 1, fins)
        arcs, pos = None, [0] * n
        top = (score, list(order), list(eng))
        for it in range(MOVES):
            seed = seed * 48271 % 2147483647
            if not arcs or it % 64 == 0:
                arcs = waits(it % len(views), fins[it % len(views)][0])
                for p, i in enumerate(order):
                    pos[i] = p
            j, i = arcs[(seed >> 8) % len(arcs)]
            kind, pj, pi = (seed >> 4) % 4, pos[j], pos[i]
            x = (i, j)[kind % 2]
            e0, heat = eng[x], HEAT * (1 - it / MOVES) * (seed >> 5 & 255) / 255
            if kind < 2:
                step = 1 if kind else -1
                for far in range((seed >> 16) % 8 - 3):
                    p = (pi if kind else pj) + step
                    while 0 <= p < n and eng[order[p]] != e0:
                        p += step
                    if 0 <= p < n:
                        pj, pi = (pj, p) if kind else (p, pi)
                span, tied = order[pj:pi + 1], {x}
                for u in (span if kind else span[::-1]):
                    if any(d in tied for d in (deps[u] if kind else subs[u])):
                        tied.add(u)
                if (order[pi] if kind else order[pj]) in tied:
                    continue
                one, two = [u for u in span if u in tied], [u for u in span if u not in tied]
                span = two + one if kind else one + two
            else:
                other = [e for e in cost[x] if e != e0]
                if not other:
                    continue
                eng[x], pj = other[(seed >> 16) % len(other)], pos[x]
                pi, span = pj, [x]
            if guess(pj, pi, span) <= heat:
                was = order[pj:pi + 1]
                order[pj:pi + 1] = span
                new, nf = times(pj, fins)
                if new <= score + heat:
                    rests(pi, nf)
                    score, fins, arcs = new, nf, None
                    if score < top[0]:
                        top = (score, list(order), list(eng))
                    continue
                order[pj:pi + 1] = was
            eng[x] = e0
        return [(i, top[2][i]) for i in top[1]]

    def emit():
        if not ORDER:
            ORDER.extend(schedule())
        for i, e in ORDER:
            nodes[i]["e"] = e
        cnt = {e: 0 for e in "VSPG"}
        seen = {e: {} for e in QU}
        total = {}

        def wait(e, tok):
            if seen[e].get(tok[0], 0) < tok[1]:
                QU[e].wait_ge(T.sem[tok[0]], tok[1])
                seen[e][tok[0]] = tok[1]
        for i, e in ORDER:
            x = nodes[i]
            if e != "R":
                need = {}
                for d in x["dep"]:
                    if not (e == "P" and nodes[d]["e"] == "P"):
                        sem, c = nodes[d]["tok"]
                        need[sem] = max(need.get(sem, 0), c)
                for tok in need.items():
                    wait(e, tok)
                if e == "G" and x["tok"] is None:
                    wait(e, ("cG", cnt[e]))
                r = x["ways"][e][0](QU[e])
                if x["tok"] is None:
                    cnt[e] += 1
                    r.then_inc(T.sem["c" + e], 1)
                    x["tok"] = ("c" + e, cnt[e])
            total[x["tok"][0]] = max(total.get(x["tok"][0], 0), x["tok"][1])
        for tok in total.items():
            wait("G", tok)

    def P(i, lo=0, hi=512, st=1, p0=0, p1=128):
        return a("P%d" % i, lo, hi, st, p0, p1)

    def col(n, i, p1=128):
        return a(n, i, i + 1, 1, 0, p1)

    def row(n, lo, hi, p1=1):
        return a(n, lo, hi, 1, 0, p1)

    def view(n, m, off=0):
        return a(n, off + 15 - m, off + 143 - m)

    def spd(q, m):
        return view("SPD", m, 144 * q)

    def Wn(s, k):
        return "W%d%d" % (s, k % 2)

    first = dmas("Y", [(a("AXO"), T.axo[:])])
    dmas("S", [(a("DEN", 0, 512), T.den[:])], 3.0)
    dmas("Y", [(h64(Wn(s, 0), 16, 1040, s=hh), T.x0[64 * s:64 * s + 64, :]) for s in range(2) for hh in range(2)]
         + [(row("PARI", 0, 6, 8), T.par[:])], 2.6, [first])
    dmas("Y", [(a("BH", 32 * r, 32 * r + 32), T.axo[r::16, :]) for r in range(16)], 6.0, [first])

    mark()
    ms(a("DEC"), -M20)
    ms(a("ONE"), 1.0)
    ms(a("BW"), 0.0)
    ms(row("E8", 0, 128), 0.125)
    fill("ONEF", 0, 144, 1.0)
    fill("TB", 0, 128, -2064.0)
    fill("SEL", 8, 16, -8.0)
    iota(a("UI", 0, 208), [[-16, 13], [0, 16]], 64, 1)
    iota(a("CI"), [[1, 128]], 0, -1)
    iota(col("PI", 0), [[0, 1]], 0, 1)
    iota(a("J"), [[16, 512]], 0, 1)
    ts(a("UI", 0, 208), a("UI", 0, 208), 4, A.arith_shift_right)
    ts(a("BLK"), a("UI", 0, 208), 0.0, A.is_equal)
    cp(a("BW", 15, 208, 16), a("BLK", 15, 208, 16))
    ts(a("ID"), a("CI"), 0.0, A.is_equal)
    sel(a("TS"), a("ONESB"), [[1, 128]], 0, -1, A.is_gt)
    sel(a("PARD"), a("ID"), [[0, 8], [1, 2], [0, 8]], 0, 0, A.is_gt)
    tt(a("DMP"), a("ONESB"), a("TS"), A.subtract)
    both(a("TRIQ"), a("TS"), scale=M20)
    sel(a("TRIQ"), a("TRIQ"), [[1, 128]], 0, -1, A.not_equal, M24)
    ts(col("PI", 1), col("PI", 0), 15, A.bitwise_and)
    ts(col("PI", 2), col("PI", 0), 112, A.bitwise_and)
    ts(col("PI", 3), col("PI", 0), 7, A.bitwise_and)
    cp(a("COL", 0, 3), a("PI", 1, 4))
    both(col("COL", 4), col("COL", 2), scale=0.5)
    both(a("COL", 10, 12), a("COL", 1, 3), scale=-1.0)
    both(a("BS32"), a("BW", 64, 208))
    for n, c in (("DT", 1152.0), ("DS", 0.0), ("DZ", 12672.0), ("DG", 8960.0), ("DZ0", 8192.0)):
        both(a(n), a("J", 0, 72), bias=c)
    fill("PA", 0, 8, 0.0)
    for s in range(2):
        sel(h64("SUM", s=s), h64("ONE", 0, 128, s=s), [[0, 2], [-1, 64]], 0, 1)
        for hh in range(2):
            sel(h64("PA", 8 + 64 * hh, 72 + 64 * hh, s=s), h64("ONEF", 0, 64, s=s), [[-16, 4], [-8, 4], [-1, 4]], -4 * hh, 1)
    both(a("SUM32"), a("SUM"))
    sel(a("PA", 8, 136), a("PA", 8, 136), [[0, 8], [-1, 4], [0, 4]], 1, 0, A.is_ge)
    mark()
    sel(row("R8", 0, 128, 8), row("ONEF", 0, 128, 8), [[-1, 8], [0, 16]], 0, 1)
    sel(row("R8X", 0, 64, 8), row("ONEF", 0, 64, 8), [[0, 8], [-1, 8]], 0, 1)
    mark()
    sel(a("SPD"), a("ONE", 0, 144), [[-16, 9], [1000, 16]], -15000, 1)
    both(a("SPD32"), a("SPD"), scale=2.0)
    for i in range(8):
        sel(a("SPR", 256 * i, 256 * i + 256), a("ONE", 0, 256), [[-1, 2], [-16, 8], [0, 16]], -2 * i, 1)
    for i in range(2):
        iota(row("TIE", 256 * i, 256 * i + 256), [[0, 32], [1, 8]], -8, 0)
    mark()
    fill("RST", 0, 512, 1.0)
    fill("RST", 0, 512, 0.0, 64, 8)
    band(a("SEL", 0, 8), a("SEL", 8, 16), [[-16, 4], [-64, 2]], 0, [[16, 4], [64, 2]], 15)
    sel(a("PT"), a("TB"), [[-8, 2], [-16, 8], [-1, 8]], 0, 1)
    band(h64("BAND"), h64("ONE", 0, 208), [[-16, 13], [1000, 2], [0, 8]], 64 - 1000, [[16, 13], [0, 2], [0, 8]], 15 - 64)
    band(h64("BX"), h64("ONE", 0, 128), [[-16, 128]], 16 * 63, [[16, 128]], 15 - 16 * 63)
    for i in range(4):
        sel(h64("XR", 256 * i, 256 * i + 256), h64("ONE", 0, 256), [[-8, 2], [-1, 8], [0, 16]], -16 * i, 1)
    for b in range(2):
        sel(a("LBM", 128 * b, 128 * b + 128), a("ONE", 0, 128), [[-16, 8], [1000, 2], [0, 8]], -1000 * b, 1)
    sel(a("TRIC"), a("TS"), [[1, 128]], 0, -1, A.not_equal, -4096.0)
    iota(a("S4", 0, 32), [[0, 16], [16, 2]], 0, 0)
    both(h64("S17"), h64("SUM"), scale=17.0)
    both(h64("S25"), h64("SUM"), scale=25.0)
    for n, c in (("NID", -1.0), ("ID32", 1.0), ("NBIG", -16384.0), ("PBIG", 16384.0), ("NID32", -1.0), ("N8K", -8192.0), ("N16K", -16384.0),
                 ("P16K", 16384.0)):
        both(a(n), a("ID"), scale=c)
    act(col("EX", 0), col("COL", 0), F.Sigmoid, -36 * LN2, LN2)
    cp(col("COL", 5), col("EX", 0))
    both(a("BWP"), a("BW", 64, 208), scale=col("COL", 5), v=(col("COL", 5), A.mult))
    ts(col("COL", 6), col("COL", 0), 0.0, A.is_equal, -64.0 / M20, A.mult)
    both(a("ONEP"), a("DEC", 0, 256), bias=-32.0, scale=col("COL", 6), v=(col("COL", 6), A.mult, -32.0, A.add))
    both(a("ONES32"), a("ONESB"))
    both(a("NHM"), a("ONESB"), scale=-M20 / 2)
    both(a("BJ"), a("BW", 64, 208), scale=col("COL", 4), v=(col("COL", 4), A.mult))
    ts(a("LM"), a("S4", 0, 32), col("COL", 0), A.add)
    for n, lo, hi, c in (("TABT", 512, 528, -8 * M20), ("TABG0", 560, 576, -8 * M20), ("TABG1", 560, 576, -8 * M20), ("FT", 512, 528, 0.0),
                         ("FG", 560, 576, 0.0), ("D0", 0, 48, 0.0), ("CT", 0, 1, 0.0), ("CG", 0, 1, 0.0), ("WB", 0, 16, 7.0),
                         ("REM", 0, 1, -3072.0), ("RM2", 0, 1, -3968.0),
                         ("W00", 0, 16, 0.0), ("W01", 0, 16, 96.0), ("W10", 0, 16, 0.0), ("W11", 0, 16, 96.0)):
        fill(n, lo, hi, c)

    def offsets(fl, nl, x, b0, b1, floor=False):
        c, pp, oo = a("C" + x, 1, nl + 1), a("PP" + x, 0, nl), a("OO" + x, 0, nl)
        mms([(P(b0, 0, nl), view("BW", m, 64), a(fl, m, 16 * nl, 16)) for m in range(16)])
        both(c, P(b0, 0, nl))
        mms([(P(b1, 128, 128 + nl), a("TS"), c), (P(b1, 128, 128 + nl), a("DMP"), a("C" + x, 0, nl))])
        mms([(P(b0, 64, 64 + nl), a("ID32"), a("D" + x, 0, nl)), (P(b0, 64, 64 + nl), a("NBIG"), c)])
        scan(pp, a("D0" if floor else "ONE", 0, nl), P(b1, 128, 128 + nl), 0.0, A.max if floor else A.mult, A.add)
        tt(oo, pp, P(b0, 64, 64 + nl), A.max)
        cp(a("LS" + x, 0, nl), oo)

    def ends(le, nl, x, b):
        mms([(P(b, 0, nl), a("ID32"), a("PP" + x, 0, nl)), (P(b, 0, nl), a("ID"), a("C" + x, 1, nl + 1))])
        ts(a(le, 0, nl), P(b, 0, nl), -1.0, A.add)

    def pack(x, nl, cuts):
        scatter("W" + x, "LS" + x, nl, "PAYG" if x == "G" else "PAY", 18)
        for lo, hi in cuts:
            scan(a("Z" + x, lo, hi), a("DEC", lo, hi), a("W" + x, lo, hi), -2 * M24 if lo == 0 else col("Z" + x, lo - 1), A.add, A.max)
            pair(a("Y" + x, lo, hi), a("Z" + x, lo, hi), (0.0, A.max, M20, A.min), (F.Relu, M20, -1.0), (F.Relu, M20, -1.0))

    def invert(src, held):
        mark()
        one = 1.0 if src == "A1" else 0.0
        pair(a("FI"), a(src), (8192.0 + one, A.is_ge), (F.Sign, -8192.5, 1.0), (F.Relu, 0.0, 1.0), "SV" if one else "V")
        if one:
            dmas("Y", [(a("WT", 0, 768), a("WG", 0, 768))], 3.0)
        else:
            fill("WT", 0, 768, -8 * M20)
            fill("WG", 0, 1152, -8 * M20, 576)
            dmas("Y", [(a("LOW"), a("WG", 0, 1152))], 3.0, [first])
        fill("INV", 1024, 4096, 0.0, 768, 4)
        offsets("FI", 32, "T", 4, 5)
        mms([(P(7), row("E8", 0, 128), row("J", 0, 512)), (P(7), row("ONE", 0, 128, 16), row("DEC", 0, 512, 16))], True, False)
        mms([(P(7), a("PARD"), a("FI")), (P(7), a("TRIQ"), a("FI"))], False, True)
        if one:
            both(a("T2"), a(src), bias=-6145.0 * 128, scale=128.0)
        else:
            ts(a("T2"), a(src), -6144.0, A.add, 128.0, A.mult)
        tt(a("PAY", 0, 512), a("T2"), P(7), A.add)
        pack("T", 32, ((0, 384), (384, 768)))
        mms([(P(4, 0, 48), view("BS32", m), a("YT", m, 768, 16)) for m in range(16)])
        cp(a("N1", 0, 48), P(4, 0, 48))
        ts(a("N2", 0, 48), a("N1", 0, 48), MASK - 1023, A.bitwise_and, 8, A.arith_shift_right)
        tt(a("OO", 0, 48), a("N2", 0, 48), a("DS", 0, 48), A.max)
        cp(a("LS"), a("OO", 0, 48))
        mark()
        scatter("INV", "LS", 48, "YT", 24)
        mms([(P(5, 0, 48), view("BS32", m), a("INV", 1024 + 4 * m, 4096, 64)) for m in range(16)])
        cp(a("N1", 0, 48), P(5, 0, 48))
        ts(a("N2", 0, 48), a("N1", 0, 48), 1023, A.bitwise_and)
        ts(a("N3", 0, 48), a("N1", 0, 48), MASK, A.bitwise_and)
        ts(a(held), a("N3", 0, 48), 0.0, A.is_gt)

    def slots():
        act(a("SGA"), a("INV", 1024, 4096, 4), F.Sign, bias=-0.5)
        act(a("SGB"), a("INV", 1024, 4096, 4), F.Sign, bias=M20 - 0.5, scale=-1.0)
        mms([(P(4, 0, 48), view("BJ", m), a(n, m, 768, 16)) for n in ("SGA", "SGB") for m in range(16)])

    def lists_a(banks):
        for e in range(2):
            for s in range(2):
                b, lo = banks[2 * e + s], 256 * s + 128 * e
                mms([(P(b, 0, 128), h64("PA", 8 - 8 * a0, 136 - 8 * a0, s=s), h64("A1", 256 * e + a0, 256 * e + 256, 2, s=s)) for a0 in range(2)])
                ts(a("LA", lo, lo + 128), P(b, 0, 128), 0.125, A.mult, 15.4375, A.add)

    def outgoing(s, k):
        w = Wn(s, k)
        for lo, hi in ((0, 24), (24, 48)):
            both(a("OB%d" % s, 16 * lo, 16 * hi), ix(a(w, 0, 1040), a("LO%d" % s, lo, hi)))
        send("OB%d" % s, 256, w, 1040, 1, "x%d" % (2 * k + s), "l%d" % s, [a("AR"), a("WB", 1040, 1808)] if (s, k) == (1, 7) else [])

    def order_tables(t, b):
        mark()
        if t == 0:
            u, c = a("UJ"), 0.0
            ts(u, a("J"), col("PL", 3), A.mult, col("PL", 4), A.add)
            ts(u, u, 8191, A.bitwise_and)
            cp(a("UI", 0, 32), a("UJ", 0, 32))
            ts(a("UH"), u, 1.0 / 512, A.mult, 191.5009765625, A.add)
        else:
            x, r, u, c = a("T2"), a("T1"), P(b), 4096.0
            both(x, a("J"), bias=col("PL", 15), scale=col("PL", 3), v=(col("PL", 3), A.mult, col("PL", 15), A.add))
            both(r, x, bias=2.0 ** -14, scale=2.0 ** -13)
            whole(r, r)
            mms([(u, a("ID32"), x), (u, a("N8K"), r)])
            ts(a("UI", 0, 32), P(b, 0, 32), c, A.add)
            both(a("UH"), u, bias=199.5009765625, scale=1.0 / 512)
        act(a("POW%d" % t), a("UH"), F.Sigmoid, bias=171 * LN2, scale=-LN2)
        ts(a("N5", 0, 32), a("UI", 0, 32), 15, A.bitwise_and)
        ts(col("COL", 12), col("N5", 0), 16384.0, A.mult, c + 1 - M24, A.add)
        if t == 0:
            ts(a("TABG0", 48, 560), u, col("COL", 12), A.add)
        else:
            both(a("TABG1", 48, 560), u, bias=col("COL", 12), v=(col("COL", 12), A.add))
        ts(a("N6", 0, 32), a("UI", 0, 32), 4, A.arith_shift_right, 31, A.bitwise_and)
        ts(a("N5", 0, 32), a("N5", 0, 32), 32.0, A.mult)
        tt(a("N5", 0, 32), a("N5", 0, 32), a("N6", 0, 32), A.add)
        cp(a("LW%d" % t), a("N5", 0, 32))

    def place(out, nl):
        x, n3, n4 = a("N2", 0, nl), a("N3", 0, nl), a("N4", 0, nl)
        ts(n3, x, 15, A.bitwise_and)
        ts(n4, x, 4, A.arith_shift_right, 511, A.bitwise_and)
        ts(x, x, 0x6000, A.bitwise_and)
        ts(n3, n3, 512.0, A.mult)
        tt(n4, n4, x, A.add)
        tt(a(out), n3, n4, A.add)

    def round_tables(t):
        mark()
        ts(a("LB"), a("B1"), 0.125, A.mult, 15.4375, A.add)
        if t == 1:
            ts(a("BH"), a("B1"), -1.0, A.add)
        ts(a("CB"), a("BH"), 7, A.bitwise_and)
        both(a("HELD"), a("A1"), F.Sign, v=(0.0, A.is_gt))
        for b in range(2):
            c0 = 32 * (8 * b + t)
            ts(a("N2", b, 64, 2), a("B1", c0, c0 + 32), -1.0, A.add)
        place("TG", 64)
        mark()
        both(a("TABT", 528, 544), a("TLK", 16 * t, 16 * t + 16))
        dmas("Y", [(a("Z", 0, 12672, 1, 0, 128, 16), a("NIL"))], 3.0)
        ts(a("LI"), a("IE1"), 0.125, A.mult, 15.4375, A.add)
        ts(a("N2", 0, 48), a("IE1"), -1.0, A.add)
        ts(a("N1", 0, 48), a("N2", 0, 48), 0x4007, A.bitwise_and)
        cp(a("TL"), a("N1", 0, 48))
        place("TI", 48)
        mms([(P(4, m, 512, 16), a("SPR", 128 * m, 128 * m + 128), a("TL", 0, 32)) for m in range(16)])
        mms([(P(5, m, 256, 16), a("SPR", 128 * m, 128 * m + 128), a("TL", 32, 48)) for m in range(16)])
        both(a("TAB", 0, 512), P(4))
        both(a("TAB", 512, 768), P(5, 0, 256))
        mark()
        mark()
        mms([(P(6), row("ONE", 0, 128), row("TIE", 0, 512))]
            + [(P(6, 256 * b + 64 * bl, 256 * b + 64 * bl + 64), a("HELD", 128 * bl, 128 * bl + 128), a("PT", 64 * b, 64 * b + 64)) for b in range(2) for bl in range(4)],
            True, False)

    def step(s, k):
        mark()
        w, gs = Wn(s, k), "G%d" % s
        if k % 4 == 3:
            for j in range(4):
                sel(a("OWN%d" % s, j, 2048, 4), a(w, 16 + 512 * DIF, 528 + 512 * DIF), [[0, 512]], 0, 0)
        for hv in range(2):
            b, v0, o = 2 * s + hv, 512 * hv, a(Wn(s, k + 1), 16 + 512 * hv, 528 + 512 * hv)
            dif = k % 4 == 3 and hv == DIF
            mm(P(b), h64("SUM" if k % 4 == 0 else "S25" if dif else "S17"), h64(w, 16 + v0, 528 + v0), True, False)
            for lo, hi in zip(PIECES, PIECES[1:]):
                if lo // 512 != hv:
                    continue
                out, got = a(gs, 4 * lo, 4 * hi), ix(a(w), a("LA", 256 * s + lo // 4, 256 * s + hi // 4))
                if dif:
                    tt(out, got, a("OWN%d" % s, 4 * (lo - v0), 4 * (hi - v0)), A.subtract)
                else:
                    both(out, got)
                    chain.append(len(nodes) - 1)
                mms([(P(b, lo - v0, hi - v0), a("SUM"), a(gs, 4 * lo + j, 4 * hi, 4)) for j in range(4)], False, hi == v0 + 512)
            if k % 4 == 0:
                both(o, P(b), bias=-768.0 if k else 96.0)
            else:
                both(a("Q%d" % hv), P(b), bias=-7.5 if k == 7 else -103.5)
                tt(o, P(b), a("Q%d" % hv), A.subtract)
        if k == 0:
            fill(w, 0, 16, 96.0)
        mark()
        if k < 7:
            outgoing(s, k + 1)
        mark()
        if k % 4 == 3:
            for hv in range(2):
                for j in range(4):
                    b = (4, 5, 7)[(8 * s + 4 * hv + j) % 3]
                    if hv == DIF:
                        act(a("D", 512 * j, 512 * j + 512), a(gs, 2048 * hv + j, 2048 * hv + 2048, 4), F.Abs)
                    else:
                        mms([(P(b), a("NID"), a(w, 16 + 512 * hv, 528 + 512 * hv)), (P(b), a("ID"), a(gs, 2048 * hv + j, 2048 * hv + 2048, 4))])
                        act(a("D", 512 * j, 512 * j + 512), P(b), F.Abs)
                    c0 = 128 * hv + 32 * s + j
                    mms([(P(6, c0 + 256 * pb + 64 * bb, c0 + 256 * pb + 64 * bb + 32 - j, 4), a("D", 512 * j + 256 * bb + pb, 512 * j + 256 * bb + 256, 2),
                          a("SEL", 0, 8)) for bb in range(2) for pb in range(2)], False, s == 1 and hv == 1 and j == 3)

    CUTS, FINE = ((0, 512), (512, 1024), (1024, 1152)), ((0, 288), (288, 576), (576, 864), (864, 1152))
    rows = a("ROW", 0, 8192, 1, 0, 128, 16)

    def partners(t, banks):
        for b, (lo, hi) in zip(banks, CUTS):
            mms([(P(b, 0, hi - lo), a("ONES32"), a("YT", lo, hi)), (P(b, 0, hi - lo), a("NHM"), a("SG", lo, hi))])
            both(a("YT", lo, hi), P(b, 0, hi - lo), bias=-8 * M20 - t)

    def control(t):
        w = [Wn(s, 0) for s in range(2)]
        th = 8 if t == 0 else 0
        mark()
        for i in range(4):
            s, u0 = i // 2, 8 * (i % 2)
            mms([(P(0, 0, 64), h64("BW", 79 - 64 * s - u, 207 - 64 * s - u), h64(w[s], 16 + 64 * u, 80 + 64 * u)) for u in range(u0, u0 + 8)], i == 0, i == 3)
        mm(P(3, 0, 64), a("ID32"), a("TG"), True, False)
        ts(a("FLK"), P(0, 0, 64), col("PL", th), A.is_ge)
        mm(P(3, 0, 64), a("PBIG"), a("FLK"), False, True)
        tt(a("S1", 0, 64), P(3, 0, 64), a("DZ", 0, 64), A.min)
        cp(a("LKA"), a("S1", 0, 64))
        marks("LKA", 64)
        mark()
        if t == 0:
            mms([(P(7, 0, 48), a("NBIG"), a("MO")), (P(7, 0, 48), a("PBIG"), a("OH")), (P(7, 0, 48), a("PBIG"), a("OH"))], True, False)
            for s in range(2):
                mms([(P(7, 0, 48), h64("BW", 79 - 64 * s - m, 207 - 64 * s - m), h64("OB%d" % s, m, 768, 16)) for m in range(16)], False, s == 1)
            ts(a("OKA"), P(7, 0, 48), col("PO", 0), A.is_ge)
        else:
            mms([(P(0, 0, 48), a("NID"), a("OH"))]
                + [(P(0, 0, 48), view("SPD32", m), a("Z", 8192 + 4096 * (m % 2) + m // 2, 8576 + 4096 * (m % 2), 8)) for m in range(16)])
            both(a("OKA"), P(0, 0, 48), F.Relu, 0.0, -1.0, (-1.0, A.mult, 0.0, A.max))
        send("OKA", 16, "AR", 0, 1, "al%d" % t, "la")
        mark()
        mms([(P(2, 0, 128, 1, 0, 64), h64("BX", 63 - 8 * q - 4 * s, 127 - 8 * q - 4 * s), h64(w[s], 16 + 256 * (q % 4) + q // 4, 272 + 256 * (q % 4), 2))
             for s in range(2) for q in range(8)])
        both(h64("ZX"), P(2, 0, 128, 1, 0, 64), F.Relu, col("PX", 2 + t, 64), -200.0, (col("PX", t, 64), A.is_lt, 100.0, A.mult))
        for s in range(2):
            mms([(P(1), h64("BAND", 72 - 64 * s - 8 * b, 200 - 64 * s - 8 * b), h64(w[s], 16 + b, 1040, 2)) for b in range(2)], s == 0, s == 1)
        both(a("STH"), P(1), F.Relu, col("PL", 12 + t), M20, (col("PL", th + 1), A.is_ge, M20, A.mult))
        mark()
        scan(a("MN"), a("RST"), P(6), 0.0, A.mult, A.min)
        ts(a("N1", 0, 64), a("MN", 7, 512, 8), 4096.0, A.add)
        ts(a("N1", 0, 64), a("N1", 0, 64), 0x1807, A.bitwise_and)
        cp(a("C0"), a("N1", 0, 64))
        mm(P(4, 0, 128, 1, 0, 64), a("C0"), a("ID"))
        tt(h64("CX"), h64("ZX"), P(4, 0, 128, 1, 0, 64), A.max)
        for b2 in range(2):
            mms([(P(2 + b2, 256 * bb + b, 256 * bb + 256, 2), h64("XR", 128 * (4 * b + 2 * b2 + bb), 128 * (4 * b + 2 * b2 + bb) + 128), h64("CX"))
                 for b in range(2) for bb in range(2)])
            both(a("WB", 16 + 512 * b2, 528 + 512 * b2), P(2 + b2))
        tt(a("BO"), ix(a("WB", 0, 1040), a("LI")), a("TAB"), A.not_equal)
        send("BO", 256, "WB", 1040, -1, "be%d" % t, "lb")
        if t == 0:
            sent = len(nodes) - 2
            fill("WT", 0, 1152, -8 * M20, 1152, es="G")
            nodes[-1]["dep"].append(sent)
            order_tables(1, 5)
        mark()
        mms([(P(0), a("LBM", 128 * b, 128 * b + 128), a("WB", 16 + b, 1040, 2)) for b in range(2)])
        pair(a("K1"), P(0), (col("COL", 2), A.is_equal, 16384.0, A.mult), (F.Abs, col("COL", 11), 1.0), (F.Relu, 16384.0, -16384.0))
        mark()
        mms([(P(7, 0, 48), a("ID32"), a("TI")), (P(7, 0, 48), a("PBIG"), a("AR"))])
        tt(a("S2", 0, 48), P(7, 0, 48), a("DZ", 0, 48), A.min)
        cp(a("LGI"), a("S2", 0, 48))
        marks("LGI", 48)
        tt(a("FG", 0, 48), a("AR"), a("IH"), A.is_gt)
        mm(P(7, 0, 48), a("ONESB"), a("FG", 0, 48))
        node({"V": (lambda q: q.tensor_reduce(ap(col("D0", 33)), ap(P(7, 0, 48)), AxisListType.X, A.add), (1, 64, 0, 0, 0)),
              "S": (lambda q: q.activation(ap(a("S2", 0, 48)), ap(P(7, 0, 48)), F.Identity, accum_out=ap(col("D0", 33))), (1.4, 64, 0, 0, 0))},
             [P(7, 0, 48)], [col("D0", 33), a("S2", 0, 48)])
        mark()
        mm(P(1), a("NID32"), a("A1"), True, False)
        mm(P(1), a("ID"), a("K1"), False, False)
        dmas("Y", [(a("ZD"), a("Z", 0, 8192, 1, 0, 128, 16))])
        mm(P(1), a("P16K"), a("ZD"), False, True)
        tt(a("F1"), P(1), a("STH"), A.is_ge)
        both(P(1) if t == 0 else a("A1"), P(1), F.Relu, 0.0, -1.0, (-1.0, A.mult, 0.0, A.max))
        mm(P(2), a("ONESB"), a("F1"))
        mm(P(3), a("TRIC"), a("F1"))
        scan(a("REM", 1, 513), a("ONE", 0, 512), P(2), -3072.0, A.mult, A.subtract)
        tt(a("FT", 0, 512), P(3), a("REM", 0, 512), A.is_lt)
        mark()
        for i in range(16):
            both(a("G%d" % (i // 8), 512 * (i % 8), 512 * (i % 8) + 512), ix(a("WB"), a("LB", 32 * i, 32 * i + 32)))
        for lo, hi in ((0, 128), (128, 256), (256, 384), (384, 448), (448, 512)):
            e = lo // 256
            mms([(P(6 * e, lo - 256 * e, hi - 256 * e), spd(0, u), a("G%d" % e, 16 * lo - 4096 * e + u, 16 * hi - 4096 * e, 16)) for u in range(16)],
                lo % 256 == 0, hi % 256 == 0)
        mark()
        mms([(P(7, 0, 48), spd(0, m), a("WB", 1040 + m, 1808, 16)) for m in range(16)])
        tt(a("OH"), a("OKA"), P(7, 0, 48), A.min)
        both(a("FR"), a("OH", 16 * t, 16 * t + 16), bias=1.0, scale=-1.0)
        mm(P(4, 0, 16), a("ONESB"), a("FR"))
        mm(P(4, 16, 32), a("TRIC"), a("FR"))
        scan(a("RM2", 1, 17), a("ONE", 0, 16), P(4, 0, 16), -3968.0, A.mult, A.subtract)
        tt(a("FT", 528, 544), P(4, 16, 32), a("RM2", 0, 16), A.is_lt)
        mark()
        for b in range(2):
            c0 = 32 * (8 * b + t)
            tt(a("FB", 256 * b, 256 * b + 256), P(6 * b, 0, 256), a("CB", 256 * b, 256 * b + 256), A.is_equal)
            tt(a("FB", c0, c0 + 32), a("FB", c0, c0 + 32), a("FLK", b, 64, 2), A.is_ge)
        for lo in (0, 16):
            both(a("WJ", 16 * lo, 16 * lo + 256), ix(a("FB"), a("LW%d" % t, lo, lo + 16)))
        mms([(P(7, 0, 32), view("BWP", m), a("WJ", m, 512, 16)) for m in range(16)])
        both(a("WF"), P(7, 0, 32), bias=0.25 * M20, scale=2.0 ** 56)
        tt(a("T1"), ix(a("WF"), a("LM")), a("POW%d" % t), A.mult)
        whole(P(7), a("T1"))
        tt(a("FG", 48, 560), P(7), a("T1"), A.is_gt)
        mark()
        mms([(P(6), a("ID32"), a("B1")), (P(6), a("NBIG"), a("FB"))])
        both(a("BM"), P(6), F.Relu, v=(0.0, A.max))
        if t == 1:
            both(a("BM"), a("BM"), bias=-1.0)
            dmas("Y", [(a("YS", 0, 512, 1, r, 128, 16), a("BM", 32 * r, 32 * r + 32)) for r in range(16)], 6.0)
        mark()
        mm(P(5), a("ID32"), a("TABT", 0, 512), True, False)
        mm(P(5), a("TRIQ"), a("FT", 0, 512), False, True)
        mm(P(3, 0, 32), a("TRIQ"), a("FT", 512, 544))
        offsets("FT", 34, "T", 4, 4, True)
        both(a("PAY", 0, 512), P(5))
        tt(a("PAY", 512, 544), P(3, 0, 32), a("TABT", 512, 544), A.add)
        ends("LE", 34, "T", 3)
        pack("T", 34, ((0, 576), (576, 1152)))
        mark()
        both(a("HIT"), a("ZT"), F.Relu, 0.0, -32.0, (-32.0, A.mult, 0.0, A.max))
        act(a("SG"), a("ZT"), F.Sign, 0.5 - M20)
        partners(t, (0, 6, 0) if t == 0 else (0, 1, 6))
        mark()
        mm(P(2), a("ID32"), a("TABG%d" % t, 0, 512), True, False)
        mm(P(2), a("TRIQ"), a("FG", 0, 512), False, True)
        mm(P(3, 0, 64), a("TRIQ"), a("FG", 512, 576))
        offsets("FG", 36, "G", 4, 4)
        both(a("PAYG", 0, 512), P(2))
        tt(a("PAYG", 512, 576), P(3, 0, 64), a("TABG%d" % t, 512, 576), A.add)
        if t == 0:
            ends("LE2", 3, "G", 2)
        pack("G", 36, FINE)
        dmas("Y", [(rows, a("YS" if t == 1 else "BM"))])
        if t == 0:
            dmas("Y", [(a(n, 0, 1152), a("LOW")) for n in ("WT", "WG")], 4.0)
        halves = ((7, 0, 72),) if t == 0 else ((7, 0, 36), (6, 36, 72))
        for b, lo, hi in halves:
            mms([(P(b, lo, hi), view("BS32", m), a("YG", 16 * lo + m, 16 * hi, 16)) for m in range(16)])
        mark()
        for b, (lo, hi) in zip((5, 3, 4, 2), FINE):
            mm(P(b, 0, hi - lo), a("NID"), a("HIT", lo, hi), True, False)
            mm(P(b, 0, hi - lo), a("ONES32"), a("YG", lo, hi), False, True)
            scan(a("FL", lo, hi), a("HIT", lo, hi), P(b, 0, hi - lo), 0.0 if lo == 0 else col("FL", lo - 1), A.min, A.max)
        if t == 0:
            for lo, hi in ((0, 256), (256, 544)):
                tt(a("FGI", lo, hi), ix(a("FL"), a("LE", lo // 16, hi // 16)), a("FT", lo, hi), A.mult)
                ts(a("FGI", lo, hi), a("FGI", lo, hi), 0x3FFF, A.bitwise_and)
                tt(a("A1", lo, lo + 256), a("FGI", lo, lo + 256), P(1, lo, lo + 256), A.add)
            lists_a((0, 2, 3, 1))
        else:
            x, r = a("PAY", 0, 512), a("REM", 16, 528)
            tt(x, ix(a("FL"), a("LE", 0, 32)), a("FT", 0, 512), A.mult)
            both(r, x, bias=-0.4375, scale=2.0 ** -14)
            whole(r, r)
            mm(P(1), a("ID32"), a("A1"), True, False)
            mm(P(1), a("ID32"), x, False, False)
            mm(P(1), a("N16K"), r, False, True)
            both(a("A1"), P(1), bias=-1.0)
            dmas("S", [(T.yd[:], a("A1"))])
        mark()
        for b, lo, hi in halves:
            n = [a("N%d" % i, lo, hi) for i in (5, 6, 7, 8)]
            ts(n[0], P(b, lo, hi), -1.0, A.add)
            if t == 0:
                ts(n[1], n[0], 9, A.arith_shift_right, 0x1E0, A.bitwise_and)
                ts(n[2], n[0], 4, A.arith_shift_right, 31, A.bitwise_and)
                ts(n[3], n[0], FLAG + 0x1E00, A.bitwise_and)
                tt(n[1], n[1], n[3], A.add)
            else:
                ts(n[1], n[0], 5, A.arith_shift_right, 0x7E00, A.bitwise_and)
                ts(n[2], n[0], 4, A.arith_shift_right, 511, A.bitwise_and)
            tt(n[1], n[1], n[2], A.add)
            tt(n[1], n[1], a("DZ0", lo, hi), A.min)
            cp(a("LZ", lo, hi), n[1])
        scatter("ROW", "LZ", 72, "YT", 18)
        if t == 1:
            dmas("Y", [(T.ya[:], rows)])
            return
        dmas("Y", [(a("B1"), rows)])
        mark()
        ts(a("S3", 0, 16), a("FGI", 528, 544), 0.0, A.is_gt)
        tt(a("OH", 0, 16), a("OH", 0, 16), a("S3", 0, 16), A.max)
        both(a("HIG"), a("ZG", 0, 768), F.Relu, 0.0, -32.0, (-32.0, A.mult, 0.0, A.max))
        for b, (lo, hi) in enumerate(((0, 512), (512, 768))):
            mms([(P(4 + b, 0, hi - lo), a("NID"), a("HIG", lo, hi)), (P(4 + b, 0, hi - lo), a("ID32"), a("YT", lo, hi))])
            scan(a("FL2", lo, hi), a("HIG", lo, hi), P(4 + b, 0, hi - lo), 0.0 if b == 0 else col("FL2", lo - 1), A.min, A.max)
        mms([(P(6, 0, 48), spd(0, m), a("BO", m, 768, 16)) for m in range(16)])
        tt(a("S4", 0, 48), ix(a("FL2"), a("LE2", 0, 3)), a("FG", 0, 48), A.mult)
        tt(a("KEEP"), a("AR"), P(6, 0, 48), A.min)
        tt(a("IE1"), a("IE1"), a("KEEP"), A.mult)
        tt(a("IE1"), a("IE1"), a("S4", 0, 48), A.add)
        ts(a("IH"), a("IE1"), 0.0, A.is_gt)

    mark()
    ts(a("A1"), a("DEN", 0, 512), 1.0, A.add)
    lists_a((0, 1, 2, 3))
    invert("AXO", "OH")
    ts(a("VO"), a("N2", 0, 48), 16.0, A.add)
    for s in range(2):
        mm(P(2 + s, 0, 48), h64("SUM32", s=s), h64("VO", s=s))
        cp(a("LO%d" % s), P(2 + s, 0, 48))
        outgoing(s, 0)
    mark()
    slots()
    ts(a("MO"), P(4, 0, 48), 0.0, A.is_equal)
    mark()
    fill("ZG", 0, 792, 0.0)
    dmas("Y", [(a("NIL"), a("ZG", 0, 792))], 3.0, [first])
    for lo in (8192, 12288):
        fill("Z", lo, lo + 384, 0.0)
    mark()
    cp(row("PARF", 0, 6, 8), row("PARI", 0, 6, 8))
    mm(P(6, 0, 6), row("R8", 0, 128, 8), row("PARF", 0, 6, 8))
    mm(P(6, 8, 14, 1, 0, 64), row("R8X", 0, 64, 8), row("PARF", 0, 6, 8))
    both(a("PL", 0, 6), P(6, 0, 6))
    both(a("PL", 8, 11), P(6, 0, 3), bias=1536.0)
    both(col("PL", 12), P(6, 1, 2), bias=-1535.5 * M20, scale=-M20)
    both(col("PL", 13), P(6, 1, 2), bias=0.5 * M20, scale=-M20)
    both(col("PO", 0), P(6, 0, 1), bias=1536.0 + 16384)
    both(col("PL", 15), P(6, 5, 6), bias=-1023.5 * 8192)
    both(col("PX", 1, 64), P(6, 10, 11, 1, 0, 64))
    both(col("PX", 0, 64), P(6, 10, 11, 1, 0, 64), bias=1536.0)
    both(a("PX", 2, 4, 1, 0, 64), a("PX", 0, 2, 1, 0, 64), bias=-100.0, scale=200.0)
    invert("A1", "IH")
    mark()
    both(a("J"), a("J"), bias=col("COL", 10), v=(col("COL", 10), A.add))
    both(a("TLK"), a("J", 0, 48), bias=8193.0 - M24, scale=8.0)
    for t in range(2):
        both(a("TABG%d" % t, 0, 48), a("TLK"), bias=float(FLAG))
    both(a("TABT", 0, 512), a("J"), bias=1.0 - M24)
    mark()
    slots()
    ts(a("S1", 0, 48), a("N2", 0, 48), 8.0, A.mult, 1.0, A.add)
    tt(a("S1", 0, 48), a("S1", 0, 48), P(4, 0, 48), A.add)
    tt(a("IE1"), a("S1", 0, 48), a("IH"), A.mult)
    ts(a("B1"), a("BH"), 1.0, A.add)
    order_tables(0, 7)
    for t in range(2):
        round_tables(t)
        for k in range(4 * t, 4 * t + 4):
            for s in range(2):
                step(s, k)
        if t == 1:
            dmas("Y", [(T.yx[64 * s:64 * s + 64, :], h64(Wn(s, 0), 16, 1040)) for s in range(2)])
        control(t)
    emit()
